import numpy as np, ml_dtypes
CORES = [66,74,82,90,194,202,210,218]
N = 8
import mx_ref
BF = ml_dtypes.bfloat16
def pick(q, e):
    c = np.concatenate([q[0].reshape(128, -1, 4), np.zeros((128, 1, 4), np.uint8)], axis=1); s = np.concatenate([q[1], np.ones((16, 1), np.uint8)], axis=1)
    return (np.ascontiguousarray(c[:, e].reshape(128, -1)), np.ascontiguousarray(s[:, e]))
def join(*qs):
    return (np.concatenate([q[0] for q in qs], axis=1), np.concatenate([q[1] for q in qs], axis=1))
def put(q, e, v):
    c, s = q[0].reshape(128, -1, 4).copy(), q[1].copy(); c[:, e] = v[0].reshape(128, -1, 4); s[:, e] = v[1]
    return (c.reshape(128, -1), s)
def pk(c, s):
    return (np.ascontiguousarray(c), mx_ref.live(s))
def emit(q):
    return q[0], q[1]
def tile(rs):
    return np.stack(rs, axis=2).reshape(128, -1).astype(BF)
def f(rng, *shape):
    return mx_ref.flush((rng.standard_normal(shape, dtype=np.float32) * np.exp2(rng.integers(-2, 3, shape[:-1] + (1,)))).astype(BF))
def wide(rng, *shape, cols=0):
    v = rng.standard_normal(shape, dtype=np.float32) * np.exp2(rng.integers(-12, 13, shape)).astype(np.float32)
    if cols: v *= np.repeat(np.exp2(rng.integers(-cols, cols + 1, shape[:-2] + (1, shape[-1] // 4))) * (rng.random(shape[:-2] + (1, shape[-1] // 4)) > 0.0625), 4, axis=-1).astype(np.float32)
    return mx_ref.flush(v.astype(BF))
P, K, CAPP, R, L, B = 160, 16, 6, 3, 3, 10
def falling(s):
    return np.argsort(-(s + np.float32(0)), kind="stable")
def bits(g, first, n):
    return np.sum([(g[first + i] > 0) * 2 ** i for i in range(n)], axis=0)
def astile(v):
    s, n = v.shape[:-2], v.shape[-1]
    return np.ascontiguousarray(np.swapaxes(v.reshape(s + (128, 4, n)), -1, -2)).reshape(s + (128, 4 * n))
def weigh(rng, t):
    c, s = mx_ref.quantize(np.ascontiguousarray(t))
    p = mx_ref.plane(s, rng)
    return {"wc": np.stack([c] * N), "ws": np.stack([p] * N)}
def steer(rng, sign, low, at, free, same=False, xs=1.0, us=2.0 ** 13, lean=None):
    v = np.zeros((N, 512, P), np.float32)
    v[:, :128] = np.where(sign < 0, 112, 0)[:, None, :]
    v[:, 128:256] = np.where(sign > 0, 112, 0)[:, None, :]
    for t in range(3):
        for k in range(3): v[:, 256 + 3 * t + k] = low[t] // 8 ** k % 8
    if lean is not None: v[:, 265:266 + B] = lean
    for k in range(4):
        for i in range(L):
            one = at[:, :, k] // 2 ** i % 2
            v[:, 288 + 8 * k + 2 * i] = one
            v[:, 289 + 8 * k + 2 * i] = 1 - one
    v[:, 320:] = free
    a = np.zeros((2, 512, 512), np.float32)
    for m in range(2):
        j = np.arange(256)
        a[m, j, j] = 20
        j = np.arange(9)
        a[m, 256 + j, 256 + (j + 3) % 9] = 20
        j = np.arange(265, 265 + B)
        a[m, j, j] = 20
        a[m, 280 + 4 * m, 265 + B] = 20
        j = np.arange(32)
        a[m, 288 + j, 288 + (j + 8 * (m + 1)) % 32] = 20
        a[m, 320:, 320:] = rng.standard_normal((192, 192))
        if same and m == 0: a[m, 320:, 320:] = 20 * np.eye(192)
    w = np.concatenate([astile(np.ascontiguousarray(a[m][b::4].T)) for m in range(2) for b in range(4)], axis=1)
    h = np.zeros((512, 128), np.float32)
    h[:128, 0] = -448
    h[128:256, 0] = 448
    h[256:259, 0] = [1, 8, 64]
    for i in range(L):
        h[288 + 2 * i, 1 + i] = 1
        h[289 + 2 * i, 1 + i] = -1
    for i in range(B):
        h[265 + i, 1 + L + i] = 256
        h[265 + i, 1 + L + (i + 1) % B] = -256
    h[280, 1 + L:1 + L + B] = -256
    h[284, 1 + L:1 + L + B] = 256
    k = rng.standard_normal((192, B))
    h[320:, 1 + L:1 + L + B] = k - np.mean(k, axis=0)
    h[:, 1 + L + B:] = rng.standard_normal((512, 127 - L - B))
    x = mx_ref.flush((astile(v) * np.float32(xs)).astype(BF))
    u = mx_ref.flush((astile(h) * np.float32(us)).astype(BF))
    return {"x": x, "u": np.stack([u] * N), **weigh(rng, mx_ref.flush(w.astype(BF)))}
def setup_inputs(rng):
    return {"x": f(rng, N, 128, 4 * P), "u": np.stack([f(rng, 128, 512)] * N), **weigh(rng, f(rng, 128, 4096))}
def setup_inputs_close(rng):
    low = rng.integers(0, P // 2 - 1, (3, N, P))
    low[0] = P // 2 + (np.arange(P) + 1) // 2
    best = np.argsort(-low[0, 0], kind="stable")
    low[1][:, best[R * K - 1]] = P // 2 - 1
    at, free = rng.integers(0, N, (N, P, 4)), rng.standard_normal((N, 192, P))
    free[:, :, best[R * K:]] = 0
    lean = np.zeros((N, B + 1, P))
    for r in range(N):
        lean[r, rng.integers(0, B, R * K), best[:R * K]] = 1
        for t in range(R):
            to, e = rng.permutation(np.arange(2 * K) % N), best[t * K:t * K + K]
            at[r, e, 1], at[r, e, 2] = to[0::2], to[1::2]
    z, s = [int(k) for k in np.sort(rng.permutation(N)[:2])]
    for r in (z, s):
        low[1, r, best[0]] = P // 2 - 1
        free[r, :, best[0]] = 0
        lean[r, :, best[0]] = 0
    lean[s, B, best[0]] = 1
    return steer(rng, np.full((N, P), -1), low, at, free, lean=lean)
def setup_inputs_ties(rng):
    n, own = P // 4, K // 4
    def some(*shape):
        return rng.integers(4, 8, shape) * np.exp2(rng.integers(-1, 2, shape)) * (rng.random(shape) < 0.25)
    low, at, free = rng.integers(0, 4, (3, n)), rng.integers(0, N, (n, 4)), some(192, n)
    low[0] = np.arange(n) % 2
    e = np.stack([rng.permutation(np.arange(P) % n) for r in range(N)])
    lows, ats = low[:, e], at[e]
    frees = np.stack([free[:, e[r]] for r in range(N)])
    none = []
    for r in range(N):
        p = rng.permutation(P)
        k = p[:own]
        none.append(p[own:own + 2])
        lows[0, r, k], lows[1, r, k] = 2, 400
        ats[r, k] = rng.integers(0, N, (own, 4))
        ats[r, k, 1], ats[r, k, 2] = r, (r + 1) % N
        frees[r][:, k] = some(192, own)
    d = steer(rng, np.full((N, P), -1), lows, ats, frees, same=True)
    x, u = np.array(d["x"]), np.array(d["u"])
    for r in 1 + rng.permutation(N - 1)[:2]:
        for j in none[r]: x[r, :, 4 * j:4 * j + 4] = 0
    u[:, 80:, 4 * (1 + L):4 * (2 + L)] = np.abs(u[:, 80:, 4 * (1 + L):4 * (2 + L)].astype(np.float32)).astype(BF)
    return {**d, "x": x, "u": u}
def setup_inputs_crowd(rng):
    a, b, c, d = [int(k) for k in rng.permutation(N)[:4]]
    low = np.stack([np.stack([rng.permutation(P) for r in range(N)])] * 3)
    low[1] = 2 * P - low[0]
    low[2] = rng.integers(400, 500, (N, P))
    at, free = rng.integers(0, N, (N, P, 4)), rng.standard_normal((N, 192, P))
    for r in range(N):
        to = rng.choice(np.delete(np.arange(N), d), 2 * K)
        if r == a or r == b: to[:] = b
        elif r == c:
            to[:] = c
            to[:CAPP] = b
            to[CAPP:2 * CAPP + 1] = a
        else: to[:CAPP + int(rng.integers(1, 3))] = b
        to = rng.permutation(to)
        top = np.argsort(-low[0, r], kind="stable")[:K]
        at[r, top, 1], at[r, top, 2] = to[0::2], to[1::2]
    top = np.argsort(-low[0, a], kind="stable")[:K]
    e = top[:CAPP // 2]
    low[1, a, top[CAPP // 2:]] += P - K
    for t in range(3): low[t, a, e] = low[t, a, e[0]]
    at[a, e] = at[a, e[0]]
    free[a][:, e] = free[a][:, e[:1]]
    return steer(rng, np.full((N, P), -1), low, at, free)
def setup_inputs_huge(rng):
    sign = np.full((N, P), -1)
    for r in rng.permutation(N)[:N // 2]: sign[r, rng.permutation(P)[:K // 2]] = 1
    return steer(rng, sign, rng.integers(0, 512, (3, N, P)), rng.integers(0, N, (N, P, 4)), rng.standard_normal((N, 192, P)), xs=2.0 ** 23, us=2.0 ** 21)
def setup_inputs_spread(rng):
    return {**setup_inputs(rng), "x": wide(rng, N, 128, 4 * P, cols=6)}
def check_inputs(d):
    b = []
    for k in ("x", "u"):
        v = np.abs(d[k].astype(np.float32))
        if not (np.isfinite(v).all() and ((v == 0) | (v >= 2.0 ** -30) & (v <= 2.0 ** 30)).all()): b.append("a value of " + k)
    for k in ("u", "wc", "ws"):
        v = d[k].astype(np.float32)
        if (v != v[:1]).any(): b.append(k + " is not the same on every rank")
    if ((d["wc"] & 127) == 127).any(): b.append("a code of wc")
    zero, least, most = [int(mx_ref.quantize(np.full((128, 16), k, np.float32).astype(BF))[1].max()) for k in (0.0, 2.0 ** -30, 2.0 ** 30)]
    for r in range(N):
        s = mx_ref.live(d["ws"][r]).astype(int)
        if ((s != zero) & ((s < least) | (s > most))).any():
            b.append("a scale of ws")
            break
    return b
def reference(x, u, wc, ws):
    y, oc, osc = np.zeros((N, 128, R * P), np.float32), np.zeros((N, 128, 4 * P), np.uint8), np.zeros((N, 16, P), np.uint8)
    held = [mx_ref.quantize(np.ascontiguousarray(x[r])) for r in range(N)]
    qu = [mx_ref.quantize(np.ascontiguousarray(u[r])) for r in range(N)]
    w = []
    for r in range(N):
        q = pk(wc[r], ws[r])
        w.append([pick(q, np.arange(128 * i, 128 * i + 128)) for i in range(8)])
    for t in range(R):
        g = [mx_ref.matmul(qu[r], held[r]) for r in range(N)]
        top = [falling(g[r][0])[:K] for r in range(N)]
        kids, to = [], []
        for r in range(N):
            v = pick(held[r], top[r])
            z = [mx_ref.matmul(w[r][i], v) for i in range(8)]
            rs = [np.stack([z[b], z[4 + b]], axis=2).reshape(128, -1) for b in range(4)]
            kids.append(mx_ref.quantize(tile([np.maximum(e, np.float32(0)) * np.float32(0.05) for e in rs])))
            to.append(bits(mx_ref.matmul(qu[r], kids[r]), 1, L))
        for q in range(N):
            e = np.full((N, CAPP), -1)
            for r in range(N):
                k = np.flatnonzero(to[r] == q)[:CAPP]
                e[r, :len(k)] = k
            came = join(*[pick(kids[r], e[r]) for r in range(N)])
            h = mx_ref.matmul(qu[q], came)
            mark = bits(h, 1 + L, B)
            seen = set(np.delete(bits(g[q], 1 + L, B), top[q]).tolist())
            new = []
            for j in np.flatnonzero(e.reshape(-1) >= 0):
                if int(mark[j]) not in seen:
                    seen.add(int(mark[j]))
                    new.append(int(j))
            new = np.array(new, dtype=int)
            new = new[falling(h[0][new])][:K]
            if len(new): held[q] = put(held[q], np.sort(top[q])[:len(new)], pick(came, new))
            y[q, :, P * t:P * t + P] = mx_ref.matmul(w[q][0], held[q])
    for q in range(N): oc[q], osc[q] = emit(held[q])
    return {"y": y, "oc": oc, "osc": osc}

@@ -1,0 +1,594 @@
+from concourse.bass import DstId, RemoteDMATransfer
+from concourse.mybir import dt, AluOpType, AxisListType, ActivationFunctionType
+
+N, P, K, CAPP, R = 8, 160, 16, 6, 3
+NS = R * K
+NA = N * CAPP
+X2, XQ, KID = N * K, N * NS, N * NS + P
+POOL = KID + R * 256
+ML = NA + (NS - K) + P
+MO, IT = 520, 264
+CODE, U8, F, B, H, I, U = "float8_e4m3fn_x4", "uint8", "float32", "bfloat16", "float16", "int32", "uint16"
+SCRATCH = {"ps": ("psum", [128, 4096], "float32")}
+for _d, _l in (
+    (CODE, dict(quc=128, qxc=P, u0c=128, uac=256, wcs=1024, pc=POOL, p1c=128, p2c=128, occ=P)),
+    (U8, dict(qus=128, qxs=P, u0s=128, uas=256, wss=1024, pl=POOL, p1s=128, p2s=128, ocs=P)),
+    (B, dict(ut=512, u0t=512, xt=640, kt0=1024, kt1=1024, kt2=1024, m0=322, r32=192, r48=3 * NS, mm=3 * ML, sm=150,
+             e0=322, e0s=322, junk=640, oh=192, oht=192, ohs=192, bits=128, bt=128, thr=3 * NS, iq=96, iqt=96, cnt=96,
+             em=3 * ML, ems=3 * ML, es=150, ess=150, fl=NA, cum=NA, sg=3 * NS, bef=3 * NS, befs=3 * NS)),
+    (I, dict(pi=2, bi=8, ci=4, exi=16)),
+    (U, dict(meta=64, ul=16, ex16=16, iq16=6, c16=8, me16=10, o16=4, p16=4, rk16=4, ok16=4, a16=8, s16=4, n16=2,
+             par16=16, own16=4 * R, l16=10)),
+    (H, dict(ml=ML)),
+    (F, dict(mf=64, bf=8, cc=48, it=4 * IT, iw=96, r16=P, dm=P, dm2=96, hm=128, qc=96, bs=100, mei=10, t1k=NS, neg=NS,
+             xc=NA, sml=48, val=128, plw=16, plb=NS, fe=P, fm=P, sp=XQ, sS=NS, sI=NS, sM=NS, uS=NS, uI=NS, uM=NS,
+             uP=R * NS, aS=64, aI=64, aM=64, kb=NS, kt=1040, mx=256, cmp=100, pos=100, dg=P, dgs=P, so=R * 256, eq=NA,
+             eqx=NA, srt=64, tr=32, ti=R * 64, tt=R * 64, yt=P + R * 256, yb=R * P, t16=R * 32, hb=P)),
+):
+    for _k, _n in _l.items():
+        SCRATCH[_k] = ("sbuf", [128, _n], _d)
+PART = {"sab": ("sml", 0, 2), "dab": ("sml", 2, 2), "wab": ("sml", 4, 2), "y1": ("sml", 6, 6), "y2": ("sml", 12, 6),
+        "y3": ("sml", 18, 4), "rw": ("sml", 22, 4), "kw": ("sml", 26, 4), "dk": ("sml", 30, 4), "da": ("sml", 34, 4),
+        "zz": ("sml", 38, 2), "k2": ("sml", 40, 2), "xo16": ("c16", 0, 2), "pw16": ("c16", 2, 2), "cw16": ("c16", 4, 4)}
+SEMAPHORES = ["V", "A", "E", "G", "lu", "lx", "lw", "ls", "m0", "a1", "a2", "m1", "m2", "b1", "b2", "sent",
+              "y0", "y1", "y2", "oc", "os0", "os1"]
+CYCLE, WAKE, LOCAL, FAR, FIRST = 1.0, 60.0, 2000.0, 2500.0, 1500.0
+SKIPS, TURNS, STEP = (0.2, 0.5, 0.9), 8, 500
+
+
+def rank_program(g, core, T, topo):
+    rank = T.rank_of(core)
+    if rank is None:
+        return
+    A_ = AluOpType
+    FN = ActivationFunctionType
+    mate = [r for r in range(N) if topo.mates(core, T.cores[r])][0]
+    peers = [r for r in range(N) if topo.same_plane(core, T.cores[r])]
+    low = min(rank, mate)
+    assert abs(rank - mate) == 1 and len(peers) == 3
+    Q = {"V": g.vector, "A": g.scalar, "E": g.tensor, "G": g, "S": g.sync}
+    nodes = []
+
+    def v(name, a=None, b=None, s=1, p=(0, 128)):
+        name, o, n = PART[name] if name in PART else (name, 0, SCRATCH[name][1][1])
+        a, b = (o, o + n) if a is None else (o + a, o + (a + 1 if b is None else b))
+        ap_ = T[name][p[0]:p[1], a:b:s] if s != 1 else T[name][p[0]:p[1], a:b]
+        if name == "ps":
+            m, pm = 1 << (a // 512), 15
+        else:
+            m = sum(1 << c_ for c_ in range(a, b, s))
+            pm = sum(1 << k for k in range(4) if p[0] < 32 * k + 32 and 32 * k < p[1])
+        return [ap_, [(name, m, pm)], len(range(a, b, s)), SCRATCH[name][2] in (B, H, U), None]
+
+    def by(win, off):
+        return [win[0].indirect(off[0]), win[1] + off[1], 16 * off[2], False, off[1]]
+
+    def w32(x):
+        return [x[0].bitcast(dt.uint32)] + x[1:]
+
+    def w8(x):
+        return [x[0].bitcast(dt.uint8)] + x[1:]
+
+    def add(q, call, outs, ins, cost, sem=None, inc=1, hold=None, after=()):
+        rd, wr = [], []
+        for x in ins:
+            if isinstance(x, list):
+                rd += x[1]
+        for x in outs:
+            wr += x[1][:1]
+            rd += x[4] or []
+        nodes.append({"q": q, "call": call, "rd": rd, "wr": wr, "cost": cost, "sem": sem or q, "inc": inc,
+                      "hold": cost if hold is None else hold, "after": list(after)})
+        return len(nodes) - 1
+
+    def price(o, i, rate, *more):
+        if o[4]:
+            return 50 + 3.5 * o[2] * CYCLE
+        if i[4]:
+            return 55 + 1.6 * i[2] * CYCLE
+        if rate is None:
+            rate = 0.5 if o[3] and i[3] and all(x[3] for x in more) else 1
+        return max(64, rate * i[2]) * CYCLE
+
+    def ap(x):
+        return x[0] if isinstance(x, list) else x
+
+    def cp(o, i):
+        add("V", lambda: g.vector.tensor_copy(o[0], i[0]), [o], [i], price(o, i, None))
+
+    def tt(o, a, b, op):
+        add("V", lambda: g.vector.tensor_tensor(o[0], a[0], b[0], op), [o], [a, b], price(o, a, 2))
+        if a[1][0][2] != b[1][0][2]:
+            nodes[-1]["drain"] = True
+            nodes[-1]["hold"] += WAKE
+
+    def ts(o, a, s1, op0, s2=None, op1=None):
+        if op1 is None:
+            add("V", lambda: g.vector.tensor_scalar(o[0], a[0], ap(s1), None, op0), [o], [a, s1], price(o, a, None))
+        else:
+            add("V", lambda: g.vector.tensor_scalar(o[0], a[0], ap(s1), ap(s2), op0, op1), [o], [a, s1, s2], price(o, a, None))
+
+    def scan(o, d0, d1, op0, op1, init=0.0):
+        add("V", lambda: g.vector.tensor_tensor_scan(o[0], d0[0], d1[0], init, op0, op1), [o], [d0, d1], price(o, d0, None, d1))
+
+    def ms(o, c_):
+        add("V", lambda: g.vector.memset(o[0], c_), [o], [], price(o, o, None))
+
+    def turn(o, i):
+        add("V", lambda: g.vector.transpose(o[0], i[0]), [o], [i], price(o, i, None))
+
+    def total(o, i):
+        add("V", lambda: g.vector.tensor_reduce(o[0], i[0], AxisListType.X, A_.add), [o], [i], price(o, i, 1))
+
+    def quant(c_, s, i):
+        add("V", lambda: g.vector.quantize_mx(c_[0], s[0], i[0]), [c_, s], [i], 12 + 0.22 * i[2])
+
+    def act(o, i, fn=None, bias=None, scale=None, acc=None):
+        kw = {}
+        if bias is not None:
+            kw["bias"] = ap(bias)
+        if scale is not None:
+            kw["scale"] = scale
+        if acc is not None:
+            kw["accum_out"] = acc[0]
+        f = FN.Copy if fn is None else fn
+        add("A", lambda: g.scalar.activation(o[0], i[0], f, **kw), [o] + ([acc] if acc else []), [i, bias], price(o, i, 1) + (20 if acc else 0))
+
+    def mm(bank, lc, ls, a, rc, rs, b, n, start=True, stop=True):
+        o, x = v("ps", 512 * bank, 512 * bank + n), [v(lc, a, a + 128), v(ls, a, a + 128), v(rc, b, b + n), v(rs, b, b + n)]
+        add("E", lambda: g.tensor.matmul_mx(o[0], x[0][0], x[1][0], x[2][0], x[3][0], start, stop), [o], x, 0.63 * (n + 16))
+
+    def iota(o, pat, base=0, ch=0):
+        if SCRATCH[o[1][0][0]][2] == I:
+            add("G", lambda: g.iota(o[0], pat, base, ch), [o], [], 130 + 2 * o[2])
+        else:
+            add("G", lambda: g.iota(o[0], pat, base, ch, allow_small_or_imprecise_dtypes=True), [o], [], 130 + 2 * o[2])
+
+    def dma(q, sem, o, i, more=0):
+        add(q, lambda: Q[q].dma_start(ap(o), ap(i)), [o] if isinstance(o, list) else [], [i], LOCAL + more, sem, 16, 60)
+
+    def pick(oc, os_, a, n, wc_, ws_, wn, off):
+        cp(w32(v(oc, a, a + n)), by(w32(v(wc_, 0, wn)), off))
+        act(v(os_, a, a + n), by(v(ws_, 0, wn), off))
+
+    def send(x, to, sem):
+        ids = []
+        for r in to:
+            rid, pid = topo.addr(T.cores[r], core)
+            ids.append(DstId(rid=rid, pnc=pid))
+        tr = RemoteDMATransfer(dst_ids=ids, dma_engine_mask=topo.mask(core, T.cores[to[0]]), remote_sem=T.sem[sem],
+                               src=x[0], dsts=[x[0]] * len(to))
+        return add("G", lambda: g.remote_dma_fused([tr], local_sem=T.sem.sent), [], [x], 400 * len(to) + FIRST * (sem == "m0"),
+                   "sent", len(topo.engines(core, T.cores[to[0]])))
+
+    def swap(sem, mine, to, theirs):
+        last = [send(x, to, sem) for x in mine]
+        n = sum(len(topo.engines(T.cores[r], core)) for r in to) * len(mine)
+        add("R", None, theirs, [], FAR + 2500 * (sem == "b2"), sem, n, 0, last)
+
+    def pieces(base, w, r, k):
+        return [w8(v("pc", base + w * r, base + w * (r + k))), v("pl", base + w * r, base + w * (r + k))]
+
+    def pair(r):
+        return r - rank + low
+
+    def spread(name, a, b, src):
+        for k, o in enumerate(o for o in range(4) if o != src):
+            (cp if k == 1 else act)(v(name, a, b, p=(32 * o, 32 * o + 32)), v(name, a, b, p=(32 * src, 32 * src + 32)))
+
+    def c(j, n=1):
+        return v("cc", j, j + n)
+
+    dma("S", "lu", v("ut", 0, 56), T.u[:, 0:56])
+    dma("S", "lx", v("xt"), T.x[:], 500)
+    dma("S", "lw", w8(v("wcs")), T.wc[:], 3000)
+    dma("S", "ls", v("wss"), T.ws[:], 3500)
+    iota(v("pi"), [[0, 2]], 0, 1)
+    iota(v("it", 0, IT), [[1, IT]])
+    iota(v("iw"), [[-32, 3], [0, 2], [-2, 16]], P - 32)
+    iota(v("dm"), [[0, 10], [1, 16]])
+    iota(v("exi"), [[16, 2], [32, 4], [0, 2]], 12)
+    iota(v("qc"), [[0, 3], [1, 2], [0, 16]])
+    iota(v("mei"), [[1, 5], [8, 2]])
+    ms(v("ut", 56, 512), 0.0)
+    ms(v("e0", 0, 322, 161), 0.0)
+    ms(v("r32"), 1.0)
+    ms(v("r32", 0, 192, 32), 0.0)
+    ms(v("ul"), 20)
+    cp(c(0), v("pi", 0))
+    ts(v("bi", 0), v("pi", 0), 15, A_.bitwise_and)
+    ts(v("bi", 1), v("pi", 0), 4, A_.logical_shift_right)
+    ts(v("bi", 2), v("pi", 0), 5, A_.logical_shift_right)
+    cp(c(1, 3), v("bi", 0, 3))
+    ts(c(5), c(0), 32.0, A_.add)
+    ts(c(4), c(0), 96.0, A_.is_ge, c(5), A_.mult)
+    ts(v("iw", 64, 96), v("iw", 64, 96), 96.0, A_.add)
+    ts(v("m0", 0, 161), v("it", 0, 161), c(0), A_.not_equal, 2.0, A_.mult)
+    ts(v("m0", 161, 322), v("it", 0, 161), c(5), A_.not_equal, 2.0, A_.mult)
+    ts(v("m0"), v("m0"), -1.0, A_.add)
+    ms(v("m0", 0, 322, 161), 0.0)
+    ts(v("k2"), v("it", 0, 2), 0.0, A_.mult, c(1), A_.add)
+    ts(c(44, 4), v("it", 0, 4), 0.0, A_.mult, c(1), A_.add)
+    ts(v("ul", 0, 8, 2), c(44, 4), 1.0, A_.add)
+    ts(v("ul", 9, 16, 2), c(44, 4), 1.0, A_.add)
+
+    for k in range(4):
+        if k % 2:
+            ts(v("u0t", k, 512, 4), v("ut", 256, 384), v("ut", k), A_.add)
+        else:
+            act(v("u0t", k, 512, 4), v("ut", 256, 384), FN.Identity, bias=v("ut", k))
+    quant(v("u0c"), v("u0s"), v("u0t"))
+    quant(v("qxc"), v("qxs"), v("xt"))
+    mm(0, "qxc", "qxs", 0, "u0c", "u0s", 0, 128)
+    mm(1, "qxc", "qxs", 32, "u0c", "u0s", 0, 128)
+    mm(2, "u0c", "u0s", 0, "qxc", "qxs", 0, P)
+    mm(3, "u0c", "u0s", 0, "qxc", "qxs", 0, P)
+    cp(v("sab", 0), v("ps", 0))
+    act(v("sab", 1), v("ps", 512))
+    for k in range(2):
+        act(v("junk", P * k, P * k + P), v("ps", 1536, 1536 + P), FN.Sign, bias=v("sab", k), scale=-1.0, acc=v("dab", k))
+        ts(v("e0", 161 * k + 1, 161 * k + 161), v("ps", 1024, 1024 + P), v("sab", k), A_.is_equal)
+    scan(v("e0s"), v("e0"), v("m0"), A_.add, A_.mult)
+    tt(v("wab"), v("e0s", 160, 322, 161), v("dab"), A_.add)
+    ts(v("oh", 0, 96), v("iw"), v("wab", 0), A_.is_equal, c(0), A_.mult)
+    ts(v("oh", 96, 192), v("iw"), v("wab", 1), A_.is_equal, c(4), A_.mult)
+    turn(v("oht"), v("oh"))
+    scan(v("ohs"), v("r32"), v("oht"), A_.mult, A_.add)
+    tt(v("y1", p=(0, 64)), v("ohs", 31, 192, 32, p=(0, 64)), v("ohs", 31, 192, 32, p=(64, 128)), A_.add)
+    tt(v("y2", p=(0, 32)), v("y1", p=(0, 32)), v("y1", p=(32, 64)), A_.add)
+    tt(v("y3", 0, 3, p=(0, 32)), v("y2", 0, 3, p=(0, 32)), v("y2", 3, 6, p=(0, 32)), A_.add)
+    spread("y3", 0, 3, 0)
+    cp(v("o16", 0, 3), v("y3", 0, 3))
+
+    def signs(cn, sn, a, b, bank=0):
+        mm(bank, "uac", "uas", 0, cn, sn, a, 128, True, False)
+        mm(bank, "uac", "uas", 128, cn, sn, b, 128, False, True)
+        ts(v("bits"), v("ps", 512 * bank, 512 * bank + 128), 0.0, A_.is_gt)
+        turn(v("bt"), v("bits"))
+        scan(v("val"), v("hm"), v("bt"), A_.mult, A_.add)
+
+    quant(v("quc"), v("qus"), v("ut"))
+    pick("uac", "uas", 0, 256, "quc", "qus", 128, v("ul"))
+    ms(v("hm"), 2.0)
+    ms(v("hm", 0, 128, 16), 0.0)
+    ms(v("hm", 3, 128, 16), 0.0)
+    ms(v("hm", 1, 128, 16), 0.5)
+    ms(v("hm", 2, 128, 16), 0.5)
+    signs("qxc", "qxs", 0, 32, 5)
+    mb = 8 * rank
+    cp(v("meta", mb, mb + 4), v("val", 12, 128, 32))
+    cp(v("meta", mb + 4), v("val", 124))
+    swap("m0", [v("meta", mb, mb + 5)], [mate], [v("meta", 8 * mate, 8 * mate + 5)])
+    pick("pc", "pl", K * rank, K, "qxc", "qxs", P, v("o16", 2))
+    swap("a1", pieces(0, K, rank, 1), [mate], pieces(0, K, mate, 1))
+    cp(v("meta", mb + 5), v("o16", 2))
+    cp(v("meta", mb + 6, mb + 8), v("o16", 0, 2))
+    pick("pc", "pl", X2 + 2 * K * rank, 2 * K, "qxc", "qxs", P, v("o16", 0, 2))
+    swap("m1", [v("meta", mb + 5, mb + 8)], [mate], [v("meta", 8 * mate + 5, 8 * mate + 8)])
+    swap("b1", pieces(X2, 2 * K, rank, 1), [mate], pieces(X2, 2 * K, mate, 1))
+    swap("a2", pieces(0, K, low, 2), peers, sum([pieces(0, K, pair(r), 2) for r in peers], []))
+    swap("m2", [v("meta", 8 * low, 8 * low + 16)], peers, [v("meta", 8 * pair(r), 8 * pair(r) + 16) for r in peers])
+    swap("b2", pieces(X2, 2 * K, low, 2), peers, sum([pieces(X2, 2 * K, pair(r), 2) for r in peers], []))
+
+    quant(v("pc", XQ, KID), v("pl", XQ, KID), v("xt"))
+    mm(4, "wcs", "wss", 0, "qxc", "qxs", 0, P)
+    for k in range(1, 4):
+        act(v("it", IT * k, IT * k + IT), v("it", 0, IT), FN.Identity, bias=float(IT * k))
+    act(v("yt", 0, P), v("ps", 2048, 2048 + P))
+    act(v("hb"), v("it", XQ, KID))
+    ts(c(6, 3), v("it", 0, 3), 16.0, A_.mult, c(1), A_.add)
+    ts(c(9, 3), c(6, 3), -1.0, A_.mult, float(NA - 1), A_.add)
+    ts(c(18, 3), c(9, 3), -(CAPP - 1) / 2, A_.add, 1.0 / CAPP, A_.mult)
+    cp(v("ci", 0, 3), c(18, 3))
+    cp(c(12, 3), v("ci", 0, 3))
+    ts(c(32, 3), c(12, 3), -float(CAPP), A_.mult)
+    tt(c(15, 3), c(32, 3), c(9, 3), A_.add)
+    ts(c(21, 3), c(6, 3), 1.0, A_.add)
+    ms(v("bs"), 1000.0)
+    ts(v("bs", 0, 99, 33), c(12, 3), 32.0 / 256, A_.mult)
+    ts(c(35, 3), c(12, 3), 4.0, A_.is_ge, -112.0, A_.mult)
+    ts(c(38, 3), c(12, 3), 32.0, A_.mult, 2.0, A_.add)
+    tt(c(27, 3), c(35, 3), c(38, 3), A_.add)
+    cp(v("iq16", 0, 6, 2), c(27, 3))
+    cp(v("iq16", 1, 6, 2), c(27, 3))
+    cp(v("ex16"), v("exi"))
+    ts(c(30), c(3), 2.0, A_.mult)
+    ts(v("qc"), v("qc"), c(30), A_.add, 0.25, A_.mult)
+    ts(c(31), c(3), 16.0, A_.mult)
+    ts(v("me16"), v("mei"), c(31), A_.add)
+    ts(v("dm"), v("dm"), c(1), A_.is_equal)
+    ts(v("dm2", 0, 48), v("dm", 0, 48), -1.0, A_.mult)
+    cp(v("dm2", 48, 96), v("dm", 0, 48))
+    ms(v("r16"), 1.0)
+    ms(v("r16", 0, P, 16), 0.0)
+    ms(v("r48"), 1.0)
+    ms(v("r48", 0, 3 * NS, NS), 0.0)
+    for k in range(3):
+        ts(v("mm", ML * k, ML * k + ML), v("it", 0, ML), c(6 + k), A_.is_gt)
+        ts(v("sm", 50 * k, 50 * k + 50), v("it", 0, 50), c(21 + k), A_.not_equal, 2.0, A_.mult)
+    ts(v("sm"), v("sm"), -1.0, A_.add)
+    ms(v("sm", 0, 150, 50), 0.0)
+    ms(v("es", 0, 150, 50), 0.0)
+    ms(v("es", 49, 150, 50), float(NA))
+    for t in range(R):
+        ms(v("so", 256 * t, 256 * t + 2 * NA), 0.0)
+    ms(v("kt", 256, MO), 0.0)
+    ms(v("kt", MO + 256, 1040), -1.0)
+    ms(v("neg"), -1.0)
+    ts(v("t1k"), v("it", 0, NS), float(K), A_.is_ge, 1000.0, A_.mult)
+    ts(v("xc"), v("it", 0, NA), float(K), A_.add)
+    ts(c(24), c(1), 1.0, A_.add)
+    cp(v("rw", 0, 3), c(6, 3))
+    cp(v("rk16", 0, 3), c(6, 3))
+    ts(c(25), c(2), 16.0, A_.mult)
+    ts(c(26), c(2), 32.0, A_.mult, float(X2 - K), A_.add)
+    ts(v("sI", 0, K), v("it", 0, K), c(25), A_.add)
+    ts(v("sI", K, NS), v("it", K, NS), c(26), A_.add)
+    cp(v("cw16", 0), c(0))
+    ts(v("cw16", 1, 3), c(7, 2), c(26), A_.add)
+    ts(c(41), c(1), 2.0, A_.min, 5.0, A_.add)
+    ts(v("pw16", 0), c(2), 8.0, A_.mult, c(41), A_.add)
+    for k, sh in enumerate((6, 5, 2, 1, 0)):
+        ts(v("bi", 3 + k), v("pi", 0), sh, A_.logical_shift_right, 1, A_.bitwise_and)
+    cp(v("bf", 3, 8), v("bi", 3, 8))
+    tt(v("bf", 0, 2), v("bf", 3, 5), v("bf", 5, 7), A_.not_equal)
+    ts(c(42), v("bf", 7), 16.0, A_.mult)
+    ts(c(43), v("bf", 0), 8.0, A_.mult, c(42), A_.add)
+    ts(v("xo16", 0), v("bf", 1), 4.0, A_.mult, c(43), A_.add)
+
+    cp(v("mf"), v("meta"))
+    cp(v("plw"), by(v("mf"), v("pw16", 0)))
+    act(v("fe"), by(v("mf"), v("me16")))
+    cp(v("p16", 0, 3), v("plw", 0, 3))
+    turn(v("fm"), v("fe"))
+    act(v("plb"), by(v("it", 0, P), v("p16", 0, 3)))
+    act(v("sM"), by(v("fm"), v("p16", 0, 3)))
+    cp(by(v("fm"), v("p16", 0, 3)), v("neg"))
+    act(v("ml", ML - P, ML), v("fm"))
+    for k in range(3):
+        ts(v("thr", NS * k, NS * k + NS), v("plb"), v("plw", k), A_.is_lt, 0.5, A_.subtract)
+
+    def opens(t):
+        ts(v("kw", 0, 3), v("rw", 0, 3), float(K), A_.is_ge, 1000.0, A_.mult)
+        tt(v("kb"), by(v("t1k"), v("rk16", 0, 3)), v("plb"), A_.add)
+        tt(v("kw", 0, 3), v("kw", 0, 3), v("plw", 0, 3), A_.add)
+        for k in range(3):
+            act(v("junk", 320 + NS * k, 320 + NS * k + NS), v("kb"), FN.Sign, bias=v("kw", k), scale=-1.0, acc=v("dk", k))
+        ts(v("ok16", 0, 3), v("dk", 0, 3), float(NS - 1), A_.add, 0.5, A_.mult)
+        o = v("ok16", 0, 3)
+        cp(by(v("uM"), o), v("sM"))
+        act(v("ml", NA, NA + NS - K), v("uM", K, NS))
+        cp(by(v("uI"), o), v("sI"))
+        cp(by(v("uP", NS * t, NS * t + NS), o), v("plb"))
+        act(v("aI", 0, K), v("uI", 0, K))
+        act(v("ti", 64 * t + 32, 64 * t + 48), v("uP", NS * t, NS * t + K))
+        act(v("ti", 64 * t + 48, 64 * t + 64), v("uP", NS * t, NS * t + K))
+        if t < R - 1:
+            act(v("aM", 0, K), v("uM", 0, K))
+
+    oq, oh_ = (32 * (rank // 2), 32 * (rank // 2) + 32), 16 * (rank % 2)
+
+    def outputs(t):
+        h = 64 * t + oh_
+        turn(v("tt", 64 * t, 64 * t + 64), v("ti", 64 * t, 64 * t + 64))
+        ts(v("tt", 33 + h, p=oq), v("tt", h, p=oq), float(XQ), A_.subtract, v("tt", 32 + h, p=oq), A_.max)
+        spread("tt", 32 + h, 34 + h, rank // 2)
+        cp(v("own16", 4 * t, 4 * t + 4, 2), v("tt", 32 + h, 34 + h))
+        n, at, new = P + 256 * (t + 1), v("own16", 4 * t), v("own16", 4 * t + 2)
+        cols, ys = v("t16", 32 * t + 16, 32 * t + 32), v("t16", 32 * t, 32 * t + 16)
+        if t == R - 1:
+            ts(cols, by(v("it", 0, n), new), float(XQ), A_.add)
+        else:
+            act(cols, by(v("it", 0, n), new), FN.Identity, bias=float(XQ))
+        act(ys, by(v("yt", 0, n), new))
+        cp(by(v("hb"), at), cols)
+        cp(by(v("yb", P * t, P * t + P), at), ys)
+        dma("S", "y%d" % t, T.y[:, P * t:P * t + P], v("yb", P * t, P * t + P))
+
+    par = [("pc", "pl"), ("p1c", "p1s"), ("p2c", "p2s")]
+    for t in range(R):
+        kid, tile = KID + 256 * t, "kt%d" % t
+        opens(t)
+        for i in range(8):
+            mm(i, "wcs", "wss", 128 * i, par[t][0], par[t][1], 0, 128)
+        for i in range(8):
+            o, z = v(tile, i, 1024, 8), v("ps", 512 * i, 512 * i + 128)
+            if i % 2:
+                ts(o, z, 0.0, A_.max, 0.05, A_.mult)
+            else:
+                act(o, z, FN.Relu, scale=0.05)
+        quant(v("pc", kid, kid + 256), v("pl", kid, kid + 256), v(tile))
+        signs("pc", "pl", kid, kid + 128)
+        mm(1, "u0c", "u0s", 0, "pc", "pl", kid, 256)
+        mm(2, "wcs", "wss", 0, "pc", "pl", kid, 256)
+        act(v("kt", 0, 256), v("ps", 512, 768))
+        act(v("mx"), by(v("val"), v("ex16")))
+        tt(v("iq"), by(v("val"), v("iq16")), v("qc"), A_.is_equal)
+        turn(v("iqt"), v("iq"))
+        scan(v("cnt"), v("r32", 0, 96), v("iqt"), A_.mult, A_.add)
+        for k in range(3):
+            ts(v("cmp", 33 * k, 33 * k + 32), v("cnt", 32 * k, 32 * k + 32), c(15 + k), A_.is_le, 1.0 / 256, A_.mult)
+        tt(v("cmp", 32, 99, 33), v("cnt", 31, 96, 32), c(15, 3), A_.is_le)
+        turn(v("kt", MO, MO + 256), v("mx"))
+        scan(v("pos", 0, 99), v("bs", 0, 99), v("cmp", 0, 99), A_.min, A_.add, 1000.0)
+        ts(v("a16", 0, 3), v("pos", 32, 99, 33), 256.0, A_.mult)
+        ts(v("a16", 3, 6), v("pos", 32, 99, 33), 256.0, A_.mult, float(MO), A_.add)
+        tt(v("dg", 0, 96), by(v("kt"), v("a16", 0, 6)), v("dm2"), A_.mult)
+        act(v("ml", 0, NA), by(v("kt", MO, 1040), v("a16", 0, 3)))
+        act(v("aS", K, 64), by(v("kt", 0, MO), v("a16", 0, 3)))
+        scan(v("dgs", 0, 96), v("r16", 0, 96), v("dg", 0, 96), A_.mult, A_.add)
+        for k in range(3):
+            act(v("junk", 480 + NA * k, 480 + NA * k + NA), v("aS", K, 64), FN.Sign, bias=v("dgs", 16 * k + 15), acc=v("da", k))
+        act(v("aI", K, 64), by(v("it", 0, MO), v("a16", 0, 3)), FN.Identity, bias=float(kid))
+        if t < R - 1:
+            act(v("aM", K, 64), by(v("kt", MO, 1040), v("a16", 0, 3)))
+        act(v("yt", P + 256 * t, P + 256 * t + 256), v("ps", 1024, 1280))
+        act(v("yb", P * t, P * t + P), v("yt", 0, P) if t == 0 else v("yb", P * t - P, P * t))
+        if t == 0:
+            mm(3, "u0c", "u0s", 0, "pc", "pl", 0, XQ)
+            act(v("sp"), v("ps", 1536, 1536 + XQ))
+            act(v("sS"), by(v("sp"), v("cw16", 0, 3)))
+        for k in range(3):
+            ts(v("em", ML * k, ML * k + ML), v("ml"), v("dgs", 63 + 16 * k), A_.is_equal, 128.0, A_.mult)
+        for k in range(3):
+            ts(v("es", 50 * k + 1, 50 * k + 49), v("aS", K, 64), v("dgs", 16 * k + 15), A_.add, 0.0, A_.is_equal)
+        scan(v("ems"), v("em"), v("mm"), A_.max, A_.mult)
+        scan(v("ess"), v("es"), v("sm"), A_.add, A_.mult)
+        for k in range(3):
+            ts(v("s16", k), v("da", k), v("ess", 50 * k + 49), A_.add, v("ems", ML * k + ML - 1), A_.add)
+        cp(by(v("so", 256 * t, 256 * t + 256), v("s16", 0, 3)), v("xc"))
+        srt = v("so", 256 * t, 256 * t + 2 * NA, 2)
+        ts(v("fl"), srt, 1.0, A_.min)
+        scan(v("cum"), v("fl"), v("fl"), A_.add, A_.max)
+        ts(v("eq"), v("cum"), c(24), A_.is_equal)
+        tt(v("eqx"), v("eq"), srt, A_.mult)
+        if t < R - 1:
+            cp(by(v("uS"), v("ok16", 0, 3)), v("sS"))
+            act(v("aS", 0, K), v("uS", 0, K))
+        total(v("zz", 0), v("eqx"))
+        ts(v("n16"), v("k2"), v("zz", 0), A_.max)
+        if t == R - 1:
+            cp(v("ti", 64 * t, 64 * t + 32), by(v("aI"), v("n16")))
+            outputs(t)
+            break
+        nc = t + 2
+        n = K * nc
+        o = v("ok16", 0, 3)
+        cp(v("uS", 0, K), by(v("aS"), v("n16", 0)))
+        act(v("uI", 0, K), by(v("aI"), v("n16", 0)))
+        tt(v("dg", 0, NS), by(v("uS"), o), v("dm", 0, NS), A_.mult)
+        act(v("sS"), by(v("uS"), o))
+        scan(v("dgs", 0, NS), v("r16", 0, NS), v("dg", 0, NS), A_.mult, A_.add)
+        act(v("sI"), by(v("uI"), o))
+        for k in range(nc):
+            act(v("sg", n * k, n * k + n), v("sS", 0, n), FN.Sign, bias=v("dgs", 16 * k + 15), scale=-1.0)
+        act(v("ti", 64 * t, 64 * t + 32), by(v("aI"), v("n16")))
+        act(v("uM", 0, K), by(v("aM"), v("n16", 0)))
+        act(v("sM"), by(v("uM"), o))
+        if nc == 3:
+            tt(v("bef"), v("sg"), v("thr"), A_.is_lt)
+            scan(v("befs"), v("r48"), v("bef"), A_.mult, A_.add)
+        else:
+            for k in range(nc):
+                tt(v("bef", n * k, n * k + n), v("sg", n * k, n * k + n), v("thr", NS * k, NS * k + n), A_.is_lt)
+            scan(v("befs", 0, n * nc), v("r32", 0, n * nc), v("bef", 0, n * nc), A_.mult, A_.add)
+        cp(v("rk16", 0, nc), v("befs", n - 1, n * nc, n))
+        cp(by(v("srt", 16, 64), v("rk16", 0, nc)), v("sI", 0, n))
+        act(v("srt", 0, 16), v("srt", 16, 32))
+        turn(v("tr"), v("srt", 0, 32))
+        cp(v("tr", 8, 32, 16, p=(0, 64)), v("tr", 0, 32, 16, p=(64, 128)))
+        act(v("tr", 8, 32, 16, p=(64, 128)), v("tr", 0, 32, 16, p=(0, 64)))
+        for a in range(4):
+            o_, i_ = v("tr", 4, 32, 8, p=(32 * a, 32 * a + 32)), v("tr", 0, 32, 8, p=(32 * (a ^ 1), 32 * (a ^ 1) + 32))
+            if a % 2:
+                act(o_, i_)
+            else:
+                cp(o_, i_)
+        cp(v("par16"), by(v("tr"), v("xo16", 0)))
+        pick(par[t + 1][0], par[t + 1][1], 0, 128, "pc", "pl", kid + 256, v("par16", 0, 8))
+        act(v("rw", 0, nc), v("befs", n - 1, n * nc, n))
+        outputs(t)
+
+    tt(v("dg"), v("hb"), v("dm"), A_.mult)
+    scan(v("dgs"), v("r16"), v("dg"), A_.mult, A_.add)
+    cp(v("l16"), v("dgs", 15, P, 16))
+    pick("occ", "ocs", 0, P, "pc", "pl", POOL, v("l16"))
+    dma("S", "oc", T.oc[:], w8(v("occ")))
+    for k in range(4):
+        dma("A" if k % 2 else "S", "os%d" % (k % 2), T.osc[4 * k:4 * k + 4, :], v("ocs", p=(32 * k, 32 * k + 4)))
+
+    log, last = {}, {}
+    for i, x in enumerate(nodes):
+        need = {j: True for j in x["after"]}
+        if x["q"] in "GS":
+            if x["q"] in last:
+                need[last[x["q"]]] = False
+            last[x["q"]] = i
+        for regs, write in ((x["rd"], False), (x["wr"], True)):
+            for name, m, pm in regs:
+                for em, ep, ew, j in log.get(name, []):
+                    if em & m and ep & pm and (write or ew or name == "ps"):
+                        y = nodes[j]
+                        inorder = y["q"] == x["q"] == y["sem"] and (x["q"] == "E" or not (write or ew))
+                        need[j] = need.get(j, False) or not inorder
+        for regs, write in ((x["rd"], False), (x["wr"], True)):
+            for name, m, pm in regs:
+                log.setdefault(name, []).append((m, pm, write, i))
+        x["need"] = need
+    users = [[] for x in nodes]
+    for i, x in enumerate(nodes):
+        for j in x["need"]:
+            users[j].append(i)
+
+    def arrange(skip, more):
+        tail = list(more)
+        for i in range(len(nodes) - 1, -1, -1):
+            tail[i] += nodes[i]["cost"]
+            for j, done in nodes[i]["need"].items():
+                tail[j] = max(tail[j], tail[i] + WAKE if done else tail[i] - nodes[j]["cost"] + nodes[j]["hold"])
+        free, start, left = {}, {}, [len(x["need"]) for x in nodes]
+        ready = {i: 0.0 for i in range(len(nodes)) if not left[i]}
+        plan_ = []
+        while ready:
+            est = {i: max(r, free.get(nodes[i]["q"], 0.0)) for i, r in ready.items()}
+            i = min(est, key=lambda k: (est[k], -tail[k]))
+            q, lim = nodes[i]["q"], est[i] + skip * nodes[i]["hold"]
+            i = max((j for j in est if j == i or nodes[j]["q"] == q and est[j] < lim), key=lambda k: tail[k])
+            start[i] = est[i]
+            free[q] = est[i] + nodes[i]["hold"]
+            plan_.append(i)
+            del ready[i]
+            for j in users[i]:
+                left[j] -= 1
+                if not left[j]:
+                    ready[j] = max(start[k] + (nodes[k]["cost"] + WAKE if d else 0) for k, d in nodes[j]["need"].items())
+        return plan_, tail
+
+    def span(plan_, own, other):
+        free, end, why, late = {}, {}, {}, {}
+        for i in plan_:
+            x = nodes[i]
+            r = max([(0.0, -1)] + [(end[j] + (own if nodes[j]["q"] == x["q"] else other), j) for j, d in x["need"].items() if d])
+            s0, why[i] = max(r, free.get(x["q"], (0.0, -1)))
+            late[i] = s0 - r[0]
+            free[x["q"]], end[i] = (s0 + x["hold"], i), s0 + x["cost"]
+        i = max(end, key=lambda k: end[k])
+        t_, off = end[i], []
+        while i >= 0:
+            if late[i] > 400:
+                off.append(i)
+            i = why[i]
+        return t_, off
+
+    best = None
+    for skip in SKIPS:
+        more = [0.0] * len(nodes)
+        for again in range(TURNS):
+            plan, tail = arrange(skip, more)
+            t_, off = span(plan, 60, 60)
+            t_ += span(plan, 0, 100)[0] + span(plan, 120, 120)[0]
+            if best is None or t_ < best[0]:
+                best = (t_, plan)
+            for i in off:
+                more[i] = tail[i] + STEP
+    count, seen, drain = {}, {q: {} for q in Q}, []
+    for i in best[1]:
+        x = nodes[i]
+        if x["q"] != "R":
+            waits = {}
+            if x["q"] == "V":
+                x["need"].update({j: True for j in drain})
+                drain[:] = [i] if x.get("drain") else []
+            for j, done in x["need"].items():
+                s_, val = nodes[j]["sem"], nodes[j]["val"]
+                if done and seen[x["q"]].get(s_, 0) < val:
+                    seen[x["q"]][s_] = waits[s_] = val
+            for s_, val in waits.items():
+                Q[x["q"]].wait_ge(T.sem[s_], val)
+            ins = x["call"]()
+            if x["sem"] != "sent":
+                ins.then_inc(T.sem[x["sem"]], x["inc"])
+        count[x["sem"]] = count.get(x["sem"], 0) + x["inc"]
+        x["val"] = count[x["sem"]]
+    for s_ in SEMAPHORES:
+        g.wait_ge(T.sem[s_], count[s_])

@@ -17,23 +17,25 @@ for _d, _l in (
              e0=322, e0s=322, junk=640, oh=192, oht=192, ohs=192, bits=128, bt=128, thr=3 * NS, iq=96, iqt=96, cnt=96,
              em=3 * ML, ems=3 * ML, es=150, ess=150, fl=NA, cum=NA, sg=3 * NS, bef=3 * NS, befs=3 * NS)),
     (I, dict(pi=2, bi=8, ci=4, exi=16)),
-    (U, dict(meta=64, ul=16, ex16=16, iq16=6, c16=8, me16=10, o16=4, p16=4, rk16=4, ok16=4, a16=8, s16=4, n16=2,
-             par16=16, own16=4 * R, l16=10)),
+    (U, dict(meta=64, ul=16, ex16=16, iq16=6, c16=10, me16=10, o16=4, p16=4, rk16=4, ok16=4, a16=8, s16=4, n16=2,
+             par16=16, own16=4 * R, l16=16)),
     (H, dict(ml=ML)),
-    (F, dict(mf=64, bf=8, cc=48, it=4 * IT, iw=96, r16=P, dm=P, dm2=96, hm=128, qc=96, bs=100, mei=10, t1k=NS, neg=NS,
-             xc=NA, sml=48, val=128, plw=16, plb=NS, fe=P, fm=P, sp=XQ, sS=NS, sI=NS, sM=NS, uS=NS, uI=NS, uM=NS,
-             uP=R * NS, aS=64, aI=64, aM=64, kb=NS, kt=1040, mx=256, cmp=100, pos=100, dg=P, dgs=P, so=R * 256, eq=NA,
-             eqx=NA, srt=64, tr=32, ti=R * 64, tt=R * 64, yt=P + R * 256, yb=R * P, t16=R * 32, hb=P)),
+    (F, dict(mf=64, bf=8, cc=48, it=4 * IT, iw=96, r16=96, dm=96, dm2=96, hm=128, qc=96, bs=100, mei=10, t1k=NS, neg=NS,
+             xc=NA, sml=48, val=128, plw=16, plb=NS, fe=P, fm=P, sp=XQ, sS=NS, sI=NS, sM=NS, uS=R * 96, uI=R * NS,
+             uM=R * NS, sw=2 * 96, swd=96, so2=512, cap=NA, ys=NA, zs=64, aS=64, aI=64, aM=64, kb=NS, kt=1040, mx=256,
+             cmp=100, pos=100, dg=96, dgs=96, so=R * 256, eq=NA, eqx=NA, srt=64, tr=32, ti=R * 64, tt=R * 64,
+             yt=P + R * 256, yb=R * P, t16=R * 32, hb=P + 32, ht=352)),
 ):
     for _k, _n in _l.items():
         SCRATCH[_k] = ("sbuf", [128, _n], _d)
 PART = {"sab": ("sml", 0, 2), "dab": ("sml", 2, 2), "wab": ("sml", 4, 2), "y1": ("sml", 6, 6), "y2": ("sml", 12, 6),
         "y3": ("sml", 18, 4), "rw": ("sml", 22, 4), "kw": ("sml", 26, 4), "dk": ("sml", 30, 4), "da": ("sml", 34, 4),
-        "zz": ("sml", 38, 2), "k2": ("sml", 40, 2), "xo16": ("c16", 0, 2), "pw16": ("c16", 2, 2), "cw16": ("c16", 4, 4)}
+        "zz": ("sml", 38, 2), "k2": ("sml", 40, 2), "xo16": ("c16", 0, 2), "pw16": ("c16", 2, 2), "cw16": ("c16", 4, 4),
+        "ho16": ("c16", 8, 2)}
 SEMAPHORES = ["V", "A", "E", "G", "lu", "lx", "lw", "ls", "m0", "a1", "a2", "m1", "m2", "b1", "b2", "sent",
               "y0", "y1", "y2", "oc", "os0", "os1"]
-CYCLE, WAKE, LOCAL, FAR, FIRST = 1.0, 60.0, 2000.0, 2500.0, 1500.0
-SKIPS, TURNS, STEP = (0.2, 0.5, 0.9), 8, 500
+CYCLE, WAKE, LOCAL, FAR, FIRST = 0.95, 120.0, 2000.0, 2500.0, 1500.0
+SKIPS, TURNS, STEP = (0.2, 0.5, 0.9), 6, 500
 
 
 def rank_program(g, core, T, topo):
@@ -186,7 +188,7 @@ def rank_program(g, core, T, topo):
     iota(v("pi"), [[0, 2]], 0, 1)
     iota(v("it", 0, IT), [[1, IT]])
     iota(v("iw"), [[-32, 3], [0, 2], [-2, 16]], P - 32)
-    iota(v("dm"), [[0, 10], [1, 16]])
+    iota(v("dm"), [[0, 6], [1, 16]])
     iota(v("exi"), [[16, 2], [32, 4], [0, 2]], 12)
     iota(v("qc"), [[0, 3], [1, 2], [0, 16]])
     iota(v("mei"), [[1, 5], [8, 2]])
@@ -237,8 +239,8 @@ def rank_program(g, core, T, topo):
     tt(v("y1", p=(0, 64)), v("ohs", 31, 192, 32, p=(0, 64)), v("ohs", 31, 192, 32, p=(64, 128)), A_.add)
     tt(v("y2", p=(0, 32)), v("y1", p=(0, 32)), v("y1", p=(32, 64)), A_.add)
     tt(v("y3", 0, 3, p=(0, 32)), v("y2", 0, 3, p=(0, 32)), v("y2", 3, 6, p=(0, 32)), A_.add)
-    spread("y3", 0, 3, 0)
-    cp(v("o16", 0, 3), v("y3", 0, 3))
+    for a in range(4):
+        cp(v("o16", 0, 3, p=(32 * a, 32 * a + 32)), v("y3", 0, 3, p=(0, 32)))
 
     def signs(cn, sn, a, b, bank=0):
         mm(bank, "uac", "uas", 0, cn, sn, a, 128, True, False)
@@ -275,7 +277,7 @@ def rank_program(g, core, T, topo):
     for k in range(1, 4):
         act(v("it", IT * k, IT * k + IT), v("it", 0, IT), FN.Identity, bias=float(IT * k))
     act(v("yt", 0, P), v("ps", 2048, 2048 + P))
-    act(v("hb"), v("it", XQ, KID))
+    act(v("hb"), v("it", XQ - 16, KID + 16))
     ts(c(6, 3), v("it", 0, 3), 16.0, A_.mult, c(1), A_.add)
     ts(c(9, 3), c(6, 3), -1.0, A_.mult, float(NA - 1), A_.add)
     ts(c(18, 3), c(9, 3), -(CAPP - 1) / 2, A_.add, 1.0 / CAPP, A_.mult)
@@ -300,7 +302,7 @@ def rank_program(g, core, T, topo):
     ts(v("dm2", 0, 48), v("dm", 0, 48), -1.0, A_.mult)
     cp(v("dm2", 48, 96), v("dm", 0, 48))
     ms(v("r16"), 1.0)
-    ms(v("r16", 0, P, 16), 0.0)
+    ms(v("r16", 0, 96, 16), 0.0)
     ms(v("r48"), 1.0)
     ms(v("r48", 0, 3 * NS, NS), 0.0)
     for k in range(3):
@@ -317,7 +319,10 @@ def rank_program(g, core, T, topo):
     ms(v("neg"), -1.0)
     ts(v("t1k"), v("it", 0, NS), float(K), A_.is_ge, 1000.0, A_.mult)
     ts(v("xc"), v("it", 0, NA), float(K), A_.add)
-    ts(c(24), c(1), 1.0, A_.add)
+    ts(c(24), c(1), 1.0, A_.add, 64.0, A_.mult)
+    ts(v("k2"), v("k2"), c(24), A_.subtract)
+    for t in range(R - 1):
+        ms(v("so2", 256 * t, 256 * t + 2 * NA), 0.0)
     cp(v("rw", 0, 3), c(6, 3))
     cp(v("rk16", 0, 3), c(6, 3))
     ts(c(25), c(2), 16.0, A_.mult)
@@ -335,6 +340,13 @@ def rank_program(g, core, T, topo):
     ts(c(42), v("bf", 7), 16.0, A_.mult)
     ts(c(43), v("bf", 0), 8.0, A_.mult, c(42), A_.add)
     ts(v("xo16", 0), v("bf", 1), 4.0, A_.mult, c(43), A_.add)
+    ts(v("ci", 3), v("pi", 0), 4, A_.logical_shift_right, 1, A_.bitwise_and)
+    cp(v("bf", 2), v("ci", 3))
+    ts(c(18), v("bf", 7), v("bf", 2), A_.not_equal, float(P), A_.mult)
+    ts(c(19), v("bf", 2), -32.0, A_.mult, 16.0, A_.add)
+    ts(c(20), v("bf", 7), c(19), A_.mult, c(18), A_.add)
+    ts(c(32), c(1), 16.0, A_.mult, 144.0, A_.min)
+    ts(v("ho16", 0), c(32), c(20), A_.add)
 
     cp(v("mf"), v("meta"))
     cp(v("plw"), by(v("mf"), v("pw16", 0)))
@@ -345,43 +357,54 @@ def rank_program(g, core, T, topo):
     act(v("sM"), by(v("fm"), v("p16", 0, 3)))
     cp(by(v("fm"), v("p16", 0, 3)), v("neg"))
     act(v("ml", ML - P, ML), v("fm"))
-    for k in range(3):
-        ts(v("thr", NS * k, NS * k + NS), v("plb"), v("plw", k), A_.is_lt, 0.5, A_.subtract)
+
+    def held(name, t, a=0, b=NS):
+        if t < 0:
+            return v({"uS": "sS", "uI": "sI", "uM": "sM", "uP": "plb"}[name], a, b)
+        name, o = {"uS": ("uS", 96 * t), "uP": ("uS", 96 * t + NS)}.get(name, (name, NS * t))
+        return v(name, o + a, o + b)
 
     def opens(t):
         ts(v("kw", 0, 3), v("rw", 0, 3), float(K), A_.is_ge, 1000.0, A_.mult)
-        tt(v("kb"), by(v("t1k"), v("rk16", 0, 3)), v("plb"), A_.add)
-        tt(v("kw", 0, 3), v("kw", 0, 3), v("plw", 0, 3), A_.add)
+        tt(v("kb"), by(v("t1k"), v("rk16", 0, 3)), held("uP", t - 1), A_.add)
+        tt(v("kw", 0, 3), v("kw", 0, 3), v("sw", 96 * t - 33, 96 * t, 16) if t else v("plw", 0, 3), A_.add)
         for k in range(3):
             act(v("junk", 320 + NS * k, 320 + NS * k + NS), v("kb"), FN.Sign, bias=v("kw", k), scale=-1.0, acc=v("dk", k))
         ts(v("ok16", 0, 3), v("dk", 0, 3), float(NS - 1), A_.add, 0.5, A_.mult)
         o = v("ok16", 0, 3)
-        cp(by(v("uM"), o), v("sM"))
-        act(v("ml", NA, NA + NS - K), v("uM", K, NS))
-        cp(by(v("uI"), o), v("sI"))
-        cp(by(v("uP", NS * t, NS * t + NS), o), v("plb"))
-        act(v("aI", 0, K), v("uI", 0, K))
-        act(v("ti", 64 * t + 32, 64 * t + 48), v("uP", NS * t, NS * t + K))
-        act(v("ti", 64 * t + 48, 64 * t + 64), v("uP", NS * t, NS * t + K))
+        for name in ("uM", "uI", "uP"):
+            cp(by(held(name, t), o), held(name, t - 1))
+        act(v("ml", NA, NA + NS - K), held("uM", t, K))
+        act(v("ti", 64 * t + 32, 64 * t + 48), held("uP", t, 0, K))
+        act(v("ti", 64 * t + 48, 64 * t + 64), held("uP", t, 0, K))
         if t < R - 1:
-            act(v("aM", 0, K), v("uM", 0, K))
+            act(v("aI", 0, K), held("uI", t, 0, K))
+            act(v("aM", 0, K), held("uM", t, 0, K))
+        else:
+            act(v("zs", 0, K), held("uI", t, 0, K), FN.Identity, bias=-float(XQ))
+            tt(v("aI", 0, K), v("zs", 0, K), held("uP", t, 0, K), A_.max)
 
     oq, oh_ = (32 * (rank // 2), 32 * (rank // 2) + 32), 16 * (rank % 2)
 
     def outputs(t):
         h = 64 * t + oh_
         turn(v("tt", 64 * t, 64 * t + 64), v("ti", 64 * t, 64 * t + 64))
-        ts(v("tt", 33 + h, p=oq), v("tt", h, p=oq), float(XQ), A_.subtract, v("tt", 32 + h, p=oq), A_.max)
-        spread("tt", 32 + h, 34 + h, rank // 2)
-        cp(v("own16", 4 * t, 4 * t + 4, 2), v("tt", 32 + h, 34 + h))
         n, at, new = P + 256 * (t + 1), v("own16", 4 * t), v("own16", 4 * t + 2)
+        if t < R - 1:
+            ts(v("tt", 33 + h, p=oq), v("tt", h, p=oq), float(XQ), A_.subtract, v("tt", 32 + h, p=oq), A_.max)
+            spread("tt", 32 + h, 34 + h, rank // 2)
+            cp(v("own16", 4 * t, 4 * t + 4, 2), v("tt", 32 + h, 34 + h))
+        else:
+            at, new = new, at
+            for a in range(4):
+                cp(v("own16", 4 * t, 4 * t + 4, 2, p=(32 * a, 32 * a + 32)), v("tt", h, h + 33, 32, p=oq))
         cols, ys = v("t16", 32 * t + 16, 32 * t + 32), v("t16", 32 * t, 32 * t + 16)
         if t == R - 1:
             ts(cols, by(v("it", 0, n), new), float(XQ), A_.add)
         else:
             act(cols, by(v("it", 0, n), new), FN.Identity, bias=float(XQ))
         act(ys, by(v("yt", 0, n), new))
-        cp(by(v("hb"), at), cols)
+        cp(by(v("hb", 16, 16 + P), at), cols)
         cp(by(v("yb", P * t, P * t + P), at), ys)
         dma("S", "y%d" % t, T.y[:, P * t:P * t + P], v("yb", P * t, P * t + P))
 
@@ -419,7 +442,7 @@ def rank_program(g, core, T, topo):
         scan(v("dgs", 0, 96), v("r16", 0, 96), v("dg", 0, 96), A_.mult, A_.add)
         for k in range(3):
             act(v("junk", 480 + NA * k, 480 + NA * k + NA), v("aS", K, 64), FN.Sign, bias=v("dgs", 16 * k + 15), acc=v("da", k))
-        act(v("aI", K, 64), by(v("it", 0, MO), v("a16", 0, 3)), FN.Identity, bias=float(kid))
+        act(v("aI", K, 64), by(v("it", 0, MO), v("a16", 0, 3)), FN.Identity, bias=float(kid - XQ * (t == R - 1)))
         if t < R - 1:
             act(v("aM", K, 64), by(v("kt", MO, 1040), v("a16", 0, 3)))
         act(v("yt", P + 256 * t, P + 256 * t + 256), v("ps", 1024, 1280))
@@ -438,42 +461,38 @@ def rank_program(g, core, T, topo):
             ts(v("s16", k), v("da", k), v("ess", 50 * k + 49), A_.add, v("ems", ML * k + ML - 1), A_.add)
         cp(by(v("so", 256 * t, 256 * t + 256), v("s16", 0, 3)), v("xc"))
         srt = v("so", 256 * t, 256 * t + 2 * NA, 2)
-        ts(v("fl"), srt, 1.0, A_.min)
+        ts(v("fl"), srt, 1.0, A_.min, 64.0, A_.mult)
         scan(v("cum"), v("fl"), v("fl"), A_.add, A_.max)
-        ts(v("eq"), v("cum"), c(24), A_.is_equal)
-        tt(v("eqx"), v("eq"), srt, A_.mult)
-        if t < R - 1:
-            cp(by(v("uS"), v("ok16", 0, 3)), v("sS"))
-            act(v("aS", 0, K), v("uS", 0, K))
-        total(v("zz", 0), v("eqx"))
-        ts(v("n16"), v("k2"), v("zz", 0), A_.max)
+        ts(v("cap"), v("cum"), c(24), A_.is_lt, -8192.0, A_.mult)
+        tt(v("eqx"), srt, v("cum"), A_.subtract)
+        scan(v("ys"), v("eqx"), v("cap"), A_.max, A_.min, -8192.0)
+        ts(v("n16"), v("k2"), v("ys", NA - 1), A_.max, c(24), A_.add)
         if t == R - 1:
             cp(v("ti", 64 * t, 64 * t + 32), by(v("aI"), v("n16")))
             outputs(t)
             break
-        nc = t + 2
-        n = K * nc
-        o = v("ok16", 0, 3)
-        cp(v("uS", 0, K), by(v("aS"), v("n16", 0)))
-        act(v("uI", 0, K), by(v("aI"), v("n16", 0)))
-        tt(v("dg", 0, NS), by(v("uS"), o), v("dm", 0, NS), A_.mult)
-        act(v("sS"), by(v("uS"), o))
-        scan(v("dgs", 0, NS), v("r16", 0, NS), v("dg", 0, NS), A_.mult, A_.add)
-        act(v("sI"), by(v("uI"), o))
-        for k in range(nc):
-            act(v("sg", n * k, n * k + n), v("sS", 0, n), FN.Sign, bias=v("dgs", 16 * k + 15), scale=-1.0)
+        sw = 96 * t
+        cp(by(held("uS", t), v("ok16", 0, 3)), held("uS", t - 1))
+        act(v("aS", 0, K), held("uS", t, 0, K))
+        tt(v("swd"), v("uS", sw, sw + 96), v("dm", 0, 96), A_.mult)
+        scan(v("sw", sw, sw + 96), v("r16", 0, 96), v("swd"), A_.mult, A_.add)
+        for k in range(3):
+            ts(v("thr", NS * k, NS * k + NS), held("uP", t), v("sw", sw + 63 + 16 * k), A_.is_lt, 0.5, A_.subtract)
+        cp(by(v("so2", 256 * t, 256 * t + 256), v("s16", 0, 3)), v("aS", K, 64))
+        ts(v("eq"), v("cum"), c(24), A_.is_equal)
+        tt(v("zs", 0, NA), v("eq"), v("so2", 256 * t, 256 * t + 2 * NA, 2), A_.mult)
+        ts(v("zs", NA), v("cum", NA - 1), c(24), A_.is_lt, v("sw", sw + 15), A_.mult)
+        total(v("zz", 0), v("zs", 0, NA + 1))
+        cp(held("uS", t, 0, K), by(v("aS"), v("n16", 0)))
+        act(held("uI", t, 0, K), by(v("aI"), v("n16", 0)))
+        for k in range(3):
+            act(v("sg", NS * k, NS * k + NS), held("uS", t), FN.Sign, bias=v("sw", sw + 15 + 16 * k) if k else v("zz", 0), scale=-1.0)
         act(v("ti", 64 * t, 64 * t + 32), by(v("aI"), v("n16")))
-        act(v("uM", 0, K), by(v("aM"), v("n16", 0)))
-        act(v("sM"), by(v("uM"), o))
-        if nc == 3:
-            tt(v("bef"), v("sg"), v("thr"), A_.is_lt)
-            scan(v("befs"), v("r48"), v("bef"), A_.mult, A_.add)
-        else:
-            for k in range(nc):
-                tt(v("bef", n * k, n * k + n), v("sg", n * k, n * k + n), v("thr", NS * k, NS * k + n), A_.is_lt)
-            scan(v("befs", 0, n * nc), v("r32", 0, n * nc), v("bef", 0, n * nc), A_.mult, A_.add)
-        cp(v("rk16", 0, nc), v("befs", n - 1, n * nc, n))
-        cp(by(v("srt", 16, 64), v("rk16", 0, nc)), v("sI", 0, n))
+        act(held("uM", t, 0, K), by(v("aM"), v("n16", 0)))
+        tt(v("bef"), v("sg"), v("thr"), A_.is_lt)
+        scan(v("befs"), v("r48"), v("bef"), A_.mult, A_.add)
+        cp(v("rk16", 0, 3), v("befs", NS - 1, 3 * NS, NS))
+        cp(by(v("srt", 16, 64), v("rk16", 0, 3)), held("uI", t))
         act(v("srt", 0, 16), v("srt", 16, 32))
         turn(v("tr"), v("srt", 0, 32))
         cp(v("tr", 8, 32, 16, p=(0, 64)), v("tr", 0, 32, 16, p=(64, 128)))
@@ -486,13 +505,13 @@ def rank_program(g, core, T, topo):
                 cp(o_, i_)
         cp(v("par16"), by(v("tr"), v("xo16", 0)))
         pick(par[t + 1][0], par[t + 1][1], 0, 128, "pc", "pl", kid + 256, v("par16", 0, 8))
-        act(v("rw", 0, nc), v("befs", n - 1, n * nc, n))
+        act(v("rw", 0, 3), v("befs", NS - 1, 3 * NS, NS))
         outputs(t)
 
-    tt(v("dg"), v("hb"), v("dm"), A_.mult)
-    scan(v("dgs"), v("r16"), v("dg"), A_.mult, A_.add)
-    cp(v("l16"), v("dgs", 15, P, 16))
-    pick("occ", "ocs", 0, P, "pc", "pl", POOL, v("l16"))
+    turn(v("ht", 0, P), v("hb", 16, 16 + P))
+    turn(v("ht", P, 352), v("hb"))
+    cp(v("l16"), by(v("ht"), v("ho16", 0)))
+    pick("occ", "ocs", 0, P, "pc", "pl", POOL, v("l16", 0, 10))
     dma("S", "oc", T.oc[:], w8(v("occ")))
     for k in range(4):
         dma("A" if k % 2 else "S", "os%d" % (k % 2), T.osc[4 * k:4 * k + 4, :], v("ocs", p=(32 * k, 32 * k + 4)))
@@ -565,8 +584,8 @@ def rank_program(g, core, T, topo):
         more = [0.0] * len(nodes)
         for again in range(TURNS):
             plan, tail = arrange(skip, more)
-            t_, off = span(plan, 60, 60)
-            t_ += span(plan, 0, 100)[0] + span(plan, 120, 120)[0]
+            t_, off = span(plan, 120, 120)
+            t_ += span(plan, 60, 60)[0] + span(plan, 200, 200)[0]
             if best is None or t_ < best[0]:
                 best = (t_, plan)
             for i in off:

@@ -11,30 +11,31 @@ MO, IT = 520, 264
 CODE, U8, F, B, H, I, U = "float8_e4m3fn_x4", "uint8", "float32", "bfloat16", "float16", "int32", "uint16"
 SCRATCH = {"ps": ("psum", [128, 4096], "float32")}
 for _d, _l in (
-    (CODE, dict(quc=128, qxc=P, u0c=128, uac=256, wcs=1024, pc=POOL, p1c=128, p2c=128, occ=P)),
-    (U8, dict(qus=128, qxs=P, u0s=128, uas=256, wss=1024, pl=POOL, p1s=128, p2s=128, ocs=P)),
+    (CODE, dict(quc=128, qxc=P, u0c=128, uac=256, wcs=1024, pc=POOL, p1c=128, p2c=128, occ=P, hc=P + K)),
+    (U8, dict(qus=128, qxs=P, u0s=128, uas=256, wss=1024, pl=POOL, p1s=128, p2s=128, ocs=P, hs=P + K)),
     (B, dict(ut=512, u0t=512, xt=640, kt0=1024, kt1=1024, kt2=1024, m0=322, r32=192, r48=3 * NS, mm=3 * ML, sm=150,
              e0=322, e0s=322, junk=640, oh=192, oht=192, ohs=192, bits=128, bt=128, thr=3 * NS, iq=96, iqt=96, cnt=96,
-             em=3 * ML, ems=3 * ML, es=150, ess=150, fl=NA, cum=NA, sg=3 * NS, bef=3 * NS, befs=3 * NS)),
+             em=3 * ML, ems=3 * ML, es=150, ess=150, cum=NA, sg=3 * NS, bef=3 * NS, befs=3 * NS)),
     (I, dict(pi=2, bi=8, ci=4, exi=16)),
     (U, dict(meta=64, ul=16, ex16=16, iq16=6, c16=10, me16=10, o16=4, p16=4, rk16=4, ok16=4, a16=8, s16=4, n16=2,
-             par16=16, own16=4 * R, l16=16)),
+             par16=16, own16=4 * R, l16=32)),
     (H, dict(ml=ML)),
-    (F, dict(mf=64, bf=8, cc=48, it=4 * IT, iw=96, r16=96, dm=96, dm2=96, hm=128, qc=96, bs=100, mei=10, t1k=NS, neg=NS,
-             xc=NA, sml=48, val=128, plw=16, plb=NS, fe=P, fm=P, sp=XQ, sS=NS, sI=NS, sM=NS, uS=R * 96, uI=R * NS,
-             uM=R * NS, sw=2 * 96, swd=96, so2=512, cap=NA, ys=NA, zs=64, aS=64, aI=64, aM=64, kb=NS, kt=1040, mx=256,
-             cmp=100, pos=100, dg=96, dgs=96, so=R * 256, eq=NA, eqx=NA, srt=64, tr=32, ti=R * 64, tt=R * 64,
-             yt=P + R * 256, yb=R * P, t16=R * 32, hb=P + 32, ht=352)),
+    (F, dict(mf=64, bf=8, cc=48, it=4 * IT, iw=96, r16=96, dm=96, dm2=96, hm=128, qc=96, bs=100, mei=10, t1k=NS,
+             neg=2 * NS, xc=NA, sml=48, val=128, plw=16, plb=NS, fe=P, fm=P, sp=XQ, sS=NS, sI=NS, sM=NS, uS=R * 96,
+             uI=R * NS, uM=R * NS, sw=2 * 96, swd=96, so2=512, wk=4 * NA, zs=64, aS=64, aI=64, aM=64, kb=NS, kt=1040,
+             mx=256, cmp=100, pos=100, dg=96, dgs=96, so=R * 512, srt=64, tr=64, ti=R * 64, tt=R * 64,
+             yt=P + R * 256, yb=R * P, t16=R * 32, hb=384, ht=704)),
 ):
     for _k, _n in _l.items():
         SCRATCH[_k] = ("sbuf", [128, _n], _d)
 PART = {"sab": ("sml", 0, 2), "dab": ("sml", 2, 2), "wab": ("sml", 4, 2), "y1": ("sml", 6, 6), "y2": ("sml", 12, 6),
         "y3": ("sml", 18, 4), "rw": ("sml", 22, 4), "kw": ("sml", 26, 4), "dk": ("sml", 30, 4), "da": ("sml", 34, 4),
         "zz": ("sml", 38, 2), "k2": ("sml", 40, 2), "xo16": ("c16", 0, 2), "pw16": ("c16", 2, 2), "cw16": ("c16", 4, 4),
-        "ho16": ("c16", 8, 2)}
+        "ho16": ("c16", 8, 2), "eq": ("wk", 0, NA), "eqx": ("wk", NA, NA), "cap": ("wk", 2 * NA, NA),
+        "ys": ("wk", 3 * NA, NA)}
 SEMAPHORES = ["V", "A", "E", "G", "lu", "lx", "lw", "ls", "m0", "a1", "a2", "m1", "m2", "b1", "b2", "sent",
-              "y0", "y1", "y2", "oc", "os0", "os1"]
-CYCLE, WAKE, LOCAL, FAR, FIRST = 0.95, 120.0, 2000.0, 2500.0, 1500.0
+              "y0", "y1", "y2", "oc", "os"]
+CYCLE, WAKE, LOCAL, FAR, FIRST = 0.9, 200.0, 2000.0, 2500.0, 1500.0
 SKIPS, TURNS, STEP = (0.2, 0.5, 0.9), 6, 500
 
 
@@ -149,9 +150,9 @@ def rank_program(g, core, T, topo):
     def dma(q, sem, o, i, more=0):
         add(q, lambda: Q[q].dma_start(ap(o), ap(i)), [o] if isinstance(o, list) else [], [i], LOCAL + more, sem, 16, 60)
 
-    def pick(oc, os_, a, n, wc_, ws_, wn, off):
-        cp(w32(v(oc, a, a + n)), by(w32(v(wc_, 0, wn)), off))
-        act(v(os_, a, a + n), by(v(ws_, 0, wn), off))
+    def pick(oc, os_, a, n, wc_, ws_, wn, off, w0=0):
+        cp(w32(v(oc, a, a + n)), by(w32(v(wc_, w0, wn)), off))
+        act(v(os_, a, a + n), by(v(ws_, w0, wn), off))
 
     def send(x, to, sem):
         ids = []
@@ -166,7 +167,7 @@ def rank_program(g, core, T, topo):
     def swap(sem, mine, to, theirs):
         last = [send(x, to, sem) for x in mine]
         n = sum(len(topo.engines(T.cores[r], core)) for r in to) * len(mine)
-        add("R", None, theirs, [], FAR + 2500 * (sem == "b2"), sem, n, 0, last)
+        add("R", None, theirs, [], FAR + 2000 * (sem == "b2"), sem, n, 0, last)
 
     def pieces(base, w, r, k):
         return [w8(v("pc", base + w * r, base + w * (r + k))), v("pl", base + w * r, base + w * (r + k))]
@@ -182,7 +183,7 @@ def rank_program(g, core, T, topo):
         return v("cc", j, j + n)
 
     dma("S", "lu", v("ut", 0, 56), T.u[:, 0:56])
-    dma("S", "lx", v("xt"), T.x[:], 500)
+    dma("A", "lx", v("xt"), T.x[:], 500)
     dma("S", "lw", w8(v("wcs")), T.wc[:], 3000)
     dma("S", "ls", v("wss"), T.ws[:], 3500)
     iota(v("pi"), [[0, 2]], 0, 1)
@@ -277,7 +278,8 @@ def rank_program(g, core, T, topo):
     for k in range(1, 4):
         act(v("it", IT * k, IT * k + IT), v("it", 0, IT), FN.Identity, bias=float(IT * k))
     act(v("yt", 0, P), v("ps", 2048, 2048 + P))
-    act(v("hb"), v("it", XQ - 16, KID + 16))
+    act(v("hb", 0, 192), v("it", XQ - 16, KID + 16))
+    act(v("hb", 192, 384), v("it", 0, 192), FN.Identity, bias=-16.0)
     ts(c(6, 3), v("it", 0, 3), 16.0, A_.mult, c(1), A_.add)
     ts(c(9, 3), c(6, 3), -1.0, A_.mult, float(NA - 1), A_.add)
     ts(c(18, 3), c(9, 3), -(CAPP - 1) / 2, A_.add, 1.0 / CAPP, A_.mult)
@@ -312,11 +314,13 @@ def rank_program(g, core, T, topo):
     ms(v("sm", 0, 150, 50), 0.0)
     ms(v("es", 0, 150, 50), 0.0)
     ms(v("es", 49, 150, 50), float(NA))
-    for t in range(R):
+    for t in range(2 * R):
         ms(v("so", 256 * t, 256 * t + 2 * NA), 0.0)
     ms(v("kt", 256, MO), 0.0)
     ms(v("kt", MO + 256, 1040), -1.0)
-    ms(v("neg"), -1.0)
+    ms(v("neg", 0, NS), -1.0)
+    ms(v("neg", NS, 2 * NS), 64.0)
+    ms(v("srt", 0, K), 0.0)
     ts(v("t1k"), v("it", 0, NS), float(K), A_.is_ge, 1000.0, A_.mult)
     ts(v("xc"), v("it", 0, NA), float(K), A_.add)
     ts(c(24), c(1), 1.0, A_.add, 64.0, A_.mult)
@@ -339,9 +343,10 @@ def rank_program(g, core, T, topo):
     tt(v("bf", 0, 2), v("bf", 3, 5), v("bf", 5, 7), A_.not_equal)
     ts(c(42), v("bf", 7), 16.0, A_.mult)
     ts(c(43), v("bf", 0), 8.0, A_.mult, c(42), A_.add)
-    ts(v("xo16", 0), v("bf", 1), 4.0, A_.mult, c(43), A_.add)
     ts(v("ci", 3), v("pi", 0), 4, A_.logical_shift_right, 1, A_.bitwise_and)
     cp(v("bf", 2), v("ci", 3))
+    ts(c(33), v("bf", 2), 32.0, A_.mult, c(43), A_.add)
+    ts(v("xo16", 0), v("bf", 1), 4.0, A_.mult, c(33), A_.add)
     ts(c(18), v("bf", 7), v("bf", 2), A_.not_equal, float(P), A_.mult)
     ts(c(19), v("bf", 2), -32.0, A_.mult, 16.0, A_.add)
     ts(c(20), v("bf", 7), c(19), A_.mult, c(18), A_.add)
@@ -355,7 +360,7 @@ def rank_program(g, core, T, topo):
     turn(v("fm"), v("fe"))
     act(v("plb"), by(v("it", 0, P), v("p16", 0, 3)))
     act(v("sM"), by(v("fm"), v("p16", 0, 3)))
-    cp(by(v("fm"), v("p16", 0, 3)), v("neg"))
+    cp(by(v("fm"), v("p16", 0, 3)), v("neg", 0, NS))
     act(v("ml", ML - P, ML), v("fm"))
 
     def held(name, t, a=0, b=NS):
@@ -388,23 +393,36 @@ def rank_program(g, core, T, topo):
 
     def outputs(t):
         h = 64 * t + oh_
-        turn(v("tt", 64 * t, 64 * t + 64), v("ti", 64 * t, 64 * t + 64))
         n, at, new = P + 256 * (t + 1), v("own16", 4 * t), v("own16", 4 * t + 2)
         if t < R - 1:
+            turn(v("tt", 64 * t, 64 * t + 64), v("ti", 64 * t, 64 * t + 64))
             ts(v("tt", 33 + h, p=oq), v("tt", h, p=oq), float(XQ), A_.subtract, v("tt", 32 + h, p=oq), A_.max)
             spread("tt", 32 + h, 34 + h, rank // 2)
             cp(v("own16", 4 * t, 4 * t + 4, 2), v("tt", 32 + h, 34 + h))
         else:
-            at, new = new, at
+            turn(v("tt", 64 * t + 32, 64 * t + 64), v("ti", 64 * t + 32, 64 * t + 64))
+            spread("tt", 32 + h, 33 + h, rank // 2)
+            cp(at, v("tt", 32 + h))
+            turn(v("tt", 64 * t, 64 * t + 32), v("ti", 64 * t, 64 * t + 32))
             for a in range(4):
-                cp(v("own16", 4 * t, 4 * t + 4, 2, p=(32 * a, 32 * a + 32)), v("tt", h, h + 33, 32, p=oq))
+                cp(v("own16", 4 * t + 2, p=(32 * a, 32 * a + 32)), v("tt", h, p=oq))
         cols, ys = v("t16", 32 * t + 16, 32 * t + 32), v("t16", 32 * t, 32 * t + 16)
-        if t == R - 1:
-            ts(cols, by(v("it", 0, n), new), float(XQ), A_.add)
-        else:
-            act(cols, by(v("it", 0, n), new), FN.Identity, bias=float(XQ))
         act(ys, by(v("yt", 0, n), new))
-        cp(by(v("hb", 16, 16 + P), at), cols)
+        if t < R - 1:
+            act(cols, by(v("it", 0, n), new), FN.Identity, bias=float(XQ))
+            cp(by(v("hb", 16, 16 + P), at), cols)
+        else:
+            cp(by(v("hb", 208, 208 + P), at), v("it", P, P + K))
+            for k in range(2):
+                turn(v("ht", 352 * k, 352 * k + P), v("hb", 192 * k + 16, 192 * k + 16 + P))
+                turn(v("ht", 352 * k + P, 352 * k + 352), v("hb", 192 * k, 192 * k + 192))
+                cp(v("l16", 16 * k, 16 * k + 16), by(v("ht", 352 * k, 352 * k + 352), v("ho16", 0)))
+            pick("hc", "hs", 0, P, "pc", "pl", POOL - 256, v("l16", 0, 10))
+            pick("hc", "hs", P, K, "pc", "pl", POOL, new, XQ)
+            pick("occ", "ocs", 0, P, "hc", "hs", P + K, v("l16", 16, 26))
+            dma("S", "oc", T.oc[:], w8(v("occ")))
+            for k in range(4):
+                dma("A", "os", T.osc[4 * k:4 * k + 4, :], v("ocs", p=(32 * k, 32 * k + 4)))
         cp(by(v("yb", P * t, P * t + P), at), ys)
         dma("S", "y%d" % t, T.y[:, P * t:P * t + P], v("yb", P * t, P * t + P))
 
@@ -459,10 +477,10 @@ def rank_program(g, core, T, topo):
         scan(v("ess"), v("es"), v("sm"), A_.add, A_.mult)
         for k in range(3):
             ts(v("s16", k), v("da", k), v("ess", 50 * k + 49), A_.add, v("ems", ML * k + ML - 1), A_.add)
-        cp(by(v("so", 256 * t, 256 * t + 256), v("s16", 0, 3)), v("xc"))
-        srt = v("so", 256 * t, 256 * t + 2 * NA, 2)
-        ts(v("fl"), srt, 1.0, A_.min, 64.0, A_.mult)
-        scan(v("cum"), v("fl"), v("fl"), A_.add, A_.max)
+        cp(by(v("so", 512 * t + 256, 512 * t + 512), v("s16", 0, 3)), v("neg", NS, 2 * NS))
+        cp(by(v("so", 512 * t, 512 * t + 256), v("s16", 0, 3)), v("xc"))
+        srt, fl = v("so", 512 * t, 512 * t + 2 * NA, 2), v("so", 512 * t + 256, 512 * t + 256 + 2 * NA, 2)
+        scan(v("cum"), fl, fl, A_.add, A_.max)
         ts(v("cap"), v("cum"), c(24), A_.is_lt, -8192.0, A_.mult)
         tt(v("eqx"), srt, v("cum"), A_.subtract)
         scan(v("ys"), v("eqx"), v("cap"), A_.max, A_.min, -8192.0)
@@ -493,12 +511,12 @@ def rank_program(g, core, T, topo):
         scan(v("befs"), v("r48"), v("bef"), A_.mult, A_.add)
         cp(v("rk16", 0, 3), v("befs", NS - 1, 3 * NS, NS))
         cp(by(v("srt", 16, 64), v("rk16", 0, 3)), held("uI", t))
-        act(v("srt", 0, 16), v("srt", 16, 32))
-        turn(v("tr"), v("srt", 0, 32))
-        cp(v("tr", 8, 32, 16, p=(0, 64)), v("tr", 0, 32, 16, p=(64, 128)))
-        act(v("tr", 8, 32, 16, p=(64, 128)), v("tr", 0, 32, 16, p=(0, 64)))
+        turn(v("tr", 0, 32), v("srt", 16, 48))
+        turn(v("tr", 32, 64), v("srt", 0, 32))
+        cp(v("tr", 8, 64, 16, p=(0, 64)), v("tr", 0, 64, 16, p=(64, 128)))
+        act(v("tr", 8, 64, 16, p=(64, 128)), v("tr", 0, 64, 16, p=(0, 64)))
         for a in range(4):
-            o_, i_ = v("tr", 4, 32, 8, p=(32 * a, 32 * a + 32)), v("tr", 0, 32, 8, p=(32 * (a ^ 1), 32 * (a ^ 1) + 32))
+            o_, i_ = v("tr", 4, 64, 8, p=(32 * a, 32 * a + 32)), v("tr", 0, 64, 8, p=(32 * (a ^ 1), 32 * (a ^ 1) + 32))
             if a % 2:
                 act(o_, i_)
             else:
@@ -507,14 +525,6 @@ def rank_program(g, core, T, topo):
         pick(par[t + 1][0], par[t + 1][1], 0, 128, "pc", "pl", kid + 256, v("par16", 0, 8))
         act(v("rw", 0, 3), v("befs", NS - 1, 3 * NS, NS))
         outputs(t)
-
-    turn(v("ht", 0, P), v("hb", 16, 16 + P))
-    turn(v("ht", P, 352), v("hb"))
-    cp(v("l16"), by(v("ht"), v("ho16", 0)))
-    pick("occ", "ocs", 0, P, "pc", "pl", POOL, v("l16", 0, 10))
-    dma("S", "oc", T.oc[:], w8(v("occ")))
-    for k in range(4):
-        dma("A" if k % 2 else "S", "os%d" % (k % 2), T.osc[4 * k:4 * k + 4, :], v("ocs", p=(32 * k, 32 * k + 4)))
 
     log, last = {}, {}
     for i, x in enumerate(nodes):
@@ -584,8 +594,8 @@ def rank_program(g, core, T, topo):
         more = [0.0] * len(nodes)
         for again in range(TURNS):
             plan, tail = arrange(skip, more)
-            t_, off = span(plan, 120, 120)
-            t_ += span(plan, 60, 60)[0] + span(plan, 200, 200)[0]
+            t_, off = span(plan, 210, 210)
+            t_ += span(plan, 150, 150)[0] + span(plan, 280, 280)[0]
             if best is None or t_ < best[0]:
                 best = (t_, plan)
             for i in off:

@@ -11,20 +11,20 @@ MO, IT = 520, 264
 CODE, U8, F, B, H, I, U = "float8_e4m3fn_x4", "uint8", "float32", "bfloat16", "float16", "int32", "uint16"
 SCRATCH = {"ps": ("psum", [128, 4096], "float32")}
 for _d, _l in (
-    (CODE, dict(quc=128, qxc=P, u0c=128, uac=256, wcs=1024, pc=POOL, p1c=128, p2c=128, occ=P, hc=P + K)),
-    (U8, dict(qus=128, qxs=P, u0s=128, uas=256, wss=1024, pl=POOL, p1s=128, p2s=128, ocs=P, hs=P + K)),
-    (B, dict(ut=512, u0t=512, xt=640, kt0=1024, kt1=1024, kt2=1024, m0=322, r32=192, r48=3 * NS, mm=3 * ML, sm=150,
-             e0=322, e0s=322, junk=640, oh=192, oht=192, ohs=192, bits=128, bt=128, thr=3 * NS, iq=96, iqt=96, cnt=96,
-             em=3 * ML, ems=3 * ML, es=150, ess=150, cum=NA, sg=3 * NS, bef=3 * NS, befs=3 * NS)),
+    (CODE, dict(quc=128, qxc=P, u0c=128, uac=256, wcs=1024, pc=POOL, p1c=128, p2c=128, occ=P, hc=P + K, ac=64)),
+    (U8, dict(qus=128, qxs=P, u0s=128, uas=256, wss=1024, pl=POOL, p1s=128, p2s=128, ocs=P, hs=P + K, asc=64)),
+    (B, dict(ut=512, u0t=512, xt=640, kt0=1024, kt1=1024, kt2=1024, m0=322, r32=192, mm=3 * ML, sm=150,
+             e0=322, e0s=322, junk=640, oh=192, oht=192, ohs=192, bits=128, bt=128, thr=150, iq=96, iqt=96, cnt=96,
+             em=3 * ML, ems=3 * ML, es=150, ess=150, cum=NA, bx=736, mm2=3 * (NA + P))),
     (I, dict(pi=2, bi=8, ci=4, exi=16)),
-    (U, dict(meta=64, ul=16, ex16=16, iq16=6, c16=10, me16=10, o16=4, p16=4, rk16=4, ok16=4, a16=8, s16=4, n16=2,
+    (U, dict(meta=64, ul=16, ex16=16, iq16=6, c16=24, me16=10, o16=4, p16=4, rk16=4, ok16=4, a16=8, s16=4, n16=2,
              par16=16, own16=4 * R, l16=32)),
     (H, dict(ml=ML)),
     (F, dict(mf=64, bf=8, cc=48, it=4 * IT, iw=96, r16=96, dm=96, dm2=96, hm=128, qc=96, bs=100, mei=10, t1k=NS,
              neg=2 * NS, xc=NA, sml=48, val=128, plw=16, plb=NS, fe=P, fm=P, sp=XQ, sS=NS, sI=NS, sM=NS, uS=R * 96,
              uI=R * NS, uM=R * NS, sw=2 * 96, swd=96, so2=512, wk=4 * NA, zs=64, aS=64, aI=64, aM=64, kb=NS, kt=1040,
              mx=256, cmp=100, pos=100, dg=96, dgs=96, so=R * 512, srt=64, tr=64, ti=R * 64, tt=R * 64,
-             yt=P + R * 256, yb=R * P, t16=R * 32, hb=384, ht=704)),
+             yt=P + R * 256, yb=R * P, t16=R * 32, hb=384, ht=704, fx=344)),
 ):
     for _k, _n in _l.items():
         SCRATCH[_k] = ("sbuf", [128, _n], _d)
@@ -32,11 +32,14 @@ PART = {"sab": ("sml", 0, 2), "dab": ("sml", 2, 2), "wab": ("sml", 4, 2), "y1": 
         "y3": ("sml", 18, 4), "rw": ("sml", 22, 4), "kw": ("sml", 26, 4), "dk": ("sml", 30, 4), "da": ("sml", 34, 4),
         "zz": ("sml", 38, 2), "k2": ("sml", 40, 2), "xo16": ("c16", 0, 2), "pw16": ("c16", 2, 2), "cw16": ("c16", 4, 4),
         "ho16": ("c16", 8, 2), "eq": ("wk", 0, NA), "eqx": ("wk", NA, NA), "cap": ("wk", 2 * NA, NA),
-        "ys": ("wk", 3 * NA, NA)}
+        "ys": ("wk", 3 * NA, NA), "ac16": ("c16", 10, 4), "mo16": ("c16", 14, 10), "mk": ("bx", 0, 150),
+        "eb": ("bx", 160, 150), "ebs": ("bx", 320, 150), "bits2": ("bx", 480, 128), "bt2": ("bx", 608, 128),
+        "val2": ("fx", 0, 128), "qo": ("fx", 128, 96), "ya": ("fx", 224, 64), "dr": ("fx", 288, 4),
+        "up5": ("fx", 296, NS)}
 SEMAPHORES = ["V", "A", "E", "G", "lu", "lx", "lw", "ls", "m0", "a1", "a2", "m1", "m2", "b1", "b2", "sent",
               "y0", "y1", "y2", "oc", "os"]
 CYCLE, WAKE, LOCAL, FAR, FIRST = 0.9, 200.0, 2000.0, 2500.0, 1500.0
-SKIPS, TURNS, STEP = (0.2, 0.5, 0.9), 6, 500
+SKIPS, TURNS, STEP = (0.1, 0.3, 0.5, 0.7, 1.0), 10, 500
 
 
 def rank_program(g, core, T, topo):
@@ -176,8 +179,9 @@ def rank_program(g, core, T, topo):
         return r - rank + low
 
     def spread(name, a, b, src):
-        for k, o in enumerate(o for o in range(4) if o != src):
-            (cp if k == 1 else act)(v(name, a, b, p=(32 * o, 32 * o + 32)), v(name, a, b, p=(32 * src, 32 * src + 32)))
+        for o in range(4):
+            if o != src:
+                act(v(name, a, b, p=(32 * o, 32 * o + 32)), v(name, a, b, p=(32 * src, 32 * src + 32)))
 
     def c(j, n=1):
         return v("cc", j, j + n)
@@ -236,19 +240,19 @@ def rank_program(g, core, T, topo):
     ts(v("oh", 0, 96), v("iw"), v("wab", 0), A_.is_equal, c(0), A_.mult)
     ts(v("oh", 96, 192), v("iw"), v("wab", 1), A_.is_equal, c(4), A_.mult)
     turn(v("oht"), v("oh"))
-    scan(v("ohs"), v("r32"), v("oht"), A_.mult, A_.add)
-    tt(v("y1", p=(0, 64)), v("ohs", 31, 192, 32, p=(0, 64)), v("ohs", 31, 192, 32, p=(64, 128)), A_.add)
-    tt(v("y2", p=(0, 32)), v("y1", p=(0, 32)), v("y1", p=(32, 64)), A_.add)
-    tt(v("y3", 0, 3, p=(0, 32)), v("y2", 0, 3, p=(0, 32)), v("y2", 3, 6, p=(0, 32)), A_.add)
+    for k in range(0, 96, 32):
+        scan(v("ohs", k, k + 32), v("oht", k, k + 32), v("oht", 96 + k, 128 + k), A_.add, A_.add)
+    tt(v("y1", 0, 3, p=(0, 64)), v("ohs", 31, 96, 32, p=(0, 64)), v("ohs", 31, 96, 32, p=(64, 128)), A_.add)
+    tt(v("y3", 0, 3, p=(0, 32)), v("y1", 0, 3, p=(0, 32)), v("y1", 0, 3, p=(32, 64)), A_.add)
     for a in range(4):
         cp(v("o16", 0, 3, p=(32 * a, 32 * a + 32)), v("y3", 0, 3, p=(0, 32)))
 
-    def signs(cn, sn, a, b, bank=0):
+    def signs(cn, sn, a, b, bank=0, x=""):
         mm(bank, "uac", "uas", 0, cn, sn, a, 128, True, False)
         mm(bank, "uac", "uas", 128, cn, sn, b, 128, False, True)
-        ts(v("bits"), v("ps", 512 * bank, 512 * bank + 128), 0.0, A_.is_gt)
-        turn(v("bt"), v("bits"))
-        scan(v("val"), v("hm"), v("bt"), A_.mult, A_.add)
+        ts(v("bits" + x), v("ps", 512 * bank, 512 * bank + 128), 0.0, A_.is_gt)
+        turn(v("bt" + x), v("bits" + x))
+        scan(v("val" + x), v("hm"), v("bt" + x), A_.mult, A_.add)
 
     quant(v("quc"), v("qus"), v("ut"))
     pick("uac", "uas", 0, 256, "quc", "qus", 128, v("ul"))
@@ -305,10 +309,17 @@ def rank_program(g, core, T, topo):
     cp(v("dm2", 48, 96), v("dm", 0, 48))
     ms(v("r16"), 1.0)
     ms(v("r16", 0, 96, 16), 0.0)
-    ms(v("r48"), 1.0)
-    ms(v("r48", 0, 3 * NS, NS), 0.0)
+    ms(v("qo"), rank * 0.25)
+    for k, o in enumerate((12, 44, 76, 108, 124)):
+        ms(v("mo16", 2 * k, 2 * k + 2), o)
+    ms(v("thr", 49, 150, 50), 1.0)
+    ms(v("mk", 0, 150, 50), 0.0)
+    ms(v("mk", 49, 150, 50), 1.0)
+    ms(v("eb", 0, 150, 50), 0.0)
+    ms(v("eb", 49, 150, 50), float(NS))
     for k in range(3):
         ts(v("mm", ML * k, ML * k + ML), v("it", 0, ML), c(6 + k), A_.is_gt)
+        ts(v("mm2", (NA + P) * k, (NA + P) * (k + 1)), v("it", 0, NA + P), c(6 + k), A_.is_gt)
         ts(v("sm", 50 * k, 50 * k + 50), v("it", 0, 50), c(21 + k), A_.not_equal, 2.0, A_.mult)
     ts(v("sm"), v("sm"), -1.0, A_.add)
     ms(v("sm", 0, 150, 50), 0.0)
@@ -377,59 +388,55 @@ def rank_program(g, core, T, topo):
             act(v("junk", 320 + NS * k, 320 + NS * k + NS), v("kb"), FN.Sign, bias=v("kw", k), scale=-1.0, acc=v("dk", k))
         ts(v("ok16", 0, 3), v("dk", 0, 3), float(NS - 1), A_.add, 0.5, A_.mult)
         o = v("ok16", 0, 3)
-        for name in ("uM", "uI", "uP"):
+        for name in ("uM", "uI", "uP") if t < R - 1 else ("uI", "uP"):
             cp(by(held(name, t), o), held(name, t - 1))
-        act(v("ml", NA, NA + NS - K), held("uM", t, K))
         act(v("ti", 64 * t + 32, 64 * t + 48), held("uP", t, 0, K))
         act(v("ti", 64 * t + 48, 64 * t + 64), held("uP", t, 0, K))
         if t < R - 1:
+            act(v("ml", NA, NA + NS - K), held("uM", t, K))
             act(v("aI", 0, K), held("uI", t, 0, K))
             act(v("aM", 0, K), held("uM", t, 0, K))
         else:
-            act(v("zs", 0, K), held("uI", t, 0, K), FN.Identity, bias=-float(XQ))
-            tt(v("aI", 0, K), v("zs", 0, K), held("uP", t, 0, K), A_.max)
+            act(v("ti", 64 * t, 64 * t + 16), held("uI", t, 0, K))
+            act(v("ti", 64 * t + 16, 64 * t + 32), held("uI", t, 0, K))
 
     oq, oh_ = (32 * (rank // 2), 32 * (rank // 2) + 32), 16 * (rank % 2)
 
     def outputs(t):
         h = 64 * t + oh_
         n, at, new = P + 256 * (t + 1), v("own16", 4 * t), v("own16", 4 * t + 2)
-        if t < R - 1:
-            turn(v("tt", 64 * t, 64 * t + 64), v("ti", 64 * t, 64 * t + 64))
-            ts(v("tt", 33 + h, p=oq), v("tt", h, p=oq), float(XQ), A_.subtract, v("tt", 32 + h, p=oq), A_.max)
-            spread("tt", 32 + h, 34 + h, rank // 2)
-            cp(v("own16", 4 * t, 4 * t + 4, 2), v("tt", 32 + h, 34 + h))
-        else:
-            turn(v("tt", 64 * t + 32, 64 * t + 64), v("ti", 64 * t + 32, 64 * t + 64))
-            spread("tt", 32 + h, 33 + h, rank // 2)
-            cp(at, v("tt", 32 + h))
-            turn(v("tt", 64 * t, 64 * t + 32), v("ti", 64 * t, 64 * t + 32))
-            for a in range(4):
-                cp(v("own16", 4 * t + 2, p=(32 * a, 32 * a + 32)), v("tt", h, p=oq))
+        turn(v("tt", 64 * t, 64 * t + 64), v("ti", 64 * t, 64 * t + 64))
+        ts(v("tt", 33 + h, p=oq), v("tt", h, p=oq), float(XQ), A_.subtract, v("tt", 32 + h, p=oq), A_.max)
+        spread("tt", 32 + h, 34 + h, rank // 2)
+        cp(v("own16", 4 * t, 4 * t + 4, 2), v("tt", 32 + h, 34 + h))
         cols, ys = v("t16", 32 * t + 16, 32 * t + 32), v("t16", 32 * t, 32 * t + 16)
-        act(ys, by(v("yt", 0, n), new))
         if t < R - 1:
+            act(ys, by(v("yt", 0, n), new))
             act(cols, by(v("it", 0, n), new), FN.Identity, bias=float(XQ))
             cp(by(v("hb", 16, 16 + P), at), cols)
-        else:
-            cp(by(v("hb", 208, 208 + P), at), v("it", P, P + K))
-            for k in range(2):
-                turn(v("ht", 352 * k, 352 * k + P), v("hb", 192 * k + 16, 192 * k + 16 + P))
-                turn(v("ht", 352 * k + P, 352 * k + 352), v("hb", 192 * k, 192 * k + 192))
-                cp(v("l16", 16 * k, 16 * k + 16), by(v("ht", 352 * k, 352 * k + 352), v("ho16", 0)))
-            pick("hc", "hs", 0, P, "pc", "pl", POOL - 256, v("l16", 0, 10))
-            pick("hc", "hs", P, K, "pc", "pl", POOL, new, XQ)
-            pick("occ", "ocs", 0, P, "hc", "hs", P + K, v("l16", 16, 26))
-            dma("S", "oc", T.oc[:], w8(v("occ")))
-            for k in range(4):
-                dma("A", "os", T.osc[4 * k:4 * k + 4, :], v("ocs", p=(32 * k, 32 * k + 4)))
-        cp(by(v("yb", P * t, P * t + P), at), ys)
+            store(t)
+            return
+        cp(by(v("hb", 208, 208 + P), at), v("it", P, P + K))
+        for k in range(2):
+            turn(v("ht", 352 * k, 352 * k + P), v("hb", 192 * k + 16, 192 * k + 16 + P))
+            turn(v("ht", 352 * k + P, 352 * k + 352), v("hb", 192 * k, 192 * k + 192))
+            cp(v("l16", 16 * k, 16 * k + 16), by(v("ht", 352 * k, 352 * k + 352), v("ho16", 0)))
+        pick("hc", "hs", 0, P, "pc", "pl", POOL - 256, v("l16", 0, 10))
+        pick("ac", "asc", 0, K, "pc", "pl", POOL - 256, new, XQ)
+        act(v("ya", 0, K), by(v("yt", 0, n - 256), new))
+
+    def store(t):
+        cp(by(v("yb", P * t, P * t + P), v("own16", 4 * t)), v("t16", 32 * t, 32 * t + 16))
         dma("S", "y%d" % t, T.y[:, P * t:P * t + P], v("yb", P * t, P * t + P))
 
     par = [("pc", "pl"), ("p1c", "p1s"), ("p2c", "p2s")]
     for t in range(R):
         kid, tile = KID + 256 * t, "kt%d" % t
+        end = t == R - 1
+        ml, mask = (NA + P, "mm2") if end else (ML, "mm")
         opens(t)
+        if end:
+            outputs(t)
         for i in range(8):
             mm(i, "wcs", "wss", 128 * i, par[t][0], par[t][1], 0, 128)
         for i in range(8):
@@ -438,13 +445,21 @@ def rank_program(g, core, T, topo):
                 ts(o, z, 0.0, A_.max, 0.05, A_.mult)
             else:
                 act(o, z, FN.Relu, scale=0.05)
-        quant(v("pc", kid, kid + 256), v("pl", kid, kid + 256), v(tile))
+        for h in range(2):
+            a = kid + 128 * h
+            quant(v("pc", a, a + 128), v("pl", a, a + 128), v(tile, 512 * h, 512 * h + 512))
         signs("pc", "pl", kid, kid + 128)
         mm(1, "u0c", "u0s", 0, "pc", "pl", kid, 256)
         mm(2, "wcs", "wss", 0, "pc", "pl", kid, 256)
         act(v("kt", 0, 256), v("ps", 512, 768))
         act(v("mx"), by(v("val"), v("ex16")))
-        tt(v("iq"), by(v("val"), v("iq16")), v("qc"), A_.is_equal)
+        if end:
+            signs("hc", "hs", 0, 32, 5, "2")
+            act(v("fe"), by(v("val2"), v("mo16")))
+            turn(v("fm"), v("fe"))
+            cp(by(v("fm"), v("own16", 4 * t)), v("neg", 0, K))
+            act(v("ml", NA, ml), v("fm"))
+        tt(v("iq"), by(v("val"), v("iq16")), v("qo" if end else "qc"), A_.is_equal)
         turn(v("iqt"), v("iq"))
         scan(v("cnt"), v("r32", 0, 96), v("iqt"), A_.mult, A_.add)
         for k in range(3):
@@ -453,30 +468,36 @@ def rank_program(g, core, T, topo):
         turn(v("kt", MO, MO + 256), v("mx"))
         scan(v("pos", 0, 99), v("bs", 0, 99), v("cmp", 0, 99), A_.min, A_.add, 1000.0)
         ts(v("a16", 0, 3), v("pos", 32, 99, 33), 256.0, A_.mult)
-        ts(v("a16", 3, 6), v("pos", 32, 99, 33), 256.0, A_.mult, float(MO), A_.add)
-        tt(v("dg", 0, 96), by(v("kt"), v("a16", 0, 6)), v("dm2"), A_.mult)
+        tt(v("dg", 48, 96), by(v("kt", MO, 1040), v("a16", 0, 3)), v("dm2", 48, 96), A_.mult)
+        tt(v("dg", 0, 48), by(v("kt", 0, MO), v("a16", 0, 3)), v("dm2", 0, 48), A_.mult)
         act(v("ml", 0, NA), by(v("kt", MO, 1040), v("a16", 0, 3)))
         act(v("aS", K, 64), by(v("kt", 0, MO), v("a16", 0, 3)))
-        scan(v("dgs", 0, 96), v("r16", 0, 96), v("dg", 0, 96), A_.mult, A_.add)
+        for k in (48, 0):
+            scan(v("dgs", k, k + 48), v("r16", 0, 48), v("dg", k, k + 48), A_.mult, A_.add)
         for k in range(3):
             act(v("junk", 480 + NA * k, 480 + NA * k + NA), v("aS", K, 64), FN.Sign, bias=v("dgs", 16 * k + 15), acc=v("da", k))
-        act(v("aI", K, 64), by(v("it", 0, MO), v("a16", 0, 3)), FN.Identity, bias=float(kid - XQ * (t == R - 1)))
-        if t < R - 1:
+        if not end:
+            act(v("aI", K, 64), by(v("it", 0, MO), v("a16", 0, 3)), FN.Identity, bias=float(kid))
             act(v("aM", K, 64), by(v("kt", MO, 1040), v("a16", 0, 3)))
         act(v("yt", P + 256 * t, P + 256 * t + 256), v("ps", 1024, 1280))
         act(v("yb", P * t, P * t + P), v("yt", 0, P) if t == 0 else v("yb", P * t - P, P * t))
+        if end:
+            ts(v("ac16", 0, 3), v("pos", 32, 99, 33), 256.0, A_.mult, 255.0, A_.min)
+            pick("ac", "asc", K, NA, "pc", "pl", POOL, v("ac16", 0, 3), kid)
+            act(v("ya", K, 64), by(v("yt", P + 256 * t, P + 256 * t + 256), v("ac16", 0, 3)))
         if t == 0:
             mm(3, "u0c", "u0s", 0, "pc", "pl", 0, XQ)
             act(v("sp"), v("ps", 1536, 1536 + XQ))
             act(v("sS"), by(v("sp"), v("cw16", 0, 3)))
         for k in range(3):
-            ts(v("em", ML * k, ML * k + ML), v("ml"), v("dgs", 63 + 16 * k), A_.is_equal, 128.0, A_.mult)
+            ts(v("em", ml * k, ml * k + ml), v("ml", 0, ml), v("dgs", 63 + 16 * k), A_.is_equal, 128.0, A_.mult)
         for k in range(3):
             ts(v("es", 50 * k + 1, 50 * k + 49), v("aS", K, 64), v("dgs", 16 * k + 15), A_.add, 0.0, A_.is_equal)
-        scan(v("ems"), v("em"), v("mm"), A_.max, A_.mult)
+        for k in range(0, 3 * ml, ml):
+            scan(v("ems", k, k + ml), v("em", k, k + ml), v(mask, k, k + ml), A_.max, A_.mult)
         scan(v("ess"), v("es"), v("sm"), A_.add, A_.mult)
         for k in range(3):
-            ts(v("s16", k), v("da", k), v("ess", 50 * k + 49), A_.add, v("ems", ML * k + ML - 1), A_.add)
+            ts(v("s16", k), v("da", k), v("ess", 50 * k + 49), A_.add, v("ems", ml * k + ml - 1), A_.add)
         cp(by(v("so", 512 * t + 256, 512 * t + 512), v("s16", 0, 3)), v("neg", NS, 2 * NS))
         cp(by(v("so", 512 * t, 512 * t + 256), v("s16", 0, 3)), v("xc"))
         srt, fl = v("so", 512 * t, 512 * t + 2 * NA, 2), v("so", 512 * t + 256, 512 * t + 256 + 2 * NA, 2)
@@ -485,17 +506,25 @@ def rank_program(g, core, T, topo):
         tt(v("eqx"), srt, v("cum"), A_.subtract)
         scan(v("ys"), v("eqx"), v("cap"), A_.max, A_.min, -8192.0)
         ts(v("n16"), v("k2"), v("ys", NA - 1), A_.max, c(24), A_.add)
-        if t == R - 1:
-            cp(v("ti", 64 * t, 64 * t + 32), by(v("aI"), v("n16")))
-            outputs(t)
+        if end:
+            pick("hc", "hs", P, K, "ac", "asc", 64, v("n16", 0))
+            pick("occ", "ocs", 0, P, "hc", "hs", P + K, v("l16", 16, 26))
+            dma("S", "oc", T.oc[:], w8(v("occ")))
+            for k in range(4):
+                dma("S" if k == 3 else "A", "os", T.osc[4 * k:4 * k + 4, :], v("ocs", p=(32 * k, 32 * k + 4)))
+            act(v("t16", 32 * t, 32 * t + 16), by(v("ya"), v("n16", 0)))
+            store(t)
             break
         sw = 96 * t
         cp(by(held("uS", t), v("ok16", 0, 3)), held("uS", t - 1))
         act(v("aS", 0, K), held("uS", t, 0, K))
-        tt(v("swd"), v("uS", sw, sw + 96), v("dm", 0, 96), A_.mult)
-        scan(v("sw", sw, sw + 96), v("r16", 0, 96), v("swd"), A_.mult, A_.add)
+        for k in (NS, 0):
+            tt(v("swd", k, k + NS), v("uS", sw + k, sw + k + NS), v("dm", 0, NS), A_.mult)
+            scan(v("sw", sw + k, sw + k + NS), v("r16", 0, NS), v("swd", k, k + NS), A_.mult, A_.add)
+        act(v("up5"), held("uP", t), FN.Identity, bias=0.5)
         for k in range(3):
-            ts(v("thr", NS * k, NS * k + NS), held("uP", t), v("sw", sw + 63 + 16 * k), A_.is_lt, 0.5, A_.subtract)
+            act(v("thr", 50 * k + 1, 50 * k + 49), v("up5"), FN.Sign, bias=v("sw", sw + 63 + 16 * k), scale=-1.0)
+            tt(v("mk", 50 * k + 1, 50 * k + 49), v("thr", 50 * k + 1, 50 * k + 49), v("thr", 50 * k + 2, 50 * k + 50), A_.mult)
         cp(by(v("so2", 256 * t, 256 * t + 256), v("s16", 0, 3)), v("aS", K, 64))
         ts(v("eq"), v("cum"), c(24), A_.is_equal)
         tt(v("zs", 0, NA), v("eq"), v("so2", 256 * t, 256 * t + 2 * NA, 2), A_.mult)
@@ -503,27 +532,28 @@ def rank_program(g, core, T, topo):
         total(v("zz", 0), v("zs", 0, NA + 1))
         cp(held("uS", t, 0, K), by(v("aS"), v("n16", 0)))
         act(held("uI", t, 0, K), by(v("aI"), v("n16", 0)))
-        for k in range(3):
-            act(v("sg", NS * k, NS * k + NS), held("uS", t), FN.Sign, bias=v("sw", sw + 15 + 16 * k) if k else v("zz", 0), scale=-1.0)
+        for k in (1, 2, 0):
+            mine = v("sw", sw + 15 + 16 * k) if k else v("zz", 0)
+            act(v("junk", NS * k, NS * k + NS), held("uS", t), FN.Sign, bias=mine, scale=-1.0, acc=v("dr", k))
+            ts(v("eb", 50 * k + 1, 50 * k + 49), held("uS", t), mine, A_.is_equal)
         act(v("ti", 64 * t, 64 * t + 32), by(v("aI"), v("n16")))
         act(held("uM", t, 0, K), by(v("aM"), v("n16", 0)))
-        tt(v("bef"), v("sg"), v("thr"), A_.is_lt)
-        scan(v("befs"), v("r48"), v("bef"), A_.mult, A_.add)
-        cp(v("rk16", 0, 3), v("befs", NS - 1, 3 * NS, NS))
+        for k in (50, 100, 0):
+            scan(v("ebs", k, k + 50), v("eb", k, k + 50), v("mk", k, k + 50), A_.add, A_.mult)
+        for k in range(3):
+            ts(v("rk16", k), v("ebs", 50 * k + 49), v("dr", k), A_.subtract, 0.5, A_.mult)
         cp(by(v("srt", 16, 64), v("rk16", 0, 3)), held("uI", t))
         turn(v("tr", 0, 32), v("srt", 16, 48))
         turn(v("tr", 32, 64), v("srt", 0, 32))
         cp(v("tr", 8, 64, 16, p=(0, 64)), v("tr", 0, 64, 16, p=(64, 128)))
         act(v("tr", 8, 64, 16, p=(64, 128)), v("tr", 0, 64, 16, p=(0, 64)))
         for a in range(4):
-            o_, i_ = v("tr", 4, 64, 8, p=(32 * a, 32 * a + 32)), v("tr", 0, 64, 8, p=(32 * (a ^ 1), 32 * (a ^ 1) + 32))
-            if a % 2:
-                act(o_, i_)
-            else:
-                cp(o_, i_)
+            for x in (1, 3):
+                o_, i_ = v("tr", 4 * x, 64, 16, p=(32 * a, 32 * a + 32)), v("tr", 0, 64, 16, p=(32 * (a ^ x), 32 * (a ^ x) + 32))
+                (cp if x == 1 else act)(o_, i_)
         cp(v("par16"), by(v("tr"), v("xo16", 0)))
         pick(par[t + 1][0], par[t + 1][1], 0, 128, "pc", "pl", kid + 256, v("par16", 0, 8))
-        act(v("rw", 0, 3), v("befs", NS - 1, 3 * NS, NS))
+        cp(v("rw", 0, 3), v("rk16", 0, 3))
         outputs(t)
 
     log, last = {}, {}

@@ -5,41 +5,45 @@ N, P, K, CAPP, R = 8, 160, 16, 6, 3
 NS = R * K
 NA = N * CAPP
 X2, XQ, KID = N * K, N * NS, N * NS + P
-POOL = KID + R * 256
+POOL = XQ + 2 * (KID + 512)
+OWN = P + 512
 ML = NA + (NS - K) + P
 MO, IT = 520, 264
 CODE, U8, F, B, H, I, U = "float8_e4m3fn_x4", "uint8", "float32", "bfloat16", "float16", "int32", "uint16"
 SCRATCH = {"ps": ("psum", [128, 4096], "float32")}
 for _d, _l in (
-    (CODE, dict(quc=128, qxc=P, u0c=128, uac=256, wcs=1024, pc=POOL, p1c=128, p2c=128, occ=P, hc=P + K, ac=64)),
-    (U8, dict(qus=128, qxs=P, u0s=128, uas=256, wss=1024, pl=POOL, p1s=128, p2s=128, ocs=P, hs=P + K, asc=64)),
-    (B, dict(ut=512, u0t=512, xt=640, kt0=1024, kt1=1024, kt2=1024, m0=322, r32=192, mm=3 * ML, sm=150,
-             e0=322, e0s=322, junk=640, oh=192, oht=192, ohs=192, bits=128, bt=128, thr=150, iq=96, iqt=96, cnt=96,
-             em=3 * ML, ems=3 * ML, es=150, ess=150, cum=NA, bx=736, mm2=3 * (NA + P))),
+    (CODE, dict(quc=128, qxc=P, u0c=128, uac=256, ubc=128, wcs=1024, pc=POOL, poc=OWN, k2c=256, occ=P, hc=P + K, ac=64)),
+    (U8, dict(qus=128, qxs=P, u0s=128, uas=256, ubs=128, wss=1024, pl=POOL, pol=OWN, k2s=256, ocs=P, hs=P + K, asc=64)),
+    (B, dict(ut=512, u0t=512, xt=640, kt0=1024, kt1=2048, kt2=2048, kt3=2048, bz=POOL - XQ, m0=322, r32=192, mm=3 * ML,
+             sm=150, e0=322, e0s=322, junk=640, oh=192, oht=192, ohs=192, bits=128, bt=128, thr=150, iq=96, iqt=96,
+             cnt=96, em=3 * ML, ems=3 * ML, es=150, ess=150, cum=NA, bx=800, cmp=100, bs=100)),
     (I, dict(pi=2, bi=8, ci=4, exi=16)),
-    (U, dict(meta=64, ul=16, ex16=16, iq16=6, c16=24, me16=10, o16=4, p16=4, rk16=4, ok16=4, a16=8, s16=4, n16=2,
-             par16=16, own16=4 * R, l16=32)),
-    (H, dict(ml=ML)),
-    (F, dict(mf=64, bf=8, cc=48, it=4 * IT, iw=96, r16=96, dm=96, dm2=96, hm=128, qc=96, bs=100, mei=10, t1k=NS,
-             neg=2 * NS, xc=NA, sml=48, val=128, plw=16, plb=NS, fe=P, fm=P, sp=XQ, sS=NS, sI=NS, sM=NS, uS=R * 96,
-             uI=R * NS, uM=R * NS, sw=2 * 96, swd=96, so2=512, wk=4 * NA, zs=64, aS=64, aI=64, aM=64, kb=NS, kt=1040,
-             mx=256, cmp=100, pos=100, dg=96, dgs=96, so=R * 512, srt=64, tr=64, ti=R * 64, tt=R * 64,
-             yt=P + R * 256, yb=R * P, t16=R * 32, hb=384, ht=704, fx=344)),
+    (U, dict(meta=64, ul=24, ex16=16, iq16=6, c16=30, me16=10, o16=4, p16=4, rk16=4, a16=8, s16=4, n16=2,
+             kl16=16, bl16=16, own16=4 * R, l16=32)),
+    (H, dict(ml=ML, pos=100)),
+    (F, dict(mf=64, bf=8, cc=56, it=4 * IT, iw=96, r16=96, dm=96, dm2=96, hm=P, qc=96, mei=10,
+             neg=2 * NS, xc=NA, sml=48, val=128, plw=16, fe=P, fm=P, sp=XQ, uS=R * 96,
+             uI=R * NS, uM=R * NS, sw=2 * 96, swd=96, so2=512, wk=160, aS=64, aI=64, aM=64, kt=1040,
+             mx=256, dg=96, dgs=96, so=R * 512, t0=64, tr=64, op=16, ti=R * 64, tt=R * 64,
+             yt=P + R * 256, yb=R * P, t16=R * 32, hb=384, ht=704, fx=560)),
 ):
     for _k, _n in _l.items():
         SCRATCH[_k] = ("sbuf", [128, _n], _d)
 PART = {"sab": ("sml", 0, 2), "dab": ("sml", 2, 2), "wab": ("sml", 4, 2), "y1": ("sml", 6, 6), "y2": ("sml", 12, 6),
-        "y3": ("sml", 18, 4), "rw": ("sml", 22, 4), "kw": ("sml", 26, 4), "dk": ("sml", 30, 4), "da": ("sml", 34, 4),
-        "zz": ("sml", 38, 2), "k2": ("sml", 40, 2), "xo16": ("c16", 0, 2), "pw16": ("c16", 2, 2), "cw16": ("c16", 4, 4),
-        "ho16": ("c16", 8, 2), "eq": ("wk", 0, NA), "eqx": ("wk", NA, NA), "cap": ("wk", 2 * NA, NA),
-        "ys": ("wk", 3 * NA, NA), "ac16": ("c16", 10, 4), "mo16": ("c16", 14, 10), "mk": ("bx", 0, 150),
-        "eb": ("bx", 160, 150), "ebs": ("bx", 320, 150), "bits2": ("bx", 480, 128), "bt2": ("bx", 608, 128),
-        "val2": ("fx", 0, 128), "qo": ("fx", 128, 96), "ya": ("fx", 224, 64), "dr": ("fx", 288, 4),
-        "up5": ("fx", 296, NS)}
+        "y3": ("sml", 18, 4), "da": ("sml", 34, 4), "od": ("sml", 38, 3), "lim": ("sml", 41, 3),
+        "xo16": ("c16", 0, 2), "pw16": ("c16", 2, 2), "cw16": ("c16", 4, 4), "ho16": ("c16", 8, 2),
+        "ac16": ("c16", 10, 4), "mo16": ("c16", 14, 10), "xb16": ("c16", 24, 2), "pg16": ("c16", 26, 4),
+        "eqx": ("wk", 0, NA + 1), "cap": ("wk", 52, NA + 1), "ys": ("wk", 104, NA + 1), "mk": ("bx", 0, 150),
+        "eb": ("bx", 160, 150), "ebs": ("bx", 320, 150), "bits2": ("bx", 480, P), "bt2": ("bx", 640, P),
+        "val2": ("fx", 400, P), "qo": ("fx", 128, 96), "ya": ("fx", 224, 64), "dr": ("fx", 288, 4),
+        "up5": ("fx", 296, NS), "zz": ("fx", 344, NA + 1)}
 SEMAPHORES = ["V", "A", "E", "G", "lu", "lx", "lw", "ls", "m0", "a1", "a2", "m1", "m2", "b1", "b2", "sent",
-              "y0", "y1", "y2", "oc", "os"]
-CYCLE, WAKE, LOCAL, FAR, FIRST = 0.9, 200.0, 2000.0, 2500.0, 1500.0
-SKIPS, TURNS, STEP = (0.1, 0.3, 0.5, 0.7, 1.0), 10, 500
+              "kc", "ks", "y0", "y1", "y2", "oc", "os"]
+CUT = ((0, NS), (50, K), (69, K))
+TINY, BIG, STEEP = 1e-37, 1e29, 1e24
+CYCLE, WAKE, LOCAL, FAR, FIRST, LONG = 0.9, 200.0, 1500.0, 2000.0, 1500.0, 120.0
+PACES = ((1.0, 210, 1.0), (1.15, 150, 1.2), (0.92, 260, 0.7), (1.3, 200, 1.0))
+SKIPS, TURNS, STEP, TRIES = (0.1, 0.3, 0.5, 0.7, 1.0), 6, 500, 300
 
 
 def rank_program(g, core, T, topo):
@@ -53,7 +57,7 @@ def rank_program(g, core, T, topo):
     low = min(rank, mate)
     assert abs(rank - mate) == 1 and len(peers) == 3
     Q = {"V": g.vector, "A": g.scalar, "E": g.tensor, "G": g, "S": g.sync}
-    nodes = []
+    nodes, gate = [], []
 
     def v(name, a=None, b=None, s=1, p=(0, 128)):
         name, o, n = PART[name] if name in PART else (name, 0, SCRATCH[name][1][1])
@@ -62,7 +66,7 @@ def rank_program(g, core, T, topo):
         if name == "ps":
             m, pm = 1 << (a // 512), 15
         else:
-            m = sum(1 << c_ for c_ in range(a, b, s))
+            m = sum(1 << c_ for c_ in range(a, b, s)) if s != 1 else (1 << b) - (1 << a)
             pm = sum(1 << k for k in range(4) if p[0] < 32 * k + 32 and 32 * k < p[1])
         return [ap_, [(name, m, pm)], len(range(a, b, s)), SCRATCH[name][2] in (B, H, U), None]
 
@@ -84,7 +88,7 @@ def rank_program(g, core, T, topo):
             wr += x[1][:1]
             rd += x[4] or []
         nodes.append({"q": q, "call": call, "rd": rd, "wr": wr, "cost": cost, "sem": sem or q, "inc": inc,
-                      "hold": cost if hold is None else hold, "after": list(after)})
+                      "hold": cost if hold is None else hold, "after": list(after), "gate": gate[:1] if cost > LONG else []})
         return len(nodes) - 1
 
     def price(o, i, rate, *more):
@@ -123,9 +127,6 @@ def rank_program(g, core, T, topo):
     def turn(o, i):
         add("V", lambda: g.vector.transpose(o[0], i[0]), [o], [i], price(o, i, None))
 
-    def total(o, i):
-        add("V", lambda: g.vector.tensor_reduce(o[0], i[0], AxisListType.X, A_.add), [o], [i], price(o, i, 1))
-
     def quant(c_, s, i):
         add("V", lambda: g.vector.quantize_mx(c_[0], s[0], i[0]), [c_, s], [i], 12 + 0.22 * i[2])
 
@@ -140,6 +141,9 @@ def rank_program(g, core, T, topo):
         f = FN.Copy if fn is None else fn
         add("A", lambda: g.scalar.activation(o[0], i[0], f, **kw), [o] + ([acc] if acc else []), [i, bias], price(o, i, 1) + (20 if acc else 0))
 
+    def fill(o, c_):
+        act(o, v("it", 0, o[2]), FN.Identity, bias=c_, scale=0.0)
+
     def mm(bank, lc, ls, a, rc, rs, b, n, start=True, stop=True):
         o, x = v("ps", 512 * bank, 512 * bank + n), [v(lc, a, a + 128), v(ls, a, a + 128), v(rc, b, b + n), v(rs, b, b + n)]
         add("E", lambda: g.tensor.matmul_mx(o[0], x[0][0], x[1][0], x[2][0], x[3][0], start, stop), [o], x, 0.63 * (n + 16))
@@ -153,9 +157,9 @@ def rank_program(g, core, T, topo):
     def dma(q, sem, o, i, more=0):
         add(q, lambda: Q[q].dma_start(ap(o), ap(i)), [o] if isinstance(o, list) else [], [i], LOCAL + more, sem, 16, 60)
 
-    def pick(oc, os_, a, n, wc_, ws_, wn, off, w0=0):
-        cp(w32(v(oc, a, a + n)), by(w32(v(wc_, w0, wn)), off))
-        act(v(os_, a, a + n), by(v(ws_, w0, wn), off))
+    def pick(oc, os_, a, n, wc_, ws_, wn, off):
+        cp(w32(v(oc, a, a + n)), by(w32(v(wc_, 0, wn)), off))
+        act(v(os_, a, a + n), by(v(ws_, 0, wn), off))
 
     def send(x, to, sem):
         ids = []
@@ -187,7 +191,7 @@ def rank_program(g, core, T, topo):
         return v("cc", j, j + n)
 
     dma("S", "lu", v("ut", 0, 56), T.u[:, 0:56])
-    dma("A", "lx", v("xt"), T.x[:], 500)
+    dma("A", "lx", v("xt"), T.x[:], 200)
     dma("S", "lw", w8(v("wcs")), T.wc[:], 3000)
     dma("S", "ls", v("wss"), T.ws[:], 3500)
     iota(v("pi"), [[0, 2]], 0, 1)
@@ -201,7 +205,6 @@ def rank_program(g, core, T, topo):
     ms(v("e0", 0, 322, 161), 0.0)
     ms(v("r32"), 1.0)
     ms(v("r32", 0, 192, 32), 0.0)
-    ms(v("ul"), 20)
     cp(c(0), v("pi", 0))
     ts(v("bi", 0), v("pi", 0), 15, A_.bitwise_and)
     ts(v("bi", 1), v("pi", 0), 4, A_.logical_shift_right)
@@ -214,10 +217,8 @@ def rank_program(g, core, T, topo):
     ts(v("m0", 161, 322), v("it", 0, 161), c(5), A_.not_equal, 2.0, A_.mult)
     ts(v("m0"), v("m0"), -1.0, A_.add)
     ms(v("m0", 0, 322, 161), 0.0)
-    ts(v("k2"), v("it", 0, 2), 0.0, A_.mult, c(1), A_.add)
-    ts(c(44, 4), v("it", 0, 4), 0.0, A_.mult, c(1), A_.add)
-    ts(v("ul", 0, 8, 2), c(44, 4), 1.0, A_.add)
-    ts(v("ul", 9, 16, 2), c(44, 4), 1.0, A_.add)
+    ts(c(44, 8), v("it", 0, 8), 0.0, A_.mult, c(1), A_.add)
+    ts(v("ul", 16, 24), c(44, 8), 1.0, A_.add)
 
     for k in range(4):
         if k % 2:
@@ -247,25 +248,27 @@ def rank_program(g, core, T, topo):
     for a in range(4):
         cp(v("o16", 0, 3, p=(32 * a, 32 * a + 32)), v("y3", 0, 3, p=(0, 32)))
 
-    def signs(cn, sn, a, b, bank=0, x=""):
-        mm(bank, "uac", "uas", 0, cn, sn, a, 128, True, False)
-        mm(bank, "uac", "uas", 128, cn, sn, b, 128, False, True)
-        ts(v("bits" + x), v("ps", 512 * bank, 512 * bank + 128), 0.0, A_.is_gt)
+    def digits(x="", n=128):
         turn(v("bt" + x), v("bits" + x))
-        scan(v("val" + x), v("hm"), v("bt" + x), A_.mult, A_.add)
+        scan(v("val" + x), v("hm", 0, n), v("bt" + x), A_.mult, A_.add)
+
+    def marks(cn, sn):
+        mm(5, "ubc", "ubs", 0, cn, sn, 0, P)
+        act(v("bits2"), v("ps", 2560, 2560 + P), FN.Sign, bias=-TINY)
+        digits("2", P)
 
     quant(v("quc"), v("qus"), v("ut"))
-    pick("uac", "uas", 0, 256, "quc", "qus", 128, v("ul"))
+    pick("ubc", "ubs", 0, 128, "quc", "qus", 128, v("ul", 16, 24))
     ms(v("hm"), 2.0)
-    ms(v("hm", 0, 128, 16), 0.0)
-    ms(v("hm", 3, 128, 16), 0.0)
-    ms(v("hm", 1, 128, 16), 0.5)
-    ms(v("hm", 2, 128, 16), 0.5)
-    signs("qxc", "qxs", 0, 32, 5)
+    ms(v("hm", 0, P, 16), 0.0)
+    ms(v("hm", 3, P, 16), 0.0)
+    ms(v("hm", 1, P, 16), 0.5)
+    ms(v("hm", 2, P, 16), 0.5)
+    marks("qxc", "qxs")
     mb = 8 * rank
-    cp(v("meta", mb, mb + 4), v("val", 12, 128, 32))
-    cp(v("meta", mb + 4), v("val", 124))
+    ts(v("meta", mb, mb + 5), v("val2", 12, P, 32), 1023.0, A_.add)
     swap("m0", [v("meta", mb, mb + 5)], [mate], [v("meta", 8 * mate, 8 * mate + 5)])
+    first = len(nodes)
     pick("pc", "pl", K * rank, K, "qxc", "qxs", P, v("o16", 2))
     swap("a1", pieces(0, K, rank, 1), [mate], pieces(0, K, mate, 1))
     cp(v("meta", mb + 5), v("o16", 2))
@@ -277,13 +280,19 @@ def rank_program(g, core, T, topo):
     swap("m2", [v("meta", 8 * low, 8 * low + 16)], peers, [v("meta", 8 * pair(r), 8 * pair(r) + 16) for r in peers])
     swap("b2", pieces(X2, 2 * K, low, 2), peers, sum([pieces(X2, 2 * K, pair(r), 2) for r in peers], []))
 
-    quant(v("pc", XQ, KID), v("pl", XQ, KID), v("xt"))
+    gate.append(first)
+    quant(v("poc", 0, P), v("pol", 0, P), v("xt"))
+    ms(v("ul", 0, 16), 20)
+    ts(v("ul", 0, 8, 2), c(44, 4), 1.0, A_.add)
+    ts(v("ul", 9, 16, 2), c(44, 4), 1.0, A_.add)
+    pick("uac", "uas", 0, 256, "quc", "qus", 128, v("ul", 0, 16))
     mm(4, "wcs", "wss", 0, "qxc", "qxs", 0, P)
     for k in range(1, 4):
         act(v("it", IT * k, IT * k + IT), v("it", 0, IT), FN.Identity, bias=float(IT * k))
     act(v("yt", 0, P), v("ps", 2048, 2048 + P))
-    act(v("hb", 0, 192), v("it", XQ - 16, KID + 16))
-    act(v("hb", 192, 384), v("it", 0, 192), FN.Identity, bias=-16.0)
+    for k in (0, 192):
+        act(v("hb", k, k + 192), v("it", 0, 192), FN.Identity, bias=-16.0)
+    fill(v("bz", 2 * XQ, 2 * KID), 0.0)
     ts(c(6, 3), v("it", 0, 3), 16.0, A_.mult, c(1), A_.add)
     ts(c(9, 3), c(6, 3), -1.0, A_.mult, float(NA - 1), A_.add)
     ts(c(18, 3), c(9, 3), -(CAPP - 1) / 2, A_.add, 1.0 / CAPP, A_.mult)
@@ -292,104 +301,97 @@ def rank_program(g, core, T, topo):
     ts(c(32, 3), c(12, 3), -float(CAPP), A_.mult)
     tt(c(15, 3), c(32, 3), c(9, 3), A_.add)
     ts(c(21, 3), c(6, 3), 1.0, A_.add)
-    ms(v("bs"), 1000.0)
-    ts(v("bs", 0, 99, 33), c(12, 3), 32.0 / 256, A_.mult)
+    ms(v("bs"), 1.0)
+    ms(v("bs", 0, 99, 33), 0.0)
+    ms(v("bs", 32, 99, 33), 1.0 / 256)
+    ts(v("cmp", 0, 99, 33), c(12, 3), 32.0, A_.mult)
     ts(c(35, 3), c(12, 3), 4.0, A_.is_ge, -112.0, A_.mult)
     ts(c(38, 3), c(12, 3), 32.0, A_.mult, 2.0, A_.add)
     tt(c(27, 3), c(35, 3), c(38, 3), A_.add)
     cp(v("iq16", 0, 6, 2), c(27, 3))
     cp(v("iq16", 1, 6, 2), c(27, 3))
     cp(v("ex16"), v("exi"))
-    ts(c(30), c(3), 2.0, A_.mult)
-    ts(v("qc"), v("qc"), c(30), A_.add, 0.25, A_.mult)
+    ts(c(30), c(3), 2.0, A_.mult, -3.5, A_.add)
+    ts(v("qc"), v("qc"), c(30), A_.add, 0.5, A_.mult)
     ts(c(31), c(3), 16.0, A_.mult)
     ts(v("me16"), v("mei"), c(31), A_.add)
     ts(v("dm"), v("dm"), c(1), A_.is_equal)
     ts(v("dm2", 0, 48), v("dm", 0, 48), -1.0, A_.mult)
-    cp(v("dm2", 48, 96), v("dm", 0, 48))
-    ms(v("r16"), 1.0)
+    act(v("dm2", 48, 96), v("dm", 0, 48))
+    fill(v("r16"), 1.0)
     ms(v("r16", 0, 96, 16), 0.0)
-    ms(v("qo"), rank * 0.25)
-    for k, o in enumerate((12, 44, 76, 108, 124)):
+    fill(v("qo"), rank * 0.5 - 1.75)
+    for k, o in enumerate(range(12, P, 32)):
         ms(v("mo16", 2 * k, 2 * k + 2), o)
-    ms(v("thr", 49, 150, 50), 1.0)
-    ms(v("mk", 0, 150, 50), 0.0)
-    ms(v("mk", 49, 150, 50), 1.0)
-    ms(v("eb", 0, 150, 50), 0.0)
-    ms(v("eb", 49, 150, 50), float(NS))
+    fill(v("thr", 0, 87), 1.0)
+    fill(v("mk", 0, 87), 1.0)
+    fill(v("eb", 0, 87), 0.0)
+    ms(v("thr", 69), 0.0)
+    ms(v("mk", 0, 51, 50), 0.0)
+    ms(v("eb", 49), float(NS))
+    ts(v("eb", 67, 87, 19), c(6, 2), 2.0, A_.mult, float(K), A_.add)
+    fill(v("mm"), 1.0)
     for k in range(3):
-        ts(v("mm", ML * k, ML * k + ML), v("it", 0, ML), c(6 + k), A_.is_gt)
-        ts(v("mm2", (NA + P) * k, (NA + P) * (k + 1)), v("it", 0, NA + P), c(6 + k), A_.is_gt)
+        ts(v("mm", ML * k, ML * k + NA), v("it", 0, NA), c(6 + k), A_.is_gt)
         ts(v("sm", 50 * k, 50 * k + 50), v("it", 0, 50), c(21 + k), A_.not_equal, 2.0, A_.mult)
     ts(v("sm"), v("sm"), -1.0, A_.add)
     ms(v("sm", 0, 150, 50), 0.0)
     ms(v("es", 0, 150, 50), 0.0)
     ms(v("es", 49, 150, 50), float(NA))
     for t in range(2 * R):
-        ms(v("so", 256 * t, 256 * t + 2 * NA), 0.0)
-    ms(v("kt", 256, MO), 0.0)
-    ms(v("kt", MO + 256, 1040), -1.0)
-    ms(v("neg", 0, NS), -1.0)
-    ms(v("neg", NS, 2 * NS), 64.0)
-    ms(v("srt", 0, K), 0.0)
-    ts(v("t1k"), v("it", 0, NS), float(K), A_.is_ge, 1000.0, A_.mult)
-    ts(v("xc"), v("it", 0, NA), float(K), A_.add)
-    ts(c(24), c(1), 1.0, A_.add, 64.0, A_.mult)
-    ts(v("k2"), v("k2"), c(24), A_.subtract)
+        fill(v("so", 256 * t, 256 * t + 2 * NA), 0.0)
+    fill(v("kt", 256, MO), 0.0)
+    fill(v("kt", MO + 256, 1040), 0.0)
+    fill(v("neg", 0, NS), 0.0)
+    fill(v("neg", NS, 2 * NS), 64.0)
+    act(v("xc"), v("it", 0, NA), FN.Identity, bias=float(K + 32))
+    ms(v("eqx", NA), -BIG)
+    ms(v("cap", NA), BIG)
     for t in range(R - 1):
-        ms(v("so2", 256 * t, 256 * t + 2 * NA), 0.0)
-    cp(v("rw", 0, 3), c(6, 3))
-    cp(v("rk16", 0, 3), c(6, 3))
+        fill(v("so2", 256 * t, 256 * t + 2 * NA), -BIG)
     ts(c(25), c(2), 16.0, A_.mult)
     ts(c(26), c(2), 32.0, A_.mult, float(X2 - K), A_.add)
-    ts(v("sI", 0, K), v("it", 0, K), c(25), A_.add)
-    ts(v("sI", K, NS), v("it", K, NS), c(26), A_.add)
+    act(v("uI", 0, K), v("it", 0, K), FN.Identity, bias=c(25))
+    act(v("uI", K, NS), v("it", K, NS), FN.Identity, bias=c(26))
     cp(v("cw16", 0), c(0))
     ts(v("cw16", 1, 3), c(7, 2), c(26), A_.add)
     ts(c(41), c(1), 2.0, A_.min, 5.0, A_.add)
     ts(v("pw16", 0), c(2), 8.0, A_.mult, c(41), A_.add)
-    for k, sh in enumerate((6, 5, 2, 1, 0)):
-        ts(v("bi", 3 + k), v("pi", 0), sh, A_.logical_shift_right, 1, A_.bitwise_and)
-    cp(v("bf", 3, 8), v("bi", 3, 8))
-    tt(v("bf", 0, 2), v("bf", 3, 5), v("bf", 5, 7), A_.not_equal)
-    ts(c(42), v("bf", 7), 16.0, A_.mult)
-    ts(c(43), v("bf", 0), 8.0, A_.mult, c(42), A_.add)
-    ts(v("ci", 3), v("pi", 0), 4, A_.logical_shift_right, 1, A_.bitwise_and)
-    cp(v("bf", 2), v("ci", 3))
-    ts(c(33), v("bf", 2), 32.0, A_.mult, c(43), A_.add)
-    ts(v("xo16", 0), v("bf", 1), 4.0, A_.mult, c(33), A_.add)
-    ts(c(18), v("bf", 7), v("bf", 2), A_.not_equal, float(P), A_.mult)
-    ts(c(19), v("bf", 2), -32.0, A_.mult, 16.0, A_.add)
+    for k, sh in enumerate((6, 4, 3, 2, 1, 0)):
+        ts(v("bi", 2 + k), v("pi", 0), sh, A_.logical_shift_right, 1, A_.bitwise_and)
+    cp(v("bf", 2, 8), v("bi", 2, 8))
+    ts(c(42), v("bf", 7), 32.0, A_.mult)
+    ts(c(43), v("bf", 6), 16.0, A_.mult, c(42), A_.add)
+    ts(c(52), v("bf", 5), 8.0, A_.mult, c(43), A_.add)
+    ts(v("bf", 0, 2), v("bf", 3, 5), v("bf", 2), A_.not_equal, 4.0, A_.mult)
+    ts(v("xb16", 0), v("bf", 0), c(52), A_.add)
+    ts(v("xo16", 0), v("bf", 1), c(52), A_.add)
+    ts(c(53), v("bf", 7), float(XQ), A_.add)
+    ts(v("pg16", 0, 2), c(44, 2), v("bf", 7), A_.subtract, 0.5, A_.mult)
+    ts(v("pg16", 2, 4), v("pg16", 0, 2), 8.0, A_.add)
+    ts(c(18), v("bf", 7), v("bf", 3), A_.not_equal, float(P), A_.mult)
+    ts(c(19), v("bf", 3), -32.0, A_.mult, 16.0, A_.add)
     ts(c(20), v("bf", 7), c(19), A_.mult, c(18), A_.add)
     ts(c(32), c(1), 16.0, A_.mult, 144.0, A_.min)
     ts(v("ho16", 0), c(32), c(20), A_.add)
 
-    cp(v("mf"), v("meta"))
-    cp(v("plw"), by(v("mf"), v("pw16", 0)))
-    act(v("fe"), by(v("mf"), v("me16")))
-    cp(v("p16", 0, 3), v("plw", 0, 3))
-    turn(v("fm"), v("fe"))
-    act(v("plb"), by(v("it", 0, P), v("p16", 0, 3)))
-    act(v("sM"), by(v("fm"), v("p16", 0, 3)))
-    cp(by(v("fm"), v("p16", 0, 3)), v("neg", 0, NS))
-    act(v("ml", ML - P, ML), v("fm"))
-
     def held(name, t, a=0, b=NS):
-        if t < 0:
-            return v({"uS": "sS", "uI": "sI", "uM": "sM", "uP": "plb"}[name], a, b)
         name, o = {"uS": ("uS", 96 * t), "uP": ("uS", 96 * t + NS)}.get(name, (name, NS * t))
         return v(name, o + a, o + b)
 
+    cp(v("mf"), v("meta"))
+    cp(v("plw"), by(v("mf"), v("pw16", 0)))
+    act(v("fe"), by(v("mf"), v("me16")), FN.Identity, bias=-1023.0)
+    cp(v("p16", 0, 3), v("plw", 0, 3))
+    turn(v("fm"), v("fe"))
+    act(held("uP", 0), by(v("it", 0, P), v("p16", 0, 3)))
+    act(held("uM", 0), by(v("fm"), v("p16", 0, 3)))
+    cp(by(v("fm"), v("p16", 0, 3)), v("neg", 0, NS))
+    act(v("ml", ML - P, ML), v("fm"))
+
     def opens(t):
-        ts(v("kw", 0, 3), v("rw", 0, 3), float(K), A_.is_ge, 1000.0, A_.mult)
-        tt(v("kb"), by(v("t1k"), v("rk16", 0, 3)), held("uP", t - 1), A_.add)
-        tt(v("kw", 0, 3), v("kw", 0, 3), v("sw", 96 * t - 33, 96 * t, 16) if t else v("plw", 0, 3), A_.add)
-        for k in range(3):
-            act(v("junk", 320 + NS * k, 320 + NS * k + NS), v("kb"), FN.Sign, bias=v("kw", k), scale=-1.0, acc=v("dk", k))
-        ts(v("ok16", 0, 3), v("dk", 0, 3), float(NS - 1), A_.add, 0.5, A_.mult)
-        o = v("ok16", 0, 3)
-        for name in ("uM", "uI", "uP") if t < R - 1 else ("uI", "uP"):
-            cp(by(held(name, t), o), held(name, t - 1))
+        for name in (("uM", "uP", "uS") if t < R - 1 else ("uP",)) if t else ():
+            cp(by(held(name, t), v("rk16", 0, 3)), held(name, t - 1))
         act(v("ti", 64 * t + 32, 64 * t + 48), held("uP", t, 0, K))
         act(v("ti", 64 * t + 48, 64 * t + 64), held("uP", t, 0, K))
         if t < R - 1:
@@ -402,6 +404,24 @@ def rank_program(g, core, T, topo):
 
     oq, oh_ = (32 * (rank // 2), 32 * (rank // 2) + 32), 16 * (rank % 2)
 
+    def rising(t, places, mine):
+        act(v("junk", 320, 320 + K), places, FN.Sign, bias=mine, scale=-1.0, acc=v("od", t))
+        ts(v("lim", t), v("od", t), 32.0, A_.mult, 512.0, A_.add)
+
+    def table(a, k):
+        mm(k, "ubc", "ubs", 0, "pc", "pl", a, 256)
+        act(v("bz", a - XQ, a - XQ + 256), v("ps", 512 * k, 512 * k + 256), FN.Sign, bias=-TINY)
+
+    def ahead(tile, cn, sn, a, to, banks):
+        for i in range(8):
+            k = banks[i % len(banks)]
+            mm(k, "wcs", "wss", 128 * i, cn, sn, a, 256)
+            act(v(tile, i, 2048, 8), v("ps", 512 * k, 512 * k + 256), FN.Relu, scale=0.05)
+        for h in range(0, 512, 128):
+            quant(v("pc", to + h, to + h + 128), v("pl", to + h, to + h + 128), v(tile, 4 * h, 4 * h + 512))
+        for h in range(2):
+            table(to + 256 * h, banks[h])
+
     def outputs(t):
         h = 64 * t + oh_
         n, at, new = P + 256 * (t + 1), v("own16", 4 * t), v("own16", 4 * t + 2)
@@ -412,49 +432,66 @@ def rank_program(g, core, T, topo):
         cols, ys = v("t16", 32 * t + 16, 32 * t + 32), v("t16", 32 * t, 32 * t + 16)
         if t < R - 1:
             act(ys, by(v("yt", 0, n), new))
-            act(cols, by(v("it", 0, n), new), FN.Identity, bias=float(XQ))
+            act(cols, by(v("it", 0, n), new))
             cp(by(v("hb", 16, 16 + P), at), cols)
             store(t)
             return
+        act(v("op"), by(v("it", 0, P), at))
+        rising(t, v("op"), v("tt", 32 + h))
         cp(by(v("hb", 208, 208 + P), at), v("it", P, P + K))
         for k in range(2):
             turn(v("ht", 352 * k, 352 * k + P), v("hb", 192 * k + 16, 192 * k + 16 + P))
             turn(v("ht", 352 * k + P, 352 * k + 352), v("hb", 192 * k, 192 * k + 192))
             cp(v("l16", 16 * k, 16 * k + 16), by(v("ht", 352 * k, 352 * k + 352), v("ho16", 0)))
-        pick("hc", "hs", 0, P, "pc", "pl", POOL - 256, v("l16", 0, 10))
-        pick("ac", "asc", 0, K, "pc", "pl", POOL - 256, new, XQ)
+        pick("hc", "hs", 0, P, "poc", "pol", OWN, v("l16", 0, 10))
+        pick("ac", "asc", 0, K, "poc", "pol", OWN, new)
         act(v("ya", 0, K), by(v("yt", 0, n - 256), new))
 
     def store(t):
         cp(by(v("yb", P * t, P * t + P), v("own16", 4 * t)), v("t16", 32 * t, 32 * t + 16))
         dma("S", "y%d" % t, T.y[:, P * t:P * t + P], v("yb", P * t, P * t + P))
 
-    par = [("pc", "pl"), ("p1c", "p1s"), ("p2c", "p2s")]
+    kids = [("pc", "pl", XQ), ("poc", "pol", P + 256), ("k2c", "k2s", 0)]
     for t in range(R):
-        kid, tile = KID + 256 * t, "kt%d" % t
+        kid, (kc, ks, k0) = KID + 256 * t, kids[t]
         end = t == R - 1
-        ml, mask = (NA + P, "mm2") if end else (ML, "mm")
+        ml = NA + P if end else ML
         opens(t)
         if end:
             outputs(t)
-        for i in range(8):
-            mm(i, "wcs", "wss", 128 * i, par[t][0], par[t][1], 0, 128)
-        for i in range(8):
-            o, z = v(tile, i, 1024, 8), v("ps", 512 * i, 512 * i + 128)
-            if i % 2:
-                ts(o, z, 0.0, A_.max, 0.05, A_.mult)
-            else:
-                act(o, z, FN.Relu, scale=0.05)
-        for h in range(2):
-            a = kid + 128 * h
-            quant(v("pc", a, a + 128), v("pl", a, a + 128), v(tile, 512 * h, 512 * h + 512))
-        signs("pc", "pl", kid, kid + 128)
-        mm(1, "u0c", "u0s", 0, "pc", "pl", kid, 256)
-        mm(2, "wcs", "wss", 0, "pc", "pl", kid, 256)
+        if t == 0:
+            for i in range(8):
+                mm(i, "wcs", "wss", 128 * i, "pc", "pl", 0, 128)
+            for i in range(8):
+                o, z = v("kt0", i, 1024, 8), v("ps", 512 * i, 512 * i + 128)
+                if i % 2:
+                    ts(o, z, 0.0, A_.max, 0.05, A_.mult)
+                else:
+                    act(o, z, FN.Relu, scale=0.05)
+            for a in (0, 128):
+                quant(v("pc", XQ + a, XQ + a + 128), v("pl", XQ + a, XQ + a + 128), v("kt0", 4 * a, 4 * a + 512))
+            mm(0, "uac", "uas", 0, "pc", "pl", XQ, 128, True, False)
+            mm(0, "uac", "uas", 128, "pc", "pl", XQ + 128, 128, False, True)
+            act(v("bits"), v("ps", 0, 128), FN.Sign, bias=-TINY)
+            digits()
+        else:
+            act(v("bits"), by(v("bz", 0, 2 * kid), v("bl16", 0, 8)))
+            digits()
+            pick(kc, ks, k0, 256, "pc", "pl", XQ + 2 * kid, v("kl16"))
+        mm(1, "u0c", "u0s", 0, kc, ks, k0, 256)
+        mm(2, "wcs", "wss", 0, kc, ks, k0, 256)
         act(v("kt", 0, 256), v("ps", 512, 768))
         act(v("mx"), by(v("val"), v("ex16")))
-        if end:
-            signs("hc", "hs", 0, 32, 5, "2")
+        if t == 0:
+            dma("S", "kc", w8(v("poc", P, P + 256)), w8(v("pc", XQ, XQ + 256)))
+            dma("S", "ks", v("pol", P, P + 256), v("pl", XQ, XQ + 256))
+            table(XQ, 4)
+            ahead("kt1", "pc", "pl", XQ, XQ + 2 * KID, (4, 5, 6, 7))
+            ahead("kt2", "pc", "pl", X2, XQ + 2 * X2, (4, 5, 6, 7))
+        elif not end:
+            ahead("kt3", kc, ks, k0, XQ + 2 * kid, (4, 5, 6, 7))
+        else:
+            marks("hc", "hs")
             act(v("fe"), by(v("val2"), v("mo16")))
             turn(v("fm"), v("fe"))
             cp(by(v("fm"), v("own16", 4 * t)), v("neg", 0, K))
@@ -463,10 +500,9 @@ def rank_program(g, core, T, topo):
         turn(v("iqt"), v("iq"))
         scan(v("cnt"), v("r32", 0, 96), v("iqt"), A_.mult, A_.add)
         for k in range(3):
-            ts(v("cmp", 33 * k, 33 * k + 32), v("cnt", 32 * k, 32 * k + 32), c(15 + k), A_.is_le, 1.0 / 256, A_.mult)
-        tt(v("cmp", 32, 99, 33), v("cnt", 31, 96, 32), c(15, 3), A_.is_le)
+            ts(v("cmp", 33 * k + 1, 33 * k + 33), v("cnt", 32 * k, 32 * k + 32), c(15 + k), A_.is_le)
         turn(v("kt", MO, MO + 256), v("mx"))
-        scan(v("pos", 0, 99), v("bs", 0, 99), v("cmp", 0, 99), A_.min, A_.add, 1000.0)
+        scan(v("pos", 0, 99), v("bs", 0, 99), v("cmp", 0, 99), A_.mult, A_.add)
         ts(v("a16", 0, 3), v("pos", 32, 99, 33), 256.0, A_.mult)
         tt(v("dg", 48, 96), by(v("kt", MO, 1040), v("a16", 0, 3)), v("dm2", 48, 96), A_.mult)
         tt(v("dg", 0, 48), by(v("kt", 0, MO), v("a16", 0, 3)), v("dm2", 0, 48), A_.mult)
@@ -483,18 +519,30 @@ def rank_program(g, core, T, topo):
         act(v("yb", P * t, P * t + P), v("yt", 0, P) if t == 0 else v("yb", P * t - P, P * t))
         if end:
             ts(v("ac16", 0, 3), v("pos", 32, 99, 33), 256.0, A_.mult, 255.0, A_.min)
-            pick("ac", "asc", K, NA, "pc", "pl", POOL, v("ac16", 0, 3), kid)
+            pick("ac", "asc", K, NA, kc, ks, 256, v("ac16", 0, 3))
             act(v("ya", K, 64), by(v("yt", P + 256 * t, P + 256 * t + 256), v("ac16", 0, 3)))
         if t == 0:
             mm(3, "u0c", "u0s", 0, "pc", "pl", 0, XQ)
             act(v("sp"), v("ps", 1536, 1536 + XQ))
-            act(v("sS"), by(v("sp"), v("cw16", 0, 3)))
+            act(held("uS", 0), by(v("sp"), v("cw16", 0, 3)))
+        sw = 96 * t
+        if not end:
+            act(v("aS", 0, K), held("uS", t, 0, K))
+            for k in (NS, 0):
+                tt(v("swd", k, k + NS), v("uS", sw + k, sw + k + NS), v("dm", 0, NS), A_.mult)
+                scan(v("sw", sw + k, sw + k + NS), v("r16", 0, NS), v("swd", k, k + NS), A_.mult, A_.add)
+            rising(t, held("uP", t, 0, K), v("sw", sw + 63))
+            act(v("up5"), held("uP", t), FN.Identity, bias=0.5)
+            for k, (a, n) in enumerate(CUT):
+                act(v("thr", a + 1, a + n + 1), v("up5", 0, n), FN.Sign, bias=v("sw", sw + 63 + 16 * k), scale=-1.0)
+            for a, b in ((1, 49), (51, 86)):
+                tt(v("mk", a, b), v("thr", a, b), v("thr", a + 1, b + 1), A_.mult)
         for k in range(3):
             ts(v("em", ml * k, ml * k + ml), v("ml", 0, ml), v("dgs", 63 + 16 * k), A_.is_equal, 128.0, A_.mult)
         for k in range(3):
             ts(v("es", 50 * k + 1, 50 * k + 49), v("aS", K, 64), v("dgs", 16 * k + 15), A_.add, 0.0, A_.is_equal)
-        for k in range(0, 3 * ml, ml):
-            scan(v("ems", k, k + ml), v("em", k, k + ml), v(mask, k, k + ml), A_.max, A_.mult)
+        for k in range(3):
+            scan(v("ems", ml * k, ml * k + ml), v("em", ml * k, ml * k + ml), v("mm", ML * k, ML * k + ml), A_.max, A_.mult)
         scan(v("ess"), v("es"), v("sm"), A_.add, A_.mult)
         for k in range(3):
             ts(v("s16", k), v("da", k), v("ess", 50 * k + 49), A_.add, v("ems", ml * k + ml - 1), A_.add)
@@ -502,10 +550,10 @@ def rank_program(g, core, T, topo):
         cp(by(v("so", 512 * t, 512 * t + 256), v("s16", 0, 3)), v("xc"))
         srt, fl = v("so", 512 * t, 512 * t + 2 * NA, 2), v("so", 512 * t + 256, 512 * t + 256 + 2 * NA, 2)
         scan(v("cum"), fl, fl, A_.add, A_.max)
-        ts(v("cap"), v("cum"), c(24), A_.is_lt, -8192.0, A_.mult)
-        tt(v("eqx"), srt, v("cum"), A_.subtract)
-        scan(v("ys"), v("eqx"), v("cap"), A_.max, A_.min, -8192.0)
-        ts(v("n16"), v("k2"), v("ys", NA - 1), A_.max, c(24), A_.add)
+        ts(v("cap", 0, NA), v("cum"), v("lim", t), A_.subtract, STEEP, A_.mult)
+        tt(v("eqx", 0, NA), srt, v("cum"), A_.subtract)
+        scan(v("ys"), v("eqx"), v("cap"), A_.max, A_.min, -BIG)
+        ts(v("n16"), v("ys", NA - 1, NA + 1), v("lim", t), A_.add, c(1), A_.max)
         if end:
             pick("hc", "hs", P, K, "ac", "asc", 64, v("n16", 0))
             pick("occ", "ocs", 0, P, "hc", "hs", P + K, v("l16", 16, 26))
@@ -515,50 +563,37 @@ def rank_program(g, core, T, topo):
             act(v("t16", 32 * t, 32 * t + 16), by(v("ya"), v("n16", 0)))
             store(t)
             break
-        sw = 96 * t
-        cp(by(held("uS", t), v("ok16", 0, 3)), held("uS", t - 1))
-        act(v("aS", 0, K), held("uS", t, 0, K))
-        for k in (NS, 0):
-            tt(v("swd", k, k + NS), v("uS", sw + k, sw + k + NS), v("dm", 0, NS), A_.mult)
-            scan(v("sw", sw + k, sw + k + NS), v("r16", 0, NS), v("swd", k, k + NS), A_.mult, A_.add)
-        act(v("up5"), held("uP", t), FN.Identity, bias=0.5)
-        for k in range(3):
-            act(v("thr", 50 * k + 1, 50 * k + 49), v("up5"), FN.Sign, bias=v("sw", sw + 63 + 16 * k), scale=-1.0)
-            tt(v("mk", 50 * k + 1, 50 * k + 49), v("thr", 50 * k + 1, 50 * k + 49), v("thr", 50 * k + 2, 50 * k + 50), A_.mult)
         cp(by(v("so2", 256 * t, 256 * t + 256), v("s16", 0, 3)), v("aS", K, 64))
-        ts(v("eq"), v("cum"), c(24), A_.is_equal)
-        tt(v("zs", 0, NA), v("eq"), v("so2", 256 * t, 256 * t + 2 * NA, 2), A_.mult)
-        ts(v("zs", NA), v("cum", NA - 1), c(24), A_.is_lt, v("sw", sw + 15), A_.mult)
-        total(v("zz", 0), v("zs", 0, NA + 1))
+        ts(v("so2", 256 * t + 2 * NA), v("cap", NA - 1), -1.0, A_.mult, v("sw", sw + 15), A_.min)
+        scan(v("zz"), v("so2", 256 * t, 256 * t + 2 * NA + 2, 2), v("cap"), A_.max, A_.min, -BIG)
         cp(held("uS", t, 0, K), by(v("aS"), v("n16", 0)))
         act(held("uI", t, 0, K), by(v("aI"), v("n16", 0)))
         for k in (1, 2, 0):
-            mine = v("sw", sw + 15 + 16 * k) if k else v("zz", 0)
-            act(v("junk", NS * k, NS * k + NS), held("uS", t), FN.Sign, bias=mine, scale=-1.0, acc=v("dr", k))
-            ts(v("eb", 50 * k + 1, 50 * k + 49), held("uS", t), mine, A_.is_equal)
+            mine, (a, n) = v("sw", sw + 15 + 16 * k) if k else v("zz", NA), CUT[k]
+            act(v("junk", NS * k, NS * k + n), held("uS", t, 0, n), FN.Sign, bias=mine, scale=-1.0, acc=v("dr", k))
+            ts(v("eb", a + 1, a + n + 1), held("uS", t, 0, n), mine, A_.is_equal)
         act(v("ti", 64 * t, 64 * t + 32), by(v("aI"), v("n16")))
         act(held("uM", t, 0, K), by(v("aM"), v("n16", 0)))
-        for k in (50, 100, 0):
-            scan(v("ebs", k, k + 50), v("eb", k, k + 50), v("mk", k, k + 50), A_.add, A_.mult)
-        for k in range(3):
-            ts(v("rk16", k), v("ebs", 50 * k + 49), v("dr", k), A_.subtract, 0.5, A_.mult)
-        cp(by(v("srt", 16, 64), v("rk16", 0, 3)), held("uI", t))
-        turn(v("tr", 0, 32), v("srt", 16, 48))
-        turn(v("tr", 32, 64), v("srt", 0, 32))
-        cp(v("tr", 8, 64, 16, p=(0, 64)), v("tr", 0, 64, 16, p=(64, 128)))
-        act(v("tr", 8, 64, 16, p=(64, 128)), v("tr", 0, 64, 16, p=(0, 64)))
+        for a, b in ((50, 87), (0, 50)):
+            scan(v("ebs", a, b), v("eb", a, b), v("mk", a, b), A_.add, A_.mult)
+        for k in (1, 2, 0):
+            ts(v("rk16", k), v("ebs", CUT[k][0] + CUT[k][1] + 1), v("dr", k), A_.subtract, 0.5, A_.mult)
+        cp(by(held("uI", t + 1), v("rk16", 0, 3)), held("uI", t))
+        cp(v("t0"), by(held("uI", t + 1), v("pg16")))
+        turn(v("tr"), v("t0"))
         for a in range(4):
-            for x in (1, 3):
-                o_, i_ = v("tr", 4 * x, 64, 16, p=(32 * a, 32 * a + 32)), v("tr", 0, 64, 16, p=(32 * (a ^ x), 32 * (a ^ x) + 32))
-                (cp if x == 1 else act)(o_, i_)
-        cp(v("par16"), by(v("tr"), v("xo16", 0)))
-        pick(par[t + 1][0], par[t + 1][1], 0, 128, "pc", "pl", kid + 256, v("par16", 0, 8))
-        cp(v("rw", 0, 3), v("rk16", 0, 3))
+            o = 8 * (1 - a % 2)
+            (act if a % 2 else cp)(v("tr", o, 64, 16, p=(32 * a, 32 * a + 32)), v("tr", o, 64, 16, p=(32 * (a ^ 1), 32 * (a ^ 1) + 32)))
+        cp(v("tr", 4, 64, 8, p=(0, 64)), v("tr", 0, 64, 8, p=(64, 128)))
+        act(v("tr", 4, 64, 8, p=(64, 128)), v("tr", 0, 64, 8, p=(0, 64)))
+        ts(v("bl16"), by(v("tr"), v("xb16", 0)), 2.0, A_.mult, v("bf", 7), A_.add)
+        ts(v("kl16"), by(v("tr"), v("xo16", 0)), 2.0, A_.mult, c(53), A_.add)
         outputs(t)
 
     log, last = {}, {}
     for i, x in enumerate(nodes):
-        need = {j: True for j in x["after"]}
+        need = {j: False for j in x["gate"]}
+        need.update({j: True for j in x["after"]})
         if x["q"] in "GS":
             if x["q"] in last:
                 need[last[x["q"]]] = False
@@ -603,33 +638,54 @@ def rank_program(g, core, T, topo):
                     ready[j] = max(start[k] + (nodes[k]["cost"] + WAKE if d else 0) for k, d in nodes[j]["need"].items())
         return plan_, tail
 
-    def span(plan_, own, other):
+    def span(plan_, pace, wake, dmas):
         free, end, why, late = {}, {}, {}, {}
         for i in plan_:
             x = nodes[i]
-            r = max([(0.0, -1)] + [(end[j] + (own if nodes[j]["q"] == x["q"] else other), j) for j, d in x["need"].items() if d])
+            r = max([(0.0, -1)] + [(end[j] + wake, j) for j in x["done"]])
             s0, why[i] = max(r, free.get(x["q"], (0.0, -1)))
             late[i] = s0 - r[0]
-            free[x["q"]], end[i] = (s0 + x["hold"], i), s0 + x["cost"]
+            f = pace if x["sem"] in "VAE" else dmas
+            free[x["q"]], end[i] = (s0 + x["hold"] * f, i), s0 + x["cost"] * f
         i = max(end, key=lambda k: end[k])
         t_, off = end[i], []
         while i >= 0:
-            if late[i] > 400:
-                off.append(i)
+            if late[i] > 0:
+                off.append((i, late[i]))
             i = why[i]
         return t_, off
 
+    def judge(plan_):
+        got = [span(plan_, *m) for m in PACES]
+        return sum(t_ for t_, off in got), [o for t_, off in got for o in off]
+
+    for x in nodes:
+        x["done"] = [j for j, d in x["need"].items() if d]
     best = None
     for skip in SKIPS:
         more = [0.0] * len(nodes)
         for again in range(TURNS):
             plan, tail = arrange(skip, more)
-            t_, off = span(plan, 210, 210)
-            t_ += span(plan, 150, 150)[0] + span(plan, 280, 280)[0]
+            t_, off = judge(plan)
             if best is None or t_ < best[0]:
-                best = (t_, plan)
-            for i in off:
-                more[i] = tail[i] + STEP
+                best = (t_, plan, off)
+            for i, late in off:
+                if late > 400:
+                    more[i] = tail[i] + STEP
+    seed = 1
+    for again in range(TRIES):
+        t_, plan, off = best
+        seed = (seed * 1103515245 + 12345) % 2147483648
+        i = off[(seed >> 8) % len(off)][0]
+        at = plan.index(i)
+        lo = max([plan.index(j) for j in nodes[i]["need"]] + [-1]) + 1
+        same = [k for k in range(lo, at) if nodes[plan[k]]["q"] == nodes[i]["q"]]
+        if same:
+            k = same[-1 - (seed >> 20) % min(3, len(same))]
+            new = plan[:k] + [i] + plan[k:at] + plan[at + 1:]
+            got = judge(new)
+            if got[0] < t_:
+                best = (got[0], new, got[1])
     count, seen, drain = {}, {q: {} for q in Q}, []
     for i in best[1]:
         x = nodes[i]

@@ -12,19 +12,19 @@ MO, IT = 520, 264
 CODE, U8, F, B, H, I, U = "float8_e4m3fn_x4", "uint8", "float32", "bfloat16", "float16", "int32", "uint16"
 SCRATCH = {"ps": ("psum", [128, 4096], "float32")}
 for _d, _l in (
-    (CODE, dict(quc=128, qxc=P, u0c=128, uac=256, ubc=128, wcs=1024, pc=POOL, poc=OWN, k2c=256, occ=P, hc=P + K, ac=64)),
-    (U8, dict(qus=128, qxs=P, u0s=128, uas=256, ubs=128, wss=1024, pl=POOL, pol=OWN, k2s=256, ocs=P, hs=P + K, asc=64)),
-    (B, dict(ut=512, u0t=512, xt=640, kt0=1024, kt1=2048, kt2=2048, kt3=2048, bz=POOL - XQ, m0=322, r32=192, mm=3 * ML,
-             sm=150, e0=322, e0s=322, junk=640, oh=192, oht=192, ohs=192, bits=128, bt=128, thr=150, iq=96, iqt=96,
-             cnt=96, em=3 * ML, ems=3 * ML, es=150, ess=150, cum=NA, bx=800, cmp=100, bs=100)),
-    (I, dict(pi=2, bi=8, ci=4, exi=16)),
-    (U, dict(meta=64, ul=24, ex16=16, iq16=6, c16=30, me16=10, o16=4, p16=4, rk16=4, a16=8, s16=4, n16=2,
+    (CODE, dict(quc=128, qxc=P, u0c=128, ubc=128, kxc=2 * P, wcs=1024, pc=POOL, poc=OWN, k2c=256, occ=P, hc=P + K, ac=64)),
+    (U8, dict(qus=128, qxs=P, u0s=128, ubs=128, kxs=2 * P, wss=1024, pl=POOL, pol=OWN, k2s=256, ocs=P, hs=P + K, asc=64)),
+    (B, dict(ut=512, u0t=512, xt=640, kt0=1024, kxt=8 * P, bo=2 * P, b0=64, kt1=2048, kt2=1024, kt3=2048, kt4=1024,
+             bz=POOL - XQ, m0=322, r32=32, mm=3 * ML, sm=150, e0=322, e0s=322, junk=640, oh=256, oht=256, bits=128,
+             bt=128, thr=150, iq=96, iqt=96, cnt=96, em=3 * ML, ems=3 * ML, es=150, ess=150, bx=800, bs=96)),
+    (I, dict(pi=2, bi=8, ci=4, exi=42)),
+    (U, dict(meta=92, ul=8, ex16=42, iq16=12, c16=44, me16=10, o16=8, p16=4, rk16=4, a16=8, s16=4, n16=2,
              kl16=16, bl16=16, own16=4 * R, l16=32)),
-    (H, dict(ml=ML, pos=100)),
-    (F, dict(mf=64, bf=8, cc=56, it=4 * IT, iw=96, r16=96, dm=96, dm2=96, hm=P, qc=96, mei=10,
-             neg=2 * NS, xc=NA, sml=48, val=128, plw=16, fe=P, fm=P, sp=XQ, uS=R * 96,
-             uI=R * NS, uM=R * NS, sw=2 * 96, swd=96, so2=512, wk=160, aS=64, aI=64, aM=64, kt=1040,
-             mx=256, dg=96, dgs=96, so=R * 512, t0=64, tr=64, op=16, ti=R * 64, tt=R * 64,
+    (H, dict(ml=ML, pos=96)),
+    (F, dict(mf=80, bf=8, cc=80, ohs=128, qc0=96, fm2=P, fm3=P, it=4 * IT, iw=128, r16=96, dm=96, dm2=96, hm=P, qc=96,
+             neg=NS, xc=NA, sml=48, val=128, plw=16, fe=P, fm=P, sp=XQ, uS=R * 96,
+             uI=R * NS, uM=R * NS, sw=2 * 96, swd=96, so2=512, wk=360, aS=64, aI=64, aM=64, kt=1040,
+             mx=256, dg=96, dgs=96, so=R * 256, t0=64, tr=64, ti=256, tt=256,
              yt=P + R * 256, yb=R * P, t16=R * 32, hb=384, ht=704, fx=560)),
 ):
     for _k, _n in _l.items():
@@ -32,18 +32,22 @@ for _d, _l in (
 PART = {"sab": ("sml", 0, 2), "dab": ("sml", 2, 2), "wab": ("sml", 4, 2), "y1": ("sml", 6, 6), "y2": ("sml", 12, 6),
         "y3": ("sml", 18, 4), "da": ("sml", 34, 4), "od": ("sml", 38, 3), "lim": ("sml", 41, 3),
         "xo16": ("c16", 0, 2), "pw16": ("c16", 2, 2), "cw16": ("c16", 4, 4), "ho16": ("c16", 8, 2),
-        "ac16": ("c16", 10, 4), "mo16": ("c16", 14, 10), "xb16": ("c16", 24, 2), "pg16": ("c16", 26, 4),
-        "eqx": ("wk", 0, NA + 1), "cap": ("wk", 52, NA + 1), "ys": ("wk", 104, NA + 1), "mk": ("bx", 0, 150),
+        "ac16": ("c16", 10, 4), "mo16": ("ex16", 32, 10), "xb16": ("c16", 24, 2), "pg16": ("c16", 26, 4),
+        "g16": ("c16", 30, 2), "ms": ("c16", 32, 5), "mk16": ("c16", 38, 2), "po16": ("c16", 40, 3),
+        "eqx": ("wk", 0, NA + 1), "cap": ("wk", 52, NA + 1), "ys": ("wk", 104, NA + 1), "yr": ("wk", 160, NA),
+        "ramp": ("wk", 208, 2 * NA), "cap2": ("wk", 304, NA + 1), "mk": ("bx", 0, 150),
         "eb": ("bx", 160, 150), "ebs": ("bx", 320, 150), "bits2": ("bx", 480, P), "bt2": ("bx", 640, P),
         "val2": ("fx", 400, P), "qo": ("fx", 128, 96), "ya": ("fx", 224, 64), "dr": ("fx", 288, 4),
-        "up5": ("fx", 296, NS), "zz": ("fx", 344, NA + 1)}
-SEMAPHORES = ["V", "A", "E", "G", "lu", "lx", "lw", "ls", "m0", "a1", "a2", "m1", "m2", "b1", "b2", "sent",
-              "kc", "ks", "y0", "y1", "y2", "oc", "os"]
+        "up5": ("fx", 296, NS), "zz": ("fx", 344, NA + 1), "op": ("fx", 0, K), "w0": ("fx", 16, 40), "mei": ("fx", 56, 10)}
+SEMAPHORES = ["V", "A", "E", "G", "lu", "lx", "lw0", "lw1", "lw2", "lw3", "ls", "m0", "a1", "a2", "m1", "m2", "b1", "b2",
+              "sent", "kc", "ks", "y0", "y1", "y2", "oc", "os"]
 CUT = ((0, NS), (50, K), (69, K))
 TINY, BIG, STEEP = 1e-37, 1e29, 1e24
-CYCLE, WAKE, LOCAL, FAR, FIRST, LONG = 0.9, 200.0, 1500.0, 2000.0, 1500.0, 120.0
+UNIT = 16384.0
+CYCLE, WAKE, LOCAL, WLOAD, FIRST, LONG = 0.9, 200.0, 1500.0, 1200.0, 2000.0, 120.0
+FAR = dict(m0=1500, a1=1500, m1=1600, b1=1800, a2=2500, m2=2900, b2=4500)
 PACES = ((1.0, 210, 1.0), (1.15, 150, 1.2), (0.92, 260, 0.7), (1.3, 200, 1.0))
-SKIPS, TURNS, STEP, TRIES = (0.1, 0.3, 0.5, 0.7, 1.0), 6, 500, 300
+TURNS, SHAKE, TRIES, ORDER = 40, 40.0, 3000, {}
 
 
 def rank_program(g, core, T, topo):
@@ -119,7 +123,8 @@ def rank_program(g, core, T, topo):
             add("V", lambda: g.vector.tensor_scalar(o[0], a[0], ap(s1), ap(s2), op0, op1), [o], [a, s1, s2], price(o, a, None))
 
     def scan(o, d0, d1, op0, op1, init=0.0):
-        add("V", lambda: g.vector.tensor_tensor_scan(o[0], d0[0], d1[0], init, op0, op1), [o], [d0, d1], price(o, d0, None, d1))
+        add("V", lambda: g.vector.tensor_tensor_scan(o[0], d0[0], d1[0], ap(init), op0, op1), [o], [d0, d1, init],
+            price(o, d0, None, d1))
 
     def ms(o, c_):
         add("V", lambda: g.vector.memset(o[0], c_), [o], [], price(o, o, None))
@@ -144,6 +149,15 @@ def rank_program(g, core, T, topo):
     def fill(o, c_):
         act(o, v("it", 0, o[2]), FN.Identity, bias=c_, scale=0.0)
 
+    def lin(o, i, a, b=0.0):
+        act(o, i, FN.Identity, bias=b, scale=a)
+
+    def relu(o, z, vector):
+        if vector:
+            ts(o, z, 0.0, A_.max, 0.05, A_.mult)
+        else:
+            act(o, z, FN.Relu, scale=0.05)
+
     def mm(bank, lc, ls, a, rc, rs, b, n, start=True, stop=True):
         o, x = v("ps", 512 * bank, 512 * bank + n), [v(lc, a, a + 128), v(ls, a, a + 128), v(rc, b, b + n), v(rs, b, b + n)]
         add("E", lambda: g.tensor.matmul_mx(o[0], x[0][0], x[1][0], x[2][0], x[3][0], start, stop), [o], x, 0.63 * (n + 16))
@@ -161,20 +175,20 @@ def rank_program(g, core, T, topo):
         cp(w32(v(oc, a, a + n)), by(w32(v(wc_, 0, wn)), off))
         act(v(os_, a, a + n), by(v(ws_, 0, wn), off))
 
-    def send(x, to, sem):
+    def send(x, to, sem, land):
         ids = []
         for r in to:
             rid, pid = topo.addr(T.cores[r], core)
             ids.append(DstId(rid=rid, pnc=pid))
         tr = RemoteDMATransfer(dst_ids=ids, dma_engine_mask=topo.mask(core, T.cores[to[0]]), remote_sem=T.sem[sem],
-                               src=x[0], dsts=[x[0]] * len(to))
-        return add("G", lambda: g.remote_dma_fused([tr], local_sem=T.sem.sent), [], [x], 400 * len(to) + FIRST * (sem == "m0"),
+                               src=x[0], dsts=[y[0] for y in land] if land else [x[0]] * len(to))
+        return add("G", lambda: g.remote_dma_fused([tr], local_sem=T.sem.sent), [], [x], 120 + 60 * len(to) + FIRST * (sem == "m0"),
                    "sent", len(topo.engines(core, T.cores[to[0]])))
 
-    def swap(sem, mine, to, theirs):
-        last = [send(x, to, sem) for x in mine]
+    def swap(sem, mine, to, theirs, land=None):
+        last = [send(x, to, sem, land) for x in mine]
         n = sum(len(topo.engines(T.cores[r], core)) for r in to) * len(mine)
-        add("R", None, theirs, [], FAR + 2000 * (sem == "b2"), sem, n, 0, last)
+        add("R", None, theirs, [], FAR[sem], sem, n, 0, last)
 
     def pieces(base, w, r, k):
         return [w8(v("pc", base + w * r, base + w * (r + k))), v("pl", base + w * r, base + w * (r + k))]
@@ -182,29 +196,31 @@ def rank_program(g, core, T, topo):
     def pair(r):
         return r - rank + low
 
-    def spread(name, a, b, src):
-        for o in range(4):
-            if o != src:
-                act(v(name, a, b, p=(32 * o, 32 * o + 32)), v(name, a, b, p=(32 * src, 32 * src + 32)))
-
     def c(j, n=1):
         return v("cc", j, j + n)
 
     dma("S", "lu", v("ut", 0, 56), T.u[:, 0:56])
     dma("A", "lx", v("xt"), T.x[:], 200)
-    dma("S", "lw", w8(v("wcs")), T.wc[:], 3000)
-    dma("S", "ls", v("wss"), T.ws[:], 3500)
+    dma("S", "ls", v("wss"), T.ws[:], WLOAD)
+    for k in range(4):
+        dma("S", "lw%d" % k, w8(v("wcs", 256 * k, 256 * k + 256)), T.wc[:, 1024 * k:1024 * k + 1024], WLOAD + 500 * (k + 1))
     iota(v("pi"), [[0, 2]], 0, 1)
     iota(v("it", 0, IT), [[1, IT]])
-    iota(v("iw"), [[-32, 3], [0, 2], [-2, 16]], P - 32)
+    iota(v("iw", 0, 32), [[0, 2], [-2, 16]], P)
+    for k in range(2):
+        iota(v("iw", 32 * k + 32, 32 * k + 64), [[0, 2], [-2, 8], [-32, 2]], P - 32 - 16 * k)
+    iota(v("iw", 96, 128), [[-2, 16], [0, 2]], P)
     iota(v("dm"), [[0, 6], [1, 16]])
-    iota(v("exi"), [[16, 2], [32, 4], [0, 2]], 12)
+    iota(v("exi", 0, 16), [[16, 2], [32, 4], [0, 2]], 12)
+    k = low or 1
+    iota(v("exi", 16, 16 + 2 * k), [[10, k], [0, 2]], -10 * low % 80 + 9)
+    iota(v("exi", 16 + 2 * k, 32), [[10, N - k], [0, 2]], 10 * (k - low) + 9)
+    iota(v("exi", 32, 42), [[32, 5], [0, 2]], 12)
     iota(v("qc"), [[0, 3], [1, 2], [0, 16]])
-    iota(v("mei"), [[1, 5], [8, 2]])
+    iota(v("mei"), [[1, 5], [10, 2]])
     ms(v("ut", 56, 512), 0.0)
     ms(v("e0", 0, 322, 161), 0.0)
     ms(v("r32"), 1.0)
-    ms(v("r32", 0, 192, 32), 0.0)
     cp(c(0), v("pi", 0))
     ts(v("bi", 0), v("pi", 0), 15, A_.bitwise_and)
     ts(v("bi", 1), v("pi", 0), 4, A_.logical_shift_right)
@@ -212,13 +228,15 @@ def rank_program(g, core, T, topo):
     cp(c(1, 3), v("bi", 0, 3))
     ts(c(5), c(0), 32.0, A_.add)
     ts(c(4), c(0), 96.0, A_.is_ge, c(5), A_.mult)
-    ts(v("iw", 64, 96), v("iw", 64, 96), 96.0, A_.add)
     ts(v("m0", 0, 161), v("it", 0, 161), c(0), A_.not_equal, 2.0, A_.mult)
     ts(v("m0", 161, 322), v("it", 0, 161), c(5), A_.not_equal, 2.0, A_.mult)
     ts(v("m0"), v("m0"), -1.0, A_.add)
     ms(v("m0", 0, 322, 161), 0.0)
     ts(c(44, 8), v("it", 0, 8), 0.0, A_.mult, c(1), A_.add)
-    ts(v("ul", 16, 24), c(44, 8), 1.0, A_.add)
+    ts(v("ul"), c(44, 8), 1.0, A_.add)
+    ts(v("bi", 3), v("pi", 0), 1, A_.bitwise_and)
+    ts(c(62), v("bi", 3), float(P), A_.mult)
+    ts(c(63), c(0), 32.0, A_.is_lt, c(62), A_.mult)
 
     for k in range(4):
         if k % 2:
@@ -238,139 +256,164 @@ def rank_program(g, core, T, topo):
         ts(v("e0", 161 * k + 1, 161 * k + 161), v("ps", 1024, 1024 + P), v("sab", k), A_.is_equal)
     scan(v("e0s"), v("e0"), v("m0"), A_.add, A_.mult)
     tt(v("wab"), v("e0s", 160, 322, 161), v("dab"), A_.add)
-    ts(v("oh", 0, 96), v("iw"), v("wab", 0), A_.is_equal, c(0), A_.mult)
-    ts(v("oh", 96, 192), v("iw"), v("wab", 1), A_.is_equal, c(4), A_.mult)
+    for k in range(2):
+        ts(v("oh", 128 * k, 128 * k + 128), v("iw"), v("wab", k), A_.is_equal, c(4 * k), A_.mult)
     turn(v("oht"), v("oh"))
-    for k in range(0, 96, 32):
-        scan(v("ohs", k, k + 32), v("oht", k, k + 32), v("oht", 96 + k, 128 + k), A_.add, A_.add)
-    tt(v("y1", 0, 3, p=(0, 64)), v("ohs", 31, 96, 32, p=(0, 64)), v("ohs", 31, 96, 32, p=(64, 128)), A_.add)
-    tt(v("y3", 0, 3, p=(0, 32)), v("y1", 0, 3, p=(0, 32)), v("y1", 0, 3, p=(32, 64)), A_.add)
+    for k in range(0, 128, 32):
+        scan(v("ohs", k, k + 32), v("oht", k, k + 32), v("oht", 128 + k, 160 + k), A_.add, A_.add, c(63) if k == 96 else 0.0)
+    tt(v("y1", 0, 4, p=(0, 64)), v("ohs", 31, 128, 32, p=(0, 64)), v("ohs", 31, 128, 32, p=(64, 128)), A_.add)
+    tt(v("y3", 0, 4, p=(0, 32)), v("y1", 0, 4, p=(0, 32)), v("y1", 0, 4, p=(32, 64)), A_.add)
     for a in range(4):
-        cp(v("o16", 0, 3, p=(32 * a, 32 * a + 32)), v("y3", 0, 3, p=(0, 32)))
+        cp(v("o16", 0, 8, 2, p=(32 * a, 32 * a + 32)), v("y3", 0, 4, p=(0, 32)))
 
     def digits(x="", n=128):
         turn(v("bt" + x), v("bits" + x))
         scan(v("val" + x), v("hm", 0, n), v("bt" + x), A_.mult, A_.add)
 
-    def marks(cn, sn):
-        mm(5, "ubc", "ubs", 0, cn, sn, 0, P)
-        act(v("bits2"), v("ps", 2560, 2560 + P), FN.Sign, bias=-TINY)
-        digits("2", P)
-
     quant(v("quc"), v("qus"), v("ut"))
-    pick("ubc", "ubs", 0, 128, "quc", "qus", 128, v("ul", 16, 24))
+    pick("ubc", "ubs", 0, 128, "quc", "qus", 128, v("ul"))
     ms(v("hm"), 2.0)
     ms(v("hm", 0, P, 16), 0.0)
     ms(v("hm", 3, P, 16), 0.0)
     ms(v("hm", 1, P, 16), 0.5)
     ms(v("hm", 2, P, 16), 0.5)
-    marks("qxc", "qxs")
-    mb = 8 * rank
-    ts(v("meta", mb, mb + 5), v("val2", 12, P, 32), 1023.0, A_.add)
-    swap("m0", [v("meta", mb, mb + 5)], [mate], [v("meta", 8 * mate, 8 * mate + 5)])
+    mm(5, "ubc", "ubs", 0, "qxc", "qxs", 0, P)
+    act(v("bits2"), v("ps", 2560, 2560 + P), FN.Sign, bias=-TINY)
+    digits("2", P)
+    mine, its = (6, 16) if rank == low else (16, 6)
+    ts(v("ms"), v("val2", 12, P, 32), 4.0, A_.mult, 4096.0, A_.add)
+    swap("m0", [v("ms")], [mate], [v("meta", its, its + 5)], [v("meta", mine, mine + 5)])
+    for i in range(8):
+        k, a = (4, 6, 7, 5, 0, 1, 2, 3)[i], i // 4 * P
+        mm(k, "wcs", "wss", 128 * i, "qxc", "qxs", 0, P)
+        relu(v("kxt", 4 * a + i % 4, 4 * a + 4 * P, 4), v("ps", 512 * k, 512 * k + P), False)
+    for k, a in ((4, 0), (6, P)):
+        quant(v("kxc", a, a + P), v("kxs", a, a + P), v("kxt", 4 * a, 4 * a + 4 * P))
+        mm(k, "ubc", "ubs", 0, "kxc", "kxs", a, P)
+        act(v("bo", a, a + P), v("ps", 512 * k, 512 * k + P), FN.Sign, bias=-TINY)
+    ts(c(64), c(1), -6.0 if rank == low else 0.0, A_.add, 0.0, A_.max)
+    ts(c(65), c(64), 9.0, A_.min, 32.0, A_.add)
+    ts(c(66), c(65), 40.0, A_.is_ge)
+    lin(c(67), c(2), 16.0, -398.0)
+    lin(c(68), c(3), -32.0, c(67))
+    lin(c(69), c(65), 9.0, c(68))
+    ts(v("g16", 0), c(69), c(66), A_.mult, c(65), A_.add)
+    act(v("w0", 32, 37), v("val2", 12, P, 32))
     first = len(nodes)
-    pick("pc", "pl", K * rank, K, "qxc", "qxs", P, v("o16", 2))
+    cp(v("b0", 0, 16), by(v("bo"), v("o16", 6)))
+    act(v("b0", 16, 32), by(v("bo"), v("o16", 6)))
+    turn(v("b0", 32, 64), v("b0", 0, 32))
+    scan(v("w0", 0, 32), v("hm", 0, 32), v("b0", 32, 64), A_.mult, A_.add)
+    cp(v("w0", 37, 40), v("o16", 0, 6, 2))
+    half = 16 * (rank - low)
+    ts(v("meta", half, half + 16), by(v("w0"), v("g16", 0)), 4.0, A_.mult, 4096.0, A_.add)
+    pick("pc", "pl", K * rank, K, "qxc", "qxs", P, v("o16", 0))
     swap("a1", pieces(0, K, rank, 1), [mate], pieces(0, K, mate, 1))
-    cp(v("meta", mb + 5), v("o16", 2))
-    cp(v("meta", mb + 6, mb + 8), v("o16", 0, 2))
-    pick("pc", "pl", X2 + 2 * K * rank, 2 * K, "qxc", "qxs", P, v("o16", 0, 2))
-    swap("m1", [v("meta", mb + 5, mb + 8)], [mate], [v("meta", 8 * mate + 5, 8 * mate + 8)])
+    for k in range(2):
+        pick("pc", "pl", X2 + 2 * K * rank + K * k, K, "qxc", "qxs", P, v("o16", 2 + 2 * k))
     swap("b1", pieces(X2, 2 * K, rank, 1), [mate], pieces(X2, 2 * K, mate, 1))
+    swap("m1", [v("meta", mine + 5, mine + 10)], [mate], [v("meta", its + 5, its + 10)])
     swap("a2", pieces(0, K, low, 2), peers, sum([pieces(0, K, pair(r), 2) for r in peers], []))
-    swap("m2", [v("meta", 8 * low, 8 * low + 16)], peers, [v("meta", 8 * pair(r), 8 * pair(r) + 16) for r in peers])
+    swap("m2", [v("meta", 6, 26)], peers, [v("meta", 32, 92)],
+         [v("meta", 12 + 10 * ((rank - r) % N), 32 + 10 * ((rank - r) % N)) for r in peers])
     swap("b2", pieces(X2, 2 * K, low, 2), peers, sum([pieces(X2, 2 * K, pair(r), 2) for r in peers], []))
 
     gate.append(first)
     quant(v("poc", 0, P), v("pol", 0, P), v("xt"))
-    ms(v("ul", 0, 16), 20)
-    ts(v("ul", 0, 8, 2), c(44, 4), 1.0, A_.add)
-    ts(v("ul", 9, 16, 2), c(44, 4), 1.0, A_.add)
-    pick("uac", "uas", 0, 256, "quc", "qus", 128, v("ul", 0, 16))
     mm(4, "wcs", "wss", 0, "qxc", "qxs", 0, P)
     for k in range(1, 4):
-        act(v("it", IT * k, IT * k + IT), v("it", 0, IT), FN.Identity, bias=float(IT * k))
+        lin(v("it", IT * k, IT * k + IT), v("it", 0, IT), 1.0, float(IT * k))
     act(v("yt", 0, P), v("ps", 2048, 2048 + P))
     for k in (0, 192):
-        act(v("hb", k, k + 192), v("it", 0, 192), FN.Identity, bias=-16.0)
-    fill(v("bz", 2 * XQ, 2 * KID), 0.0)
-    ts(c(6, 3), v("it", 0, 3), 16.0, A_.mult, c(1), A_.add)
-    ts(c(9, 3), c(6, 3), -1.0, A_.mult, float(NA - 1), A_.add)
+        lin(v("hb", k, k + 192), v("it", 0, 192), 1.0, -16.0)
+    fill(v("bz", 4 * X2, 2 * KID), 0.0)
+    lin(c(6, 3), v("it", 0, 3), 16.0, c(1))
+    lin(c(9, 3), c(6, 3), -1.0, float(NA - 1))
     ts(c(18, 3), c(9, 3), -(CAPP - 1) / 2, A_.add, 1.0 / CAPP, A_.mult)
     cp(v("ci", 0, 3), c(18, 3))
     cp(c(12, 3), v("ci", 0, 3))
-    ts(c(32, 3), c(12, 3), -float(CAPP), A_.mult)
-    tt(c(15, 3), c(32, 3), c(9, 3), A_.add)
-    ts(c(21, 3), c(6, 3), 1.0, A_.add)
-    ms(v("bs"), 1.0)
-    ms(v("bs", 0, 99, 33), 0.0)
-    ms(v("bs", 32, 99, 33), 1.0 / 256)
-    ts(v("cmp", 0, 99, 33), c(12, 3), 32.0, A_.mult)
+    lin(c(32, 3), c(12, 3), float(CAPP), -0.5)
+    tt(c(15, 3), c(32, 3), c(9, 3), A_.subtract)
+    lin(c(21, 3), c(6, 3), -128.0)
+    lin(c(54, 3), c(12, 3), -32.0 / 1024)
+    for k in range(3):
+        lin(v("bs", 32 * k, 32 * k + 32), v("it", 0, 32), -1.0 / 1024, c(54 + k))
     ts(c(35, 3), c(12, 3), 4.0, A_.is_ge, -112.0, A_.mult)
-    ts(c(38, 3), c(12, 3), 32.0, A_.mult, 2.0, A_.add)
+    lin(c(38, 3), c(12, 3), 32.0, 2.0)
     tt(c(27, 3), c(35, 3), c(38, 3), A_.add)
     cp(v("iq16", 0, 6, 2), c(27, 3))
     cp(v("iq16", 1, 6, 2), c(27, 3))
+    lin(c(70, 3), c(12, 3), 10.0, float(88 - 10 * low))
+    ts(c(73, 3), c(70, 3), 88.0, A_.is_ge, -80.0, A_.mult)
+    tt(c(76, 3), c(70, 3), c(73, 3), A_.add)
+    cp(v("iq16", 6, 12, 2), c(76, 3))
+    cp(v("iq16", 7, 12, 2), c(76, 3))
     cp(v("ex16"), v("exi"))
-    ts(c(30), c(3), 2.0, A_.mult, -3.5, A_.add)
-    ts(v("qc"), v("qc"), c(30), A_.add, 0.5, A_.mult)
-    ts(c(31), c(3), 16.0, A_.mult)
+    lin(c(30), c(3), 1.0, -1.75)
+    lin(v("qc"), v("qc"), 0.5, c(30))
+    lin(v("qc0"), v("qc"), 4.0, 4096.0)
+    lin(c(28), c(3), 1.0, float(4 - low // 2))
+    ts(c(29), c(28), 4.0, A_.is_ge, -4.0, A_.mult)
+    ts(c(31), c(28), c(29), A_.add, 20.0, A_.mult)
     ts(v("me16"), v("mei"), c(31), A_.add)
     ts(v("dm"), v("dm"), c(1), A_.is_equal)
-    ts(v("dm2", 0, 48), v("dm", 0, 48), -1.0, A_.mult)
+    lin(v("dm2", 0, 48), v("dm", 0, 48), -1.0)
     act(v("dm2", 48, 96), v("dm", 0, 48))
     fill(v("r16"), 1.0)
     ms(v("r16", 0, 96, 16), 0.0)
     fill(v("qo"), rank * 0.5 - 1.75)
-    for k, o in enumerate(range(12, P, 32)):
-        ms(v("mo16", 2 * k, 2 * k + 2), o)
     fill(v("thr", 0, 87), 1.0)
     fill(v("mk", 0, 87), 1.0)
     fill(v("eb", 0, 87), 0.0)
     ms(v("thr", 69), 0.0)
     ms(v("mk", 0, 51, 50), 0.0)
     ms(v("eb", 49), float(NS))
-    ts(v("eb", 67, 87, 19), c(6, 2), 2.0, A_.mult, float(K), A_.add)
-    fill(v("mm"), 1.0)
+    fill(v("sm"), 1.0)
     for k in range(3):
-        ts(v("mm", ML * k, ML * k + NA), v("it", 0, NA), c(6 + k), A_.is_gt)
-        ts(v("sm", 50 * k, 50 * k + 50), v("it", 0, 50), c(21 + k), A_.not_equal, 2.0, A_.mult)
-    ts(v("sm"), v("sm"), -1.0, A_.add)
+        act(v("mm", ML * k, ML * k + ML), v("it", 0, ML), FN.Relu, bias=c(21 + k), scale=128.0)
+        lin(v("sm", 66 * k + 1, 66 * k + 17), v("dm", 0, 16), -2.0, 1.0)
     ms(v("sm", 0, 150, 50), 0.0)
     ms(v("es", 0, 150, 50), 0.0)
     ms(v("es", 49, 150, 50), float(NA))
-    for t in range(2 * R):
+    for t in range(R):
         fill(v("so", 256 * t, 256 * t + 2 * NA), 0.0)
     fill(v("kt", 256, MO), 0.0)
     fill(v("kt", MO + 256, 1040), 0.0)
-    fill(v("neg", 0, NS), 0.0)
-    fill(v("neg", NS, 2 * NS), 64.0)
-    act(v("xc"), v("it", 0, NA), FN.Identity, bias=float(K + 32))
+    fill(v("neg"), 0.0)
+    for k in range(2):
+        lin(v("ramp", NA * k, NA * k + NA), v("it", 0, NA), -64.0, -64.0 - UNIT * k)
+    lin(v("xc"), v("it", 0, NA), 1.0, K + UNIT)
     ms(v("eqx", NA), -BIG)
     ms(v("cap", NA), BIG)
+    ms(v("cap2", NA), BIG)
     for t in range(R - 1):
         fill(v("so2", 256 * t, 256 * t + 2 * NA), -BIG)
-    ts(c(25), c(2), 16.0, A_.mult)
-    ts(c(26), c(2), 32.0, A_.mult, float(X2 - K), A_.add)
-    act(v("uI", 0, K), v("it", 0, K), FN.Identity, bias=c(25))
-    act(v("uI", K, NS), v("it", K, NS), FN.Identity, bias=c(26))
+    lin(c(25), c(2), 16.0)
+    lin(c(26), c(2), 32.0, float(X2 - K))
+    lin(v("uI", 0, K), v("it", 0, K), 1.0, c(25))
+    for k in range(2):
+        ts(v("uI", K + k, NS, 2), v("it", 0, K), c(25), A_.add, float(X2 * (k + 1)), A_.add)
     cp(v("cw16", 0), c(0))
     ts(v("cw16", 1, 3), c(7, 2), c(26), A_.add)
     ts(c(41), c(1), 2.0, A_.min, 5.0, A_.add)
-    ts(v("pw16", 0), c(2), 8.0, A_.mult, c(41), A_.add)
     for k, sh in enumerate((6, 4, 3, 2, 1, 0)):
         ts(v("bi", 2 + k), v("pi", 0), sh, A_.logical_shift_right, 1, A_.bitwise_and)
     cp(v("bf", 2, 8), v("bi", 2, 8))
-    ts(c(42), v("bf", 7), 32.0, A_.mult)
-    ts(c(43), v("bf", 6), 16.0, A_.mult, c(42), A_.add)
-    ts(c(52), v("bf", 5), 8.0, A_.mult, c(43), A_.add)
+    lin(c(79), v("bf", 3), 10.0, c(41))
+    ts(v("pw16", 0), c(79), c(31), A_.add)
+    lin(c(42), v("bf", 7), 32.0)
+    lin(c(43), v("bf", 6), 16.0, c(42))
+    lin(c(52), v("bf", 5), 8.0, c(43))
     ts(v("bf", 0, 2), v("bf", 3, 5), v("bf", 2), A_.not_equal, 4.0, A_.mult)
     ts(v("xb16", 0), v("bf", 0), c(52), A_.add)
     ts(v("xo16", 0), v("bf", 1), c(52), A_.add)
-    ts(c(53), v("bf", 7), float(XQ), A_.add)
+    lin(c(53), v("bf", 7), 1.0, float(XQ))
     ts(v("pg16", 0, 2), c(44, 2), v("bf", 7), A_.subtract, 0.5, A_.mult)
     ts(v("pg16", 2, 4), v("pg16", 0, 2), 8.0, A_.add)
+    lin(c(57), v("bf", 7), 31.0, float(K))
+    ts(v("eb", 67, 87, 19), c(6, 2), c(57), A_.add)
     ts(c(18), v("bf", 7), v("bf", 3), A_.not_equal, float(P), A_.mult)
-    ts(c(19), v("bf", 3), -32.0, A_.mult, 16.0, A_.add)
+    lin(c(19), v("bf", 3), -32.0, 16.0)
     ts(c(20), v("bf", 7), c(19), A_.mult, c(18), A_.add)
     ts(c(32), c(1), 16.0, A_.mult, 144.0, A_.min)
     ts(v("ho16", 0), c(32), c(20), A_.add)
@@ -379,18 +422,24 @@ def rank_program(g, core, T, topo):
         name, o = {"uS": ("uS", 96 * t), "uP": ("uS", 96 * t + NS)}.get(name, (name, NS * t))
         return v(name, o + a, o + b)
 
-    cp(v("mf"), v("meta"))
+    act(v("fe"), by(v("val2"), v("mo16")))
+    turn(v("fm2"), v("fe"))
+    cp(v("po16"), v("o16", 0, 6, 2))
+    cp(by(v("fm2"), v("po16")), v("neg"))
+    cp(v("mf", 0, 20), v("meta", 6, 26))
+    cp(v("mf", 20, 80), v("meta", 32, 92))
     cp(v("plw"), by(v("mf"), v("pw16", 0)))
-    act(v("fe"), by(v("mf"), v("me16")), FN.Identity, bias=-1023.0)
-    cp(v("p16", 0, 3), v("plw", 0, 3))
+    act(v("fe"), by(v("mf"), v("me16")), FN.Identity, bias=-1024.0, scale=0.25)
+    ts(v("p16", 0, 3), v("plw", 0, 3), 0.25, A_.mult, -1024.0, A_.add)
     turn(v("fm"), v("fe"))
     act(held("uP", 0), by(v("it", 0, P), v("p16", 0, 3)))
-    act(held("uM", 0), by(v("fm"), v("p16", 0, 3)))
-    cp(by(v("fm"), v("p16", 0, 3)), v("neg", 0, NS))
+    act(v("fm3"), v("fm"))
+    act(held("uM", 0), by(v("fm3"), v("p16", 0, 3)))
+    cp(by(v("fm"), v("p16", 0, 3)), v("neg"))
     act(v("ml", ML - P, ML), v("fm"))
 
     def opens(t):
-        for name in (("uM", "uP", "uS") if t < R - 1 else ("uP",)) if t else ():
+        for name in (("uM", "uP", "uS") if t < R - 1 else ("uM", "uP")) if t else ():
             cp(by(held(name, t), v("rk16", 0, 3)), held(name, t - 1))
         act(v("ti", 64 * t + 32, 64 * t + 48), held("uP", t, 0, K))
         act(v("ti", 64 * t + 48, 64 * t + 64), held("uP", t, 0, K))
@@ -401,34 +450,38 @@ def rank_program(g, core, T, topo):
         else:
             act(v("ti", 64 * t, 64 * t + 16), held("uI", t, 0, K))
             act(v("ti", 64 * t + 16, 64 * t + 32), held("uI", t, 0, K))
+            for k in range(4):
+                act(v("ti", 192 + K * k, 208 + K * k), held("uM", t, K + K * (k // 2), 2 * K + K * (k // 2)))
 
     oq, oh_ = (32 * (rank // 2), 32 * (rank // 2) + 32), 16 * (rank % 2)
 
-    def rising(t, places, mine):
-        act(v("junk", 320, 320 + K), places, FN.Sign, bias=mine, scale=-1.0, acc=v("od", t))
-        ts(v("lim", t), v("od", t), 32.0, A_.mult, 512.0, A_.add)
+    def rising(t, places, own):
+        act(v("junk", 320, 320 + K), places, FN.Sign, bias=own, scale=-1.0, acc=v("od", t))
+        ts(v("lim", t), v("od", t), 17.0, A_.add, -UNIT / 2, A_.mult)
 
     def table(a, k):
         mm(k, "ubc", "ubs", 0, "pc", "pl", a, 256)
         act(v("bz", a - XQ, a - XQ + 256), v("ps", 512 * k, 512 * k + 256), FN.Sign, bias=-TINY)
 
-    def ahead(tile, cn, sn, a, to, banks):
+    def ahead(tile, cn, sn, a, n, to, banks, e=0):
         for i in range(8):
-            k = banks[i % len(banks)]
+            k = 4 + i % 4
             mm(k, "wcs", "wss", 128 * i, cn, sn, a, 256)
-            act(v(tile, i, 2048, 8), v("ps", 512 * k, 512 * k + 256), FN.Relu, scale=0.05)
-        for h in range(0, 512, 128):
+            relu(v(tile, i, 8 * n, 8), v("ps", 512 * k + e, 512 * k + 256, 256 // n), tile == "kt1" and i % 4 == 1)
+        for h in range(0, 2 * n, 128):
             quant(v("pc", to + h, to + h + 128), v("pl", to + h, to + h + 128), v(tile, 4 * h, 4 * h + 512))
-        for h in range(2):
+        for h in range(n // 128):
             table(to + 256 * h, banks[h])
 
     def outputs(t):
-        h = 64 * t + oh_
-        n, at, new = P + 256 * (t + 1), v("own16", 4 * t), v("own16", 4 * t + 2)
-        turn(v("tt", 64 * t, 64 * t + 64), v("ti", 64 * t, 64 * t + 64))
-        ts(v("tt", 33 + h, p=oq), v("tt", h, p=oq), float(XQ), A_.subtract, v("tt", 32 + h, p=oq), A_.max)
-        spread("tt", 32 + h, 34 + h, rank // 2)
-        cp(v("own16", 4 * t, 4 * t + 4, 2), v("tt", 32 + h, 34 + h))
+        h, w = 64 * t + oh_, 64 if t < R - 1 else 128
+        n, new, at = P + 256 * (t + 1), v("own16", 4 * t), v("own16", 4 * t + 2)
+        turn(v("tt", 64 * t, 64 * t + w), v("ti", 64 * t, 64 * t + w))
+        ts(v("tt", h, p=oq), v("tt", h, p=oq), float(XQ), A_.subtract, v("tt", 32 + h, p=oq), A_.max)
+        for o in range(0, 128, 32):
+            if o != oq[0]:
+                act(v("tt", h, h + w - 31, 32, p=(o, o + 32)), v("tt", h, h + w - 31, 32, p=oq))
+        cp(v("own16", 4 * t, 4 * t + 4, 2), v("tt", h, h + 33, 32))
         cols, ys = v("t16", 32 * t + 16, 32 * t + 32), v("t16", 32 * t, 32 * t + 16)
         if t < R - 1:
             act(ys, by(v("yt", 0, n), new))
@@ -436,6 +489,9 @@ def rank_program(g, core, T, topo):
             cp(by(v("hb", 16, 16 + P), at), cols)
             store(t)
             return
+        ts(v("mk16"), v("tt", h + 64, h + 97, 32), 1023.0, A_.add, 0.5, A_.mult)
+        act(v("ml", NA, NA + NS - K), by(v("it", 0, 1024), v("mk16")), FN.Identity, bias=-1023.0, scale=2.0)
+        act(v("ml", ML - P, ML), v("fm2"))
         act(v("op"), by(v("it", 0, P), at))
         rising(t, v("op"), v("tt", 32 + h))
         cp(by(v("hb", 208, 208 + P), at), v("it", P, P + K))
@@ -448,14 +504,13 @@ def rank_program(g, core, T, topo):
         act(v("ya", 0, K), by(v("yt", 0, n - 256), new))
 
     def store(t):
-        cp(by(v("yb", P * t, P * t + P), v("own16", 4 * t)), v("t16", 32 * t, 32 * t + 16))
+        cp(by(v("yb", P * t, P * t + P), v("own16", 4 * t + 2)), v("t16", 32 * t, 32 * t + 16))
         dma("S", "y%d" % t, T.y[:, P * t:P * t + P], v("yb", P * t, P * t + P))
 
     kids = [("pc", "pl", XQ), ("poc", "pol", P + 256), ("k2c", "k2s", 0)]
     for t in range(R):
         kid, (kc, ks, k0) = KID + 256 * t, kids[t]
         end = t == R - 1
-        ml = NA + P if end else ML
         opens(t)
         if end:
             outputs(t)
@@ -463,47 +518,33 @@ def rank_program(g, core, T, topo):
             for i in range(8):
                 mm(i, "wcs", "wss", 128 * i, "pc", "pl", 0, 128)
             for i in range(8):
-                o, z = v("kt0", i, 1024, 8), v("ps", 512 * i, 512 * i + 128)
-                if i % 2:
-                    ts(o, z, 0.0, A_.max, 0.05, A_.mult)
-                else:
-                    act(o, z, FN.Relu, scale=0.05)
+                relu(v("kt0", i, 1024, 8), v("ps", 512 * i, 512 * i + 128), i in (5, 7))
             for a in (0, 128):
                 quant(v("pc", XQ + a, XQ + a + 128), v("pl", XQ + a, XQ + a + 128), v("kt0", 4 * a, 4 * a + 512))
-            mm(0, "uac", "uas", 0, "pc", "pl", XQ, 128, True, False)
-            mm(0, "uac", "uas", 128, "pc", "pl", XQ + 128, 128, False, True)
-            act(v("bits"), v("ps", 0, 128), FN.Sign, bias=-TINY)
-            digits()
         else:
             act(v("bits"), by(v("bz", 0, 2 * kid), v("bl16", 0, 8)))
             digits()
-            pick(kc, ks, k0, 256, "pc", "pl", XQ + 2 * kid, v("kl16"))
+            for k in (0, 8):
+                pick(kc, ks, k0 + 16 * k, 128, "pc", "pl", XQ + 2 * kid, v("kl16", k, k + 8))
         mm(1, "u0c", "u0s", 0, kc, ks, k0, 256)
         mm(2, "wcs", "wss", 0, kc, ks, k0, 256)
         act(v("kt", 0, 256), v("ps", 512, 768))
-        act(v("mx"), by(v("val"), v("ex16")))
-        if t == 0:
+        if t:
+            act(v("mx"), by(v("val"), v("ex16", 0, 16)))
+        else:
+            act(v("mx"), by(v("mf"), v("ex16", 16, 32)), FN.Identity, bias=-1024.0, scale=0.25)
             dma("S", "kc", w8(v("poc", P, P + 256)), w8(v("pc", XQ, XQ + 256)))
             dma("S", "ks", v("pol", P, P + 256), v("pl", XQ, XQ + 256))
-            table(XQ, 4)
-            ahead("kt1", "pc", "pl", XQ, XQ + 2 * KID, (4, 5, 6, 7))
-            ahead("kt2", "pc", "pl", X2, XQ + 2 * X2, (4, 5, 6, 7))
-        elif not end:
-            ahead("kt3", kc, ks, k0, XQ + 2 * kid, (4, 5, 6, 7))
+        if t:
+            tt(v("iq"), by(v("val"), v("iq16", 0, 6)), v("qo" if end else "qc"), A_.is_equal)
         else:
-            marks("hc", "hs")
-            act(v("fe"), by(v("val2"), v("mo16")))
-            turn(v("fm"), v("fe"))
-            cp(by(v("fm"), v("own16", 4 * t)), v("neg", 0, K))
-            act(v("ml", NA, ml), v("fm"))
-        tt(v("iq"), by(v("val"), v("iq16")), v("qo" if end else "qc"), A_.is_equal)
+            tt(v("iq"), by(v("mf"), v("iq16", 6, 12)), v("qc0"), A_.is_equal)
         turn(v("iqt"), v("iq"))
-        scan(v("cnt"), v("r32", 0, 96), v("iqt"), A_.mult, A_.add)
-        for k in range(3):
-            ts(v("cmp", 33 * k + 1, 33 * k + 33), v("cnt", 32 * k, 32 * k + 32), c(15 + k), A_.is_le)
+        for k in range(0, 96, 32):
+            scan(v("cnt", k, k + 32), v("r32", 0, 32), v("iqt", k, k + 32), A_.mult, A_.add, c(15 + k // 32))
         turn(v("kt", MO, MO + 256), v("mx"))
-        scan(v("pos", 0, 99), v("bs", 0, 99), v("cmp", 0, 99), A_.mult, A_.add)
-        ts(v("a16", 0, 3), v("pos", 32, 99, 33), 256.0, A_.mult)
+        scan(v("pos"), v("bs"), v("cnt"), A_.max, A_.min, -1.0)
+        ts(v("a16", 0, 3), v("pos", 31, 96, 32), -1024.0, A_.mult, 511.0, A_.min)
         tt(v("dg", 48, 96), by(v("kt", MO, 1040), v("a16", 0, 3)), v("dm2", 48, 96), A_.mult)
         tt(v("dg", 0, 48), by(v("kt", 0, MO), v("a16", 0, 3)), v("dm2", 0, 48), A_.mult)
         act(v("ml", 0, NA), by(v("kt", MO, 1040), v("a16", 0, 3)))
@@ -518,13 +559,19 @@ def rank_program(g, core, T, topo):
         act(v("yt", P + 256 * t, P + 256 * t + 256), v("ps", 1024, 1280))
         act(v("yb", P * t, P * t + P), v("yt", 0, P) if t == 0 else v("yb", P * t - P, P * t))
         if end:
-            ts(v("ac16", 0, 3), v("pos", 32, 99, 33), 256.0, A_.mult, 255.0, A_.min)
+            ts(v("ac16", 0, 3), v("pos", 31, 96, 32), -1024.0, A_.mult, 255.0, A_.min)
             pick("ac", "asc", K, NA, kc, ks, 256, v("ac16", 0, 3))
             act(v("ya", K, 64), by(v("yt", P + 256 * t, P + 256 * t + 256), v("ac16", 0, 3)))
         if t == 0:
             mm(3, "u0c", "u0s", 0, "pc", "pl", 0, XQ)
             act(v("sp"), v("ps", 1536, 1536 + XQ))
             act(held("uS", 0), by(v("sp"), v("cw16", 0, 3)))
+            table(XQ, 0)
+            ahead("kt1", "pc", "pl", XQ, 256, XQ + 2 * KID, (0, 1))
+            ahead("kt2", "pc", "pl", X2, 128, XQ + 2 * X2, (3,))
+        elif not end:
+            ahead("kt3", kc, ks, k0, 256, XQ + 2 * kid, (0, 1))
+            ahead("kt4", "pc", "pl", X2, 128, XQ + 4 * X2, (3,), 1)
         sw = 96 * t
         if not end:
             act(v("aS", 0, K), held("uS", t, 0, K))
@@ -538,22 +585,21 @@ def rank_program(g, core, T, topo):
             for a, b in ((1, 49), (51, 86)):
                 tt(v("mk", a, b), v("thr", a, b), v("thr", a + 1, b + 1), A_.mult)
         for k in range(3):
-            ts(v("em", ml * k, ml * k + ml), v("ml", 0, ml), v("dgs", 63 + 16 * k), A_.is_equal, 128.0, A_.mult)
+            ts(v("em", ML * k, ML * k + ML), v("ml"), v("dgs", 63 + 16 * k), A_.is_equal, 128.0, A_.mult)
         for k in range(3):
             ts(v("es", 50 * k + 1, 50 * k + 49), v("aS", K, 64), v("dgs", 16 * k + 15), A_.add, 0.0, A_.is_equal)
-        for k in range(3):
-            scan(v("ems", ml * k, ml * k + ml), v("em", ml * k, ml * k + ml), v("mm", ML * k, ML * k + ml), A_.max, A_.mult)
+        for k in range(0, 3 * ML, ML):
+            scan(v("ems", k, k + ML), v("em", k, k + ML), v("mm", k, k + ML), A_.max, A_.min)
         scan(v("ess"), v("es"), v("sm"), A_.add, A_.mult)
         for k in range(3):
-            ts(v("s16", k), v("da", k), v("ess", 50 * k + 49), A_.add, v("ems", ml * k + ml - 1), A_.add)
-        cp(by(v("so", 512 * t + 256, 512 * t + 512), v("s16", 0, 3)), v("neg", NS, 2 * NS))
-        cp(by(v("so", 512 * t, 512 * t + 256), v("s16", 0, 3)), v("xc"))
-        srt, fl = v("so", 512 * t, 512 * t + 2 * NA, 2), v("so", 512 * t + 256, 512 * t + 256 + 2 * NA, 2)
-        scan(v("cum"), fl, fl, A_.add, A_.max)
-        ts(v("cap", 0, NA), v("cum"), v("lim", t), A_.subtract, STEEP, A_.mult)
-        tt(v("eqx", 0, NA), srt, v("cum"), A_.subtract)
+            ts(v("s16", k), v("da", k), v("ess", 50 * k + 49), A_.add, v("ems", ML * k + ML - 1), A_.add)
+        cp(by(v("so", 256 * t, 256 * t + 256), v("s16", 0, 3)), v("xc"))
+        srt = v("so", 256 * t, 256 * t + 2 * NA, 2)
+        scan(v("cap", 0, NA), srt, v("neg"), A_.add, A_.add, v("lim", t))
+        tt(v("eqx", 0, NA), srt, v("ramp", NA, 2 * NA), A_.add)
+        scan(v("yr"), v("ramp", 0, NA), v("cap", 0, NA), A_.max, A_.min, -BIG)
         scan(v("ys"), v("eqx"), v("cap"), A_.max, A_.min, -BIG)
-        ts(v("n16"), v("ys", NA - 1, NA + 1), v("lim", t), A_.add, c(1), A_.max)
+        ts(v("n16"), v("ys", NA - 1, NA + 1), v("yr", NA - 1), A_.subtract, c(1), A_.max)
         if end:
             pick("hc", "hs", P, K, "ac", "asc", 64, v("n16", 0))
             pick("occ", "ocs", 0, P, "hc", "hs", P + K, v("l16", 16, 26))
@@ -564,20 +610,23 @@ def rank_program(g, core, T, topo):
             store(t)
             break
         cp(by(v("so2", 256 * t, 256 * t + 256), v("s16", 0, 3)), v("aS", K, 64))
-        ts(v("so2", 256 * t + 2 * NA), v("cap", NA - 1), -1.0, A_.mult, v("sw", sw + 15), A_.min)
-        scan(v("zz"), v("so2", 256 * t, 256 * t + 2 * NA + 2, 2), v("cap"), A_.max, A_.min, -BIG)
+        ts(v("so2", 256 * t + 2 * NA), v("cap", NA - 1), -STEEP, A_.mult, v("sw", sw + 15), A_.min)
+        act(v("cap2", 0, NA), v("cap", 0, NA), scale=STEEP)
+        scan(v("zz"), v("so2", 256 * t, 256 * t + 2 * NA + 2, 2), v("cap2"), A_.max, A_.min, -BIG)
         cp(held("uS", t, 0, K), by(v("aS"), v("n16", 0)))
         act(held("uI", t, 0, K), by(v("aI"), v("n16", 0)))
         for k in (1, 2, 0):
-            mine, (a, n) = v("sw", sw + 15 + 16 * k) if k else v("zz", NA), CUT[k]
-            act(v("junk", NS * k, NS * k + n), held("uS", t, 0, n), FN.Sign, bias=mine, scale=-1.0, acc=v("dr", k))
-            ts(v("eb", a + 1, a + n + 1), held("uS", t, 0, n), mine, A_.is_equal)
+            own, (a, n) = v("sw", sw + 15 + 16 * k) if k else v("zz", NA), CUT[k]
+            act(v("junk", NS * k, NS * k + n), held("uS", t, 0, n), FN.Sign, bias=own, scale=-1.0, acc=v("dr", k))
+            ts(v("eb", a + 1, a + n + 1), held("uS", t, 0, n), own, A_.is_equal)
         act(v("ti", 64 * t, 64 * t + 32), by(v("aI"), v("n16")))
         act(held("uM", t, 0, K), by(v("aM"), v("n16", 0)))
         for a, b in ((50, 87), (0, 50)):
             scan(v("ebs", a, b), v("eb", a, b), v("mk", a, b), A_.add, A_.mult)
         for k in (1, 2, 0):
             ts(v("rk16", k), v("ebs", CUT[k][0] + CUT[k][1] + 1), v("dr", k), A_.subtract, 0.5, A_.mult)
+        if t == 0:
+            ts(v("eb", 67, 87, 19), c(6, 2), 2.0, A_.mult, float(K), A_.add)
         cp(by(held("uI", t + 1), v("rk16", 0, 3)), held("uI", t))
         cp(v("t0"), by(held("uI", t + 1), v("pg16")))
         turn(v("tr"), v("t0"))
@@ -609,34 +658,50 @@ def rank_program(g, core, T, topo):
             for name, m, pm in regs:
                 log.setdefault(name, []).append((m, pm, write, i))
         x["need"] = need
-    users = [[] for x in nodes]
+        x["done"] = [j for j, d in need.items() if d]
+    users = [{} for x in nodes]
     for i, x in enumerate(nodes):
-        for j in x["need"]:
-            users[j].append(i)
+        for j, done in x["need"].items():
+            users[j][i] = done
 
-    def arrange(skip, more):
-        tail = list(more)
-        for i in range(len(nodes) - 1, -1, -1):
-            tail[i] += nodes[i]["cost"]
-            for j, done in nodes[i]["need"].items():
-                tail[j] = max(tail[j], tail[i] + WAKE if done else tail[i] - nodes[j]["cost"] + nodes[j]["hold"])
-        free, start, left = {}, {}, [len(x["need"]) for x in nodes]
-        ready = {i: 0.0 for i in range(len(nodes)) if not left[i]}
-        plan_ = []
+    def place(order, back, pace, wake, dmas):
+        at, busy = {}, {}
+        for i in order:
+            x = nodes[i]
+            f = pace if x["sem"] in "VAE" else dmas
+            hold, cost, t_ = x["hold"] * f, x["cost"] * f, 0.0
+            for j, done in (users[i] if back else x["need"]).items():
+                y = nodes[j]
+                f = pace if y["sem"] in "VAE" else dmas
+                if back:
+                    t_ = max(t_, at[j] + y["hold"] * f + (wake + cost - hold if done else 0.0 if y["q"] == x["q"] else -hold))
+                else:
+                    t_ = max(t_, at[j] + (y["cost"] * f + wake if done else y["hold"] * f if y["q"] == x["q"] else 0.0))
+            if back:
+                t_ = max(t_, cost - hold)
+            line = busy.setdefault(x["q"], [])
+            k = 0
+            for a_, b_ in line:
+                if t_ + hold <= a_:
+                    break
+                t_ = max(t_, b_)
+                k += 1
+            line.insert(k, (t_, t_ + hold))
+            at[i] = t_
+        return {i: at[i] + (nodes[i]["hold"] * (pace if nodes[i]["sem"] in "VAE" else dmas) if back else 0.0) for i in at}
+
+    def sort(key):
+        left, out = [len(x["need"]) for x in nodes], []
+        ready = [i for i in range(len(nodes)) if not left[i]]
         while ready:
-            est = {i: max(r, free.get(nodes[i]["q"], 0.0)) for i, r in ready.items()}
-            i = min(est, key=lambda k: (est[k], -tail[k]))
-            q, lim = nodes[i]["q"], est[i] + skip * nodes[i]["hold"]
-            i = max((j for j in est if j == i or nodes[j]["q"] == q and est[j] < lim), key=lambda k: tail[k])
-            start[i] = est[i]
-            free[q] = est[i] + nodes[i]["hold"]
-            plan_.append(i)
-            del ready[i]
+            i = min(ready, key=lambda k: key[k])
+            ready.remove(i)
+            out.append(i)
             for j in users[i]:
                 left[j] -= 1
                 if not left[j]:
-                    ready[j] = max(start[k] + (nodes[k]["cost"] + WAKE if d else 0) for k, d in nodes[j]["need"].items())
-        return plan_, tail
+                    ready.append(j)
+        return out
 
     def span(plan_, pace, wake, dmas):
         free, end, why, late = {}, {}, {}, {}
@@ -659,21 +724,26 @@ def rank_program(g, core, T, topo):
         got = [span(plan_, *m) for m in PACES]
         return sum(t_ for t_, off in got), [o for t_, off in got for o in off]
 
-    for x in nodes:
-        x["done"] = [j for j, d in x["need"].items() if d]
-    best = None
-    for skip in SKIPS:
-        more = [0.0] * len(nodes)
+    best, seed = None, 1
+    for m in [] if ORDER else PACES:
+        tail = [0.0] * len(nodes)
+        for i in range(len(nodes) - 1, -1, -1):
+            tail[i] += nodes[i]["cost"] * (m[0] if nodes[i]["sem"] in "VAE" else m[2])
+            for j, done in nodes[i]["need"].items():
+                tail[j] = max(tail[j], tail[i] + m[1] if done else tail[i] - nodes[j]["cost"] + nodes[j]["hold"])
+        key = [-t_ for t_ in tail]
         for again in range(TURNS):
-            plan, tail = arrange(skip, more)
-            t_, off = judge(plan)
-            if best is None or t_ < best[0]:
-                best = (t_, plan, off)
-            for i, late in off:
-                if late > 400:
-                    more[i] = tail[i] + STEP
-    seed = 1
-    for again in range(TRIES):
+            at = place(sort(key), False, *m)
+            plan = sort(at)
+            got = judge(plan)
+            if best is None or got[0] < best[0]:
+                best = (got[0], plan, got[1])
+            at = place(plan[::-1], True, *m)
+            key = []
+            for i in range(len(nodes)):
+                seed = (seed * 1103515245 + 12345) % 2147483648
+                key.append(-at[i] + SHAKE * (again % 3) * (seed >> 16) / 32768)
+    for again in range(0 if ORDER else TRIES):
         t_, plan, off = best
         seed = (seed * 1103515245 + 12345) % 2147483648
         i = off[(seed >> 8) % len(off)][0]
@@ -686,8 +756,10 @@ def rank_program(g, core, T, topo):
             got = judge(new)
             if got[0] < t_:
                 best = (got[0], new, got[1])
+    if not ORDER:
+        ORDER.update({i: k for k, i in enumerate(best[1])})
     count, seen, drain = {}, {q: {} for q in Q}, []
-    for i in best[1]:
+    for i in sort(ORDER):
         x = nodes[i]
         if x["q"] != "R":
             waits = {}

@@ -1,5 +1,5 @@
 from concourse.bass import DstId, RemoteDMATransfer
-from concourse.mybir import dt, AluOpType, AxisListType, ActivationFunctionType
+from concourse.mybir import dt, AluOpType, ActivationFunctionType
 
 N, P, K, CAPP, R = 8, 160, 16, 6, 3
 NS = R * K
@@ -12,42 +12,70 @@ MO, IT = 520, 264
 CODE, U8, F, B, H, I, U = "float8_e4m3fn_x4", "uint8", "float32", "bfloat16", "float16", "int32", "uint16"
 SCRATCH = {"ps": ("psum", [128, 4096], "float32")}
 for _d, _l in (
-    (CODE, dict(quc=128, qxc=P, u0c=128, ubc=128, kxc=2 * P, wcs=1024, pc=POOL, poc=OWN, k2c=256, occ=P, hc=P + K, ac=64)),
-    (U8, dict(qus=128, qxs=P, u0s=128, ubs=128, kxs=2 * P, wss=1024, pl=POOL, pol=OWN, k2s=256, ocs=P, hs=P + K, asc=64)),
+    (CODE, dict(quc=128, qxc=P, u0c=128, ubc=128, kxc=2 * P, wcs=1024, pc=POOL, poc=OWN, k2c=256, occ=P, hc=OWN + K, ac=64)),
+    (U8, dict(qus=128, qxs=P, u0s=128, ubs=128, kxs=2 * P, wss=1024, pl=POOL, pol=OWN, k2s=256, ocs=P, hs=OWN + K, asc=64)),
     (B, dict(ut=512, u0t=512, xt=640, kt0=1024, kxt=8 * P, bo=2 * P, b0=64, kt1=2048, kt2=1024, kt3=2048, kt4=1024,
-             bz=POOL - XQ, m0=322, r32=32, mm=3 * ML, sm=150, e0=322, e0s=322, junk=640, oh=256, oht=256, bits=128,
-             bt=128, thr=150, iq=96, iqt=96, cnt=96, em=3 * ML, ems=3 * ML, es=150, ess=150, bx=800, bs=96)),
+             bz=POOL - XQ, m0=322, pb=2, mm=3 * ML, sm=150, e0=322, e0s=322, junk=640, oh=256, oht=256, bits=128,
+             bt=128, thr=150, iq=96, iqt=96, cnt=96, em=3 * ML, ems=3 * ML, es=150, ess=150, bx=928, bs=96)),
     (I, dict(pi=2, bi=8, ci=4, exi=42)),
-    (U, dict(meta=92, ul=8, ex16=42, iq16=12, c16=44, me16=10, o16=8, p16=4, rk16=4, a16=8, s16=4, n16=2,
-             kl16=16, bl16=16, own16=4 * R, l16=32)),
+    (U, dict(meta=92, ul=8, ex16=42, iq16=12, c16=44, me16=10, o16=8, p16=4, rk16=4, a16=8, s16=4, n16=4,
+             kl16=16, bl16=16, own16=4 * R, l16=16)),
     (H, dict(ml=ML, pos=96)),
     (F, dict(mf=80, bf=8, cc=80, ohs=128, qc0=96, fm2=P, fm3=P, it=4 * IT, iw=128, r16=96, dm=96, dm2=96, hm=P, qc=96,
              neg=NS, xc=NA, sml=48, val=128, plw=16, fe=P, fm=P, sp=XQ, uS=R * 96,
-             uI=R * NS, uM=R * NS, sw=2 * 96, swd=96, so2=512, wk=360, aS=64, aI=64, aM=64, kt=1040,
+             uI=R * NS, uM=R * NS, sw=2 * 96, swd=96, so2=512, wk=360, aS=96, aI=64, aM=64, kt=1040,
              mx=256, dg=96, dgs=96, so=R * 256, t0=64, tr=64, ti=256, tt=256,
-             yt=P + R * 256, yb=R * P, t16=R * 32, hb=384, ht=704, fx=560)),
+             yt=P + R * 256, yb=R * P, t16=R * 32, hb=192, ht=352, fx=560)),
 ):
     for _k, _n in _l.items():
         SCRATCH[_k] = ("sbuf", [128, _n], _d)
-PART = {"sab": ("sml", 0, 2), "dab": ("sml", 2, 2), "wab": ("sml", 4, 2), "y1": ("sml", 6, 6), "y2": ("sml", 12, 6),
+PART = {"sab": ("sml", 0, 2), "dab": ("sml", 2, 2), "y1": ("sml", 6, 6),
         "y3": ("sml", 18, 4), "da": ("sml", 34, 4), "od": ("sml", 38, 3), "lim": ("sml", 41, 3),
         "xo16": ("c16", 0, 2), "pw16": ("c16", 2, 2), "cw16": ("c16", 4, 4), "ho16": ("c16", 8, 2),
         "ac16": ("c16", 10, 4), "mo16": ("ex16", 32, 10), "xb16": ("c16", 24, 2), "pg16": ("c16", 26, 4),
         "g16": ("c16", 30, 2), "ms": ("c16", 32, 5), "mk16": ("c16", 38, 2), "po16": ("c16", 40, 3),
-        "eqx": ("wk", 0, NA + 1), "cap": ("wk", 52, NA + 1), "ys": ("wk", 104, NA + 1), "yr": ("wk", 160, NA),
-        "ramp": ("wk", 208, 2 * NA), "cap2": ("wk", 304, NA + 1), "mk": ("bx", 0, 150),
-        "eb": ("bx", 160, 150), "ebs": ("bx", 320, 150), "bits2": ("bx", 480, P), "bt2": ("bx", 640, P),
+        "eqx": ("wk", 0, NA), "cap": ("wk", 52, NA), "ys": ("wk", 104, NA), "yr": ("wk", 160, NA),
+        "ramp": ("wk", 208, 2 * NA), "cap2": ("wk", 304, NA + 1), "mk": ("bx", 0, 150), "eb": ("bx", 160, 150),
+        "ebs": ("bx", 320, 150), "hm2": ("bx", 800, 128), "bits2": ("bx", 480, P), "bt2": ("bx", 640, P),
         "val2": ("fx", 400, P), "qo": ("fx", 128, 96), "ya": ("fx", 224, 64), "dr": ("fx", 288, 4),
         "up5": ("fx", 296, NS), "zz": ("fx", 344, NA + 1), "op": ("fx", 0, K), "w0": ("fx", 16, 40), "mei": ("fx", 56, 10)}
 SEMAPHORES = ["V", "A", "E", "G", "lu", "lx", "lw0", "lw1", "lw2", "lw3", "ls", "m0", "a1", "a2", "m1", "m2", "b1", "b2",
-              "sent", "kc", "ks", "y0", "y1", "y2", "oc", "os"]
+              "sent", "kc", "ks", "hc", "hs", "y0", "y1", "y2", "oc", "os"]
 CUT = ((0, NS), (50, K), (69, K))
 TINY, BIG, STEEP = 1e-37, 1e29, 1e24
 UNIT = 16384.0
-CYCLE, WAKE, LOCAL, WLOAD, FIRST, LONG = 0.9, 200.0, 1500.0, 1200.0, 2000.0, 120.0
+CYCLE, WAKE, LOCAL, WLOAD, FIRST, LONG = 0.9, 200.0, 1500.0, 800.0, 1500.0, 120.0
 FAR = dict(m0=1500, a1=1500, m1=1600, b1=1800, a2=2500, m2=2900, b2=4500)
-PACES = ((1.0, 210, 1.0), (1.15, 150, 1.2), (0.92, 260, 0.7), (1.3, 200, 1.0))
-TURNS, SHAKE, TRIES, ORDER = 40, 40.0, 3000, {}
+ORDER = [
+    0, 1, 7, 72, 20, 21, 23, 74, 22, 25, 228, 24, 73, 76, 27, 75, 35, 26, 2, 3, 8, 4, 5, 6, 9, 10, 210, 212, 211, 189, 185,
+    150, 190, 40, 38, 151, 109, 218, 205, 216, 30, 28, 31, 33, 106, 41, 39, 44, 43, 34, 42, 107, 152, 70, 11, 12, 13, 14,
+    15, 16, 17, 45, 110, 71, 46, 18, 49, 36, 153, 32, 48, 47, 219, 157, 50, 213, 111, 19, 77, 51, 84, 55, 86, 52, 56, 29,
+    37, 53, 154, 57, 78, 173, 85, 220, 79, 54, 88, 174, 188, 90, 58, 80, 59, 172, 92, 81, 108, 158, 91, 89, 93, 87, 94, 95,
+    61, 63, 60, 62, 100, 98, 99, 96, 82, 97, 64, 103, 65, 67, 66, 68, 69, 159, 155, 167, 175, 113, 160, 184, 101, 102, 206,
+    229, 112, 104, 143, 105, 161, 120, 114, 121, 115, 163, 127, 128, 122, 162, 116, 230, 118, 251, 126, 83, 123, 117, 168,
+    164, 147, 209, 119, 165, 166, 125, 226, 124, 217, 231, 227, 176, 169, 208, 225, 156, 129, 232, 170, 195, 177, 131, 171,
+    252, 197, 132, 130, 178, 180, 144, 186, 202, 179, 133, 199, 145, 203, 194, 204, 223, 224, 233, 215, 149, 214, 134, 201,
+    234, 191, 193, 135, 192, 221, 222, 182, 242, 183, 238, 181, 253, 196, 246, 198, 243, 200, 136, 249, 244, 235, 255, 137,
+    241, 187, 247, 245, 254, 236, 148, 142, 237, 138, 146, 139, 248, 239, 207, 240, 140, 250, 267, 425, 141, 273, 271, 275,
+    276, 270, 269, 274, 272, 281, 279, 283, 278, 277, 280, 284, 256, 282, 258, 292, 285, 286, 293, 289, 260, 257, 294, 295,
+    296, 259, 287, 290, 291, 298, 297, 262, 316, 288, 320, 318, 299, 264, 322, 263, 261, 321, 314, 300, 266, 302, 265, 303,
+    309, 368, 301, 362, 268, 428, 304, 376, 311, 429, 319, 305, 363, 374, 375, 377, 378, 379, 380, 382, 383, 381, 308, 306,
+    307, 317, 370, 369, 371, 366, 312, 423, 386, 384, 385, 367, 323, 313, 361, 373, 387, 393, 388, 389, 364, 360, 328, 326,
+    324, 329, 395, 325, 310, 330, 390, 391, 365, 340, 344, 372, 392, 394, 327, 331, 398, 400, 341, 346, 396, 401, 399, 402,
+    345, 397, 347, 342, 348, 343, 352, 354, 350, 403, 335, 406, 407, 334, 408, 409, 410, 333, 332, 315, 349, 353, 355, 351,
+    427, 426, 412, 442, 413, 445, 405, 336, 356, 414, 357, 411, 430, 417, 415, 338, 337, 424, 416, 418, 358, 339, 420, 524,
+    431, 419, 441, 446, 359, 404, 421, 525, 422, 530, 588, 444, 589, 447, 448, 453, 454, 449, 455, 443, 450, 451, 459, 452,
+    433, 528, 532, 533, 531, 523, 432, 434, 522, 458, 460, 534, 456, 480, 461, 463, 462, 435, 535, 457, 465, 464, 482, 478,
+    481, 436, 437, 484, 466, 526, 529, 467, 583, 470, 469, 479, 486, 468, 471, 527, 472, 538, 474, 473, 483, 475, 485, 488,
+    536, 541, 540, 539, 537, 542, 544, 545, 543, 490, 548, 546, 547, 439, 440, 585, 492, 489, 491, 487, 493, 549, 555, 504,
+    506, 502, 550, 551, 438, 552, 553, 556, 505, 557, 477, 476, 503, 507, 512, 508, 496, 554, 558, 494, 510, 514, 559, 560,
+    509, 562, 564, 515, 513, 511, 563, 561, 565, 495, 567, 568, 516, 517, 498, 497, 569, 570, 571, 587, 586, 590, 572, 500,
+    499, 608, 607, 591, 519, 573, 518, 574, 602, 520, 566, 619, 501, 578, 576, 593, 577, 575, 601, 609, 610, 580, 521, 605,
+    606, 603, 604, 579, 581, 582, 632, 633, 640, 611, 634, 639, 635, 612, 636, 644, 637, 584, 638, 594, 613, 615, 614, 592,
+    643, 645, 616, 595, 596, 620, 641, 647, 648, 646, 617, 629, 597, 642, 621, 618, 661, 650, 649, 651, 664, 599, 652, 654,
+    600, 663, 653, 622, 656, 598, 657, 655, 627, 628, 662, 669, 668, 673, 672, 671, 670, 631, 658, 659, 660, 666, 630, 667,
+    675, 676, 677, 674, 623, 680, 679, 678, 625, 681, 624, 682, 683, 684, 685, 665, 686, 626, 687, 688, 696, 689, 690, 697,
+    691, 692, 694, 693, 695, 698]
 
 
 def rank_program(g, core, T, topo):
@@ -152,6 +180,10 @@ def rank_program(g, core, T, topo):
     def lin(o, i, a, b=0.0):
         act(o, i, FN.Identity, bias=b, scale=a)
 
+    def move(o, i):
+        add("G", lambda: g.affine_select(o[0], i[0], [[0, o[2]]], A_.is_ge, 0.0, 0, 0), [o], [i], 170 + 2 * CYCLE * o[2])
+        nodes[-1]["free"] = True
+
     def relu(o, z, vector):
         if vector:
             ts(o, z, 0.0, A_.max, 0.05, A_.mult)
@@ -203,7 +235,7 @@ def rank_program(g, core, T, topo):
     dma("A", "lx", v("xt"), T.x[:], 200)
     dma("S", "ls", v("wss"), T.ws[:], WLOAD)
     for k in range(4):
-        dma("S", "lw%d" % k, w8(v("wcs", 256 * k, 256 * k + 256)), T.wc[:, 1024 * k:1024 * k + 1024], WLOAD + 500 * (k + 1))
+        dma("S", "lw%d" % k, w8(v("wcs", 256 * k, 256 * k + 256)), T.wc[:, 1024 * k:1024 * k + 1024], WLOAD + 400 * (k + 1))
     iota(v("pi"), [[0, 2]], 0, 1)
     iota(v("it", 0, IT), [[1, IT]])
     iota(v("iw", 0, 32), [[0, 2], [-2, 16]], P)
@@ -220,7 +252,6 @@ def rank_program(g, core, T, topo):
     iota(v("mei"), [[1, 5], [10, 2]])
     ms(v("ut", 56, 512), 0.0)
     ms(v("e0", 0, 322, 161), 0.0)
-    ms(v("r32"), 1.0)
     cp(c(0), v("pi", 0))
     ts(v("bi", 0), v("pi", 0), 15, A_.bitwise_and)
     ts(v("bi", 1), v("pi", 0), 4, A_.logical_shift_right)
@@ -228,10 +259,10 @@ def rank_program(g, core, T, topo):
     cp(c(1, 3), v("bi", 0, 3))
     ts(c(5), c(0), 32.0, A_.add)
     ts(c(4), c(0), 96.0, A_.is_ge, c(5), A_.mult)
+    cp(v("pb"), v("cc", 0, 5, 4))
     ts(v("m0", 0, 161), v("it", 0, 161), c(0), A_.not_equal, 2.0, A_.mult)
     ts(v("m0", 161, 322), v("it", 0, 161), c(5), A_.not_equal, 2.0, A_.mult)
     ts(v("m0"), v("m0"), -1.0, A_.add)
-    ms(v("m0", 0, 322, 161), 0.0)
     ts(c(44, 8), v("it", 0, 8), 0.0, A_.mult, c(1), A_.add)
     ts(v("ul"), c(44, 8), 1.0, A_.add)
     ts(v("bi", 3), v("pi", 0), 1, A_.bitwise_and)
@@ -245,19 +276,19 @@ def rank_program(g, core, T, topo):
             act(v("u0t", k, 512, 4), v("ut", 256, 384), FN.Identity, bias=v("ut", k))
     quant(v("u0c"), v("u0s"), v("u0t"))
     quant(v("qxc"), v("qxs"), v("xt"))
-    mm(0, "qxc", "qxs", 0, "u0c", "u0s", 0, 128)
-    mm(1, "qxc", "qxs", 32, "u0c", "u0s", 0, 128)
+    quant(v("quc"), v("qus"), v("ut"))
+    mm(0, "qxc", "qxs", 0, "quc", "qus", 0, 128)
+    mm(1, "qxc", "qxs", 32, "quc", "qus", 0, 128)
     mm(2, "u0c", "u0s", 0, "qxc", "qxs", 0, P)
     mm(3, "u0c", "u0s", 0, "qxc", "qxs", 0, P)
-    cp(v("sab", 0), v("ps", 0))
-    act(v("sab", 1), v("ps", 512))
+    ts(v("sab", 0), v("ps", 0), -1.0, A_.mult)
+    act(v("sab", 1), v("ps", 512), scale=-1.0)
     for k in range(2):
-        act(v("junk", P * k, P * k + P), v("ps", 1536, 1536 + P), FN.Sign, bias=v("sab", k), scale=-1.0, acc=v("dab", k))
-        ts(v("e0", 161 * k + 1, 161 * k + 161), v("ps", 1024, 1024 + P), v("sab", k), A_.is_equal)
-    scan(v("e0s"), v("e0"), v("m0"), A_.add, A_.mult)
-    tt(v("wab"), v("e0s", 160, 322, 161), v("dab"), A_.add)
-    for k in range(2):
-        ts(v("oh", 128 * k, 128 * k + 128), v("iw"), v("wab", k), A_.is_equal, c(4 * k), A_.mult)
+        a = 161 * k
+        act(v("junk", P * k, P * k + P), v("ps", 1536, 1536 + P), FN.Sign, bias=v("sab", k), acc=v("dab", k))
+        ts(v("e0", a + 1, a + 161), v("ps", 1024, 1024 + P), v("sab", k), A_.add, 0.0, A_.is_equal)
+        scan(v("e0s", a, a + 161), v("e0", a, a + 161), v("m0", a, a + 161), A_.add, A_.mult, v("dab", k))
+        ts(v("oh", 128 * k, 128 * k + 128), v("iw"), v("e0s", a + P), A_.is_equal, v("pb", k), A_.mult)
     turn(v("oht"), v("oh"))
     for k in range(0, 128, 32):
         scan(v("ohs", k, k + 32), v("oht", k, k + 32), v("oht", 128 + k, 160 + k), A_.add, A_.add, c(63) if k == 96 else 0.0)
@@ -266,11 +297,6 @@ def rank_program(g, core, T, topo):
     for a in range(4):
         cp(v("o16", 0, 8, 2, p=(32 * a, 32 * a + 32)), v("y3", 0, 4, p=(0, 32)))
 
-    def digits(x="", n=128):
-        turn(v("bt" + x), v("bits" + x))
-        scan(v("val" + x), v("hm", 0, n), v("bt" + x), A_.mult, A_.add)
-
-    quant(v("quc"), v("qus"), v("ut"))
     pick("ubc", "ubs", 0, 128, "quc", "qus", 128, v("ul"))
     ms(v("hm"), 2.0)
     ms(v("hm", 0, P, 16), 0.0)
@@ -279,7 +305,8 @@ def rank_program(g, core, T, topo):
     ms(v("hm", 2, P, 16), 0.5)
     mm(5, "ubc", "ubs", 0, "qxc", "qxs", 0, P)
     act(v("bits2"), v("ps", 2560, 2560 + P), FN.Sign, bias=-TINY)
-    digits("2", P)
+    turn(v("bt2"), v("bits2"))
+    scan(v("val2"), v("hm"), v("bt2"), A_.mult, A_.add)
     mine, its = (6, 16) if rank == low else (16, 6)
     ts(v("ms"), v("val2", 12, P, 32), 4.0, A_.mult, 4096.0, A_.add)
     swap("m0", [v("ms")], [mate], [v("meta", its, its + 5)], [v("meta", mine, mine + 5)])
@@ -311,8 +338,8 @@ def rank_program(g, core, T, topo):
     swap("a1", pieces(0, K, rank, 1), [mate], pieces(0, K, mate, 1))
     for k in range(2):
         pick("pc", "pl", X2 + 2 * K * rank + K * k, K, "qxc", "qxs", P, v("o16", 2 + 2 * k))
-    swap("b1", pieces(X2, 2 * K, rank, 1), [mate], pieces(X2, 2 * K, mate, 1))
     swap("m1", [v("meta", mine + 5, mine + 10)], [mate], [v("meta", its + 5, its + 10)])
+    swap("b1", pieces(X2, 2 * K, rank, 1), [mate], pieces(X2, 2 * K, mate, 1))
     swap("a2", pieces(0, K, low, 2), peers, sum([pieces(0, K, pair(r), 2) for r in peers], []))
     swap("m2", [v("meta", 6, 26)], peers, [v("meta", 32, 92)],
          [v("meta", 12 + 10 * ((rank - r) % N), 32 + 10 * ((rank - r) % N)) for r in peers])
@@ -324,8 +351,7 @@ def rank_program(g, core, T, topo):
     for k in range(1, 4):
         lin(v("it", IT * k, IT * k + IT), v("it", 0, IT), 1.0, float(IT * k))
     act(v("yt", 0, P), v("ps", 2048, 2048 + P))
-    for k in (0, 192):
-        lin(v("hb", k, k + 192), v("it", 0, 192), 1.0, -16.0)
+    lin(v("hb"), v("it", 0, 192), 1.0, -16.0)
     fill(v("bz", 4 * X2, 2 * KID), 0.0)
     lin(c(6, 3), v("it", 0, 3), 16.0, c(1))
     lin(c(9, 3), c(6, 3), -1.0, float(NA - 1))
@@ -358,7 +384,9 @@ def rank_program(g, core, T, topo):
     ts(v("me16"), v("mei"), c(31), A_.add)
     ts(v("dm"), v("dm"), c(1), A_.is_equal)
     lin(v("dm2", 0, 48), v("dm", 0, 48), -1.0)
-    act(v("dm2", 48, 96), v("dm", 0, 48))
+    act(v("dm2", 48, 80), v("dm", 0, 32))
+    act(v("dm2", 80, 96), v("dm", 0, 16), scale=-128.0)
+    act(v("hm2"), v("hm", 0, 128))
     fill(v("r16"), 1.0)
     ms(v("r16", 0, 96, 16), 0.0)
     fill(v("qo"), rank * 0.5 - 1.75)
@@ -370,11 +398,15 @@ def rank_program(g, core, T, topo):
     ms(v("eb", 49), float(NS))
     fill(v("sm"), 1.0)
     for k in range(3):
-        act(v("mm", ML * k, ML * k + ML), v("it", 0, ML), FN.Relu, bias=c(21 + k), scale=128.0)
+        if k < 2:
+            act(v("mm", ML * k, ML * k + ML), v("it", 0, ML), FN.Relu, bias=c(21 + k), scale=128.0)
+        else:
+            ts(v("mm", ML * k, ML * k + ML), v("it", 0, ML), c(6 + k), A_.is_le, 128.0, A_.mult)
         lin(v("sm", 66 * k + 1, 66 * k + 17), v("dm", 0, 16), -2.0, 1.0)
     ms(v("sm", 0, 150, 50), 0.0)
     ms(v("es", 0, 150, 50), 0.0)
-    ms(v("es", 49, 150, 50), float(NA))
+    ms(v("es", 49, 100, 50), float(NA))
+    ms(v("es", 149), float(NA + 128))
     for t in range(R):
         fill(v("so", 256 * t, 256 * t + 2 * NA), 0.0)
     fill(v("kt", 256, MO), 0.0)
@@ -383,8 +415,7 @@ def rank_program(g, core, T, topo):
     for k in range(2):
         lin(v("ramp", NA * k, NA * k + NA), v("it", 0, NA), -64.0, -64.0 - UNIT * k)
     lin(v("xc"), v("it", 0, NA), 1.0, K + UNIT)
-    ms(v("eqx", NA), -BIG)
-    ms(v("cap", NA), BIG)
+    ts(v("n16", 1, 3), c(7, 2), float(NA), A_.add)
     ms(v("cap2", NA), BIG)
     for t in range(R - 1):
         fill(v("so2", 256 * t, 256 * t + 2 * NA), -BIG)
@@ -441,15 +472,11 @@ def rank_program(g, core, T, topo):
     def opens(t):
         for name in (("uM", "uP", "uS") if t < R - 1 else ("uM", "uP")) if t else ():
             cp(by(held(name, t), v("rk16", 0, 3)), held(name, t - 1))
-        act(v("ti", 64 * t + 32, 64 * t + 48), held("uP", t, 0, K))
-        act(v("ti", 64 * t + 48, 64 * t + 64), held("uP", t, 0, K))
         if t < R - 1:
             act(v("ml", NA, NA + NS - K), held("uM", t, K))
-            act(v("aI", 0, K), held("uI", t, 0, K))
-            act(v("aM", 0, K), held("uM", t, 0, K))
+            move(v("aI", 0, K), held("uI", t, 0, K))
+            move(v("aM", 0, K), held("uM", t, 0, K))
         else:
-            act(v("ti", 64 * t, 64 * t + 16), held("uI", t, 0, K))
-            act(v("ti", 64 * t + 16, 64 * t + 32), held("uI", t, 0, K))
             for k in range(4):
                 act(v("ti", 192 + K * k, 208 + K * k), held("uM", t, K + K * (k // 2), 2 * K + K * (k // 2)))
 
@@ -476,15 +503,17 @@ def rank_program(g, core, T, topo):
     def outputs(t):
         h, w = 64 * t + oh_, 64 if t < R - 1 else 128
         n, new, at = P + 256 * (t + 1), v("own16", 4 * t), v("own16", 4 * t + 2)
+        for k in range(4):
+            (move if t < R - 1 else act)(v("ti", 64 * t + K * k, 64 * t + K * k + K), held("uP" if k // 2 else "uI", t, 0, K))
         turn(v("tt", 64 * t, 64 * t + w), v("ti", 64 * t, 64 * t + w))
         ts(v("tt", h, p=oq), v("tt", h, p=oq), float(XQ), A_.subtract, v("tt", 32 + h, p=oq), A_.max)
         for o in range(0, 128, 32):
             if o != oq[0]:
                 act(v("tt", h, h + w - 31, 32, p=(o, o + 32)), v("tt", h, h + w - 31, 32, p=oq))
         cp(v("own16", 4 * t, 4 * t + 4, 2), v("tt", h, h + 33, 32))
-        cols, ys = v("t16", 32 * t + 16, 32 * t + 32), v("t16", 32 * t, 32 * t + 16)
+        cols, yn = v("t16", 32 * t + 16, 32 * t + 32), v("t16", 32 * t, 32 * t + 16)
         if t < R - 1:
-            act(ys, by(v("yt", 0, n), new))
+            act(yn, by(v("yt", 0, n), new))
             act(cols, by(v("it", 0, n), new))
             cp(by(v("hb", 16, 16 + P), at), cols)
             store(t)
@@ -494,14 +523,20 @@ def rank_program(g, core, T, topo):
         act(v("ml", ML - P, ML), v("fm2"))
         act(v("op"), by(v("it", 0, P), at))
         rising(t, v("op"), v("tt", 32 + h))
-        cp(by(v("hb", 208, 208 + P), at), v("it", P, P + K))
-        for k in range(2):
-            turn(v("ht", 352 * k, 352 * k + P), v("hb", 192 * k + 16, 192 * k + 16 + P))
-            turn(v("ht", 352 * k + P, 352 * k + 352), v("hb", 192 * k, 192 * k + 192))
-            cp(v("l16", 16 * k, 16 * k + 16), by(v("ht", 352 * k, 352 * k + 352), v("ho16", 0)))
-        pick("hc", "hs", 0, P, "poc", "pol", OWN, v("l16", 0, 10))
+        cp(by(v("hb", 16, 16 + P), at), v("it", OWN, OWN + K))
+        turn(v("ht", 0, P), v("hb", 16, 16 + P))
+        turn(v("ht", P, 352), v("hb"))
+        cp(v("l16"), by(v("ht"), v("ho16", 0)))
+        dma("S", "hc", w8(v("hc", 0, OWN)), w8(v("poc")))
+        dma("S", "hs", v("hs", 0, OWN), v("pol"))
         pick("ac", "asc", 0, K, "poc", "pol", OWN, new)
         act(v("ya", 0, K), by(v("yt", 0, n - 256), new))
+
+    def ys(t):
+        cn, sn, a = ("poc", "pol", P + 256 * t) if t < R - 1 else kids[t]
+        mm(2, "wcs", "wss", 0, cn, sn, a, 256)
+        act(v("yt", P + 256 * t, P + 256 * t + 256), v("ps", 1024, 1280))
+        move(v("yb", P * t, P * t + P), v("yt", 0, P) if t == 0 else v("yb", P * t - P, P * t))
 
     def store(t):
         cp(by(v("yb", P * t, P * t + P), v("own16", 4 * t + 2)), v("t16", 32 * t, 32 * t + 16))
@@ -522,12 +557,14 @@ def rank_program(g, core, T, topo):
             for a in (0, 128):
                 quant(v("pc", XQ + a, XQ + a + 128), v("pl", XQ + a, XQ + a + 128), v("kt0", 4 * a, 4 * a + 512))
         else:
-            act(v("bits"), by(v("bz", 0, 2 * kid), v("bl16", 0, 8)))
-            digits()
+            cp(v("bits", 0, 64), by(v("bz", 0, 2 * kid), v("bl16", 0, 4)))
+            act(v("bits", 64, 128), by(v("bz", 0, 2 * kid), v("bl16", 4, 8)))
+            turn(v("bt"), v("bits"))
+            scan(v("bits"), v("hm2"), v("bt"), A_.mult, A_.add)
+            scan(v("val"), v("hm", 0, 128), v("bt"), A_.mult, A_.add)
             for k in (0, 8):
                 pick(kc, ks, k0 + 16 * k, 128, "pc", "pl", XQ + 2 * kid, v("kl16", k, k + 8))
         mm(1, "u0c", "u0s", 0, kc, ks, k0, 256)
-        mm(2, "wcs", "wss", 0, kc, ks, k0, 256)
         act(v("kt", 0, 256), v("ps", 512, 768))
         if t:
             act(v("mx"), by(v("val"), v("ex16", 0, 16)))
@@ -536,12 +573,12 @@ def rank_program(g, core, T, topo):
             dma("S", "kc", w8(v("poc", P, P + 256)), w8(v("pc", XQ, XQ + 256)))
             dma("S", "ks", v("pol", P, P + 256), v("pl", XQ, XQ + 256))
         if t:
-            tt(v("iq"), by(v("val"), v("iq16", 0, 6)), v("qo" if end else "qc"), A_.is_equal)
+            tt(v("iq"), by(v("bits"), v("iq16", 0, 6)), v("qo" if end else "qc"), A_.is_equal)
         else:
             tt(v("iq"), by(v("mf"), v("iq16", 6, 12)), v("qc0"), A_.is_equal)
         turn(v("iqt"), v("iq"))
         for k in range(0, 96, 32):
-            scan(v("cnt", k, k + 32), v("r32", 0, 32), v("iqt", k, k + 32), A_.mult, A_.add, c(15 + k // 32))
+            scan(v("cnt", k, k + 32), v("iqt", k, k + 32), v("neg", 0, 32), A_.add, A_.add, c(15 + k // 32))
         turn(v("kt", MO, MO + 256), v("mx"))
         scan(v("pos"), v("bs"), v("cnt"), A_.max, A_.min, -1.0)
         ts(v("a16", 0, 3), v("pos", 31, 96, 32), -1024.0, A_.mult, 511.0, A_.min)
@@ -556,9 +593,8 @@ def rank_program(g, core, T, topo):
         if not end:
             act(v("aI", K, 64), by(v("it", 0, MO), v("a16", 0, 3)), FN.Identity, bias=float(kid))
             act(v("aM", K, 64), by(v("kt", MO, 1040), v("a16", 0, 3)))
-        act(v("yt", P + 256 * t, P + 256 * t + 256), v("ps", 1024, 1280))
-        act(v("yb", P * t, P * t + P), v("yt", 0, P) if t == 0 else v("yb", P * t - P, P * t))
         if end:
+            ys(t)
             ts(v("ac16", 0, 3), v("pos", 31, 96, 32), -1024.0, A_.mult, 255.0, A_.min)
             pick("ac", "asc", K, NA, kc, ks, 256, v("ac16", 0, 3))
             act(v("ya", K, 64), by(v("yt", P + 256 * t, P + 256 * t + 256), v("ac16", 0, 3)))
@@ -574,7 +610,8 @@ def rank_program(g, core, T, topo):
             ahead("kt4", "pc", "pl", X2, 128, XQ + 4 * X2, (3,), 1)
         sw = 96 * t
         if not end:
-            act(v("aS", 0, K), held("uS", t, 0, K))
+            move(v("aS", 0, K), held("uS", t, 0, K))
+            move(v("aS", 64, 96), held("uS", t, K))
             for k in (NS, 0):
                 tt(v("swd", k, k + NS), v("uS", sw + k, sw + k + NS), v("dm", 0, NS), A_.mult)
                 scan(v("sw", sw + k, sw + k + NS), v("r16", 0, NS), v("swd", k, k + NS), A_.mult, A_.add)
@@ -585,24 +622,28 @@ def rank_program(g, core, T, topo):
             for a, b in ((1, 49), (51, 86)):
                 tt(v("mk", a, b), v("thr", a, b), v("thr", a + 1, b + 1), A_.mult)
         for k in range(3):
-            ts(v("em", ML * k, ML * k + ML), v("ml"), v("dgs", 63 + 16 * k), A_.is_equal, 128.0, A_.mult)
+            if k == 2:
+                act(v("em", ML * k, ML * k + ML), v("ml"), FN.Abs, bias=v("dgs", 63 + 16 * k), scale=128.0)
+            else:
+                ts(v("em", ML * k, ML * k + ML), v("ml"), v("dgs", 63 + 16 * k), A_.is_equal, 128.0, A_.mult)
         for k in range(3):
             ts(v("es", 50 * k + 1, 50 * k + 49), v("aS", K, 64), v("dgs", 16 * k + 15), A_.add, 0.0, A_.is_equal)
         for k in range(0, 3 * ML, ML):
-            scan(v("ems", k, k + ML), v("em", k, k + ML), v("mm", k, k + ML), A_.max, A_.min)
+            scan(v("ems", k, k + ML), v("em", k, k + ML), v("mm", k, k + ML),
+                 *((A_.min, A_.max, 128.0) if k == 2 * ML else (A_.max, A_.min)))
         scan(v("ess"), v("es"), v("sm"), A_.add, A_.mult)
         for k in range(3):
-            ts(v("s16", k), v("da", k), v("ess", 50 * k + 49), A_.add, v("ems", ML * k + ML - 1), A_.add)
+            ts(v("s16", k), v("da", k), v("ess", 50 * k + 49), A_.add, v("ems", ML * k + ML - 1), A_.subtract if k == 2 else A_.add)
         cp(by(v("so", 256 * t, 256 * t + 256), v("s16", 0, 3)), v("xc"))
         srt = v("so", 256 * t, 256 * t + 2 * NA, 2)
-        scan(v("cap", 0, NA), srt, v("neg"), A_.add, A_.add, v("lim", t))
-        tt(v("eqx", 0, NA), srt, v("ramp", NA, 2 * NA), A_.add)
-        scan(v("yr"), v("ramp", 0, NA), v("cap", 0, NA), A_.max, A_.min, -BIG)
+        scan(v("cap"), srt, v("neg"), A_.add, A_.add, v("lim", t))
+        tt(v("eqx"), srt, v("ramp", NA, 2 * NA), A_.add)
+        scan(v("yr"), v("ramp", 0, NA), v("cap"), A_.max, A_.min, -BIG)
         scan(v("ys"), v("eqx"), v("cap"), A_.max, A_.min, -BIG)
-        ts(v("n16"), v("ys", NA - 1, NA + 1), v("yr", NA - 1), A_.subtract, c(1), A_.max)
+        ts(v("n16", 0), v("ys", NA - 1), v("yr", NA - 1), A_.subtract, c(1), A_.max)
         if end:
-            pick("hc", "hs", P, K, "ac", "asc", 64, v("n16", 0))
-            pick("occ", "ocs", 0, P, "hc", "hs", P + K, v("l16", 16, 26))
+            pick("hc", "hs", OWN, K, "ac", "asc", 64, v("n16", 0))
+            pick("occ", "ocs", 0, P, "hc", "hs", OWN + K, v("l16", 0, 10))
             dma("S", "oc", T.oc[:], w8(v("occ")))
             for k in range(4):
                 dma("S" if k == 3 else "A", "os", T.osc[4 * k:4 * k + 4, :], v("ocs", p=(32 * k, 32 * k + 4)))
@@ -611,15 +652,16 @@ def rank_program(g, core, T, topo):
             break
         cp(by(v("so2", 256 * t, 256 * t + 256), v("s16", 0, 3)), v("aS", K, 64))
         ts(v("so2", 256 * t + 2 * NA), v("cap", NA - 1), -STEEP, A_.mult, v("sw", sw + 15), A_.min)
-        act(v("cap2", 0, NA), v("cap", 0, NA), scale=STEEP)
+        act(v("cap2", 0, NA), v("cap"), scale=STEEP)
         scan(v("zz"), v("so2", 256 * t, 256 * t + 2 * NA + 2, 2), v("cap2"), A_.max, A_.min, -BIG)
-        cp(held("uS", t, 0, K), by(v("aS"), v("n16", 0)))
         act(held("uI", t, 0, K), by(v("aI"), v("n16", 0)))
         for k in (1, 2, 0):
             own, (a, n) = v("sw", sw + 15 + 16 * k) if k else v("zz", NA), CUT[k]
-            act(v("junk", NS * k, NS * k + n), held("uS", t, 0, n), FN.Sign, bias=own, scale=-1.0, acc=v("dr", k))
-            ts(v("eb", a + 1, a + n + 1), held("uS", t, 0, n), own, A_.is_equal)
-        act(v("ti", 64 * t, 64 * t + 32), by(v("aI"), v("n16")))
+            new = by(v("aS"), v("n16", 0, n // 16))
+            act(v("junk", NS * k, NS * k + n), new, FN.Sign, bias=own, scale=-1.0, acc=v("dr", k))
+            ts(v("eb", a + 1, a + n + 1), new, own, A_.is_equal)
+        if t == 0:
+            act(held("uS", t, 0, K), by(v("aS"), v("n16", 0)))
         act(held("uM", t, 0, K), by(v("aM"), v("n16", 0)))
         for a, b in ((50, 87), (0, 50)):
             scan(v("ebs", a, b), v("eb", a, b), v("mk", a, b), A_.add, A_.mult)
@@ -637,6 +679,7 @@ def rank_program(g, core, T, topo):
         act(v("tr", 4, 64, 8, p=(64, 128)), v("tr", 0, 64, 8, p=(0, 64)))
         ts(v("bl16"), by(v("tr"), v("xb16", 0)), 2.0, A_.mult, v("bf", 7), A_.add)
         ts(v("kl16"), by(v("tr"), v("xo16", 0)), 2.0, A_.mult, c(53), A_.add)
+        ys(t)
         outputs(t)
 
     log, last = {}, {}
@@ -646,7 +689,8 @@ def rank_program(g, core, T, topo):
         if x["q"] in "GS":
             if x["q"] in last:
                 need[last[x["q"]]] = False
-            last[x["q"]] = i
+            if not x.get("free"):
+                last[x["q"]] = i
         for regs, write in ((x["rd"], False), (x["wr"], True)):
             for name, m, pm in regs:
                 for em, ep, ew, j in log.get(name, []):
@@ -658,108 +702,23 @@ def rank_program(g, core, T, topo):
             for name, m, pm in regs:
                 log.setdefault(name, []).append((m, pm, write, i))
         x["need"] = need
-        x["done"] = [j for j, d in need.items() if d]
-    users = [{} for x in nodes]
+    users = [[] for x in nodes]
     for i, x in enumerate(nodes):
-        for j, done in x["need"].items():
-            users[j][i] = done
-
-    def place(order, back, pace, wake, dmas):
-        at, busy = {}, {}
-        for i in order:
-            x = nodes[i]
-            f = pace if x["sem"] in "VAE" else dmas
-            hold, cost, t_ = x["hold"] * f, x["cost"] * f, 0.0
-            for j, done in (users[i] if back else x["need"]).items():
-                y = nodes[j]
-                f = pace if y["sem"] in "VAE" else dmas
-                if back:
-                    t_ = max(t_, at[j] + y["hold"] * f + (wake + cost - hold if done else 0.0 if y["q"] == x["q"] else -hold))
-                else:
-                    t_ = max(t_, at[j] + (y["cost"] * f + wake if done else y["hold"] * f if y["q"] == x["q"] else 0.0))
-            if back:
-                t_ = max(t_, cost - hold)
-            line = busy.setdefault(x["q"], [])
-            k = 0
-            for a_, b_ in line:
-                if t_ + hold <= a_:
-                    break
-                t_ = max(t_, b_)
-                k += 1
-            line.insert(k, (t_, t_ + hold))
-            at[i] = t_
-        return {i: at[i] + (nodes[i]["hold"] * (pace if nodes[i]["sem"] in "VAE" else dmas) if back else 0.0) for i in at}
-
-    def sort(key):
-        left, out = [len(x["need"]) for x in nodes], []
-        ready = [i for i in range(len(nodes)) if not left[i]]
-        while ready:
-            i = min(ready, key=lambda k: key[k])
-            ready.remove(i)
-            out.append(i)
-            for j in users[i]:
-                left[j] -= 1
-                if not left[j]:
-                    ready.append(j)
-        return out
-
-    def span(plan_, pace, wake, dmas):
-        free, end, why, late = {}, {}, {}, {}
-        for i in plan_:
-            x = nodes[i]
-            r = max([(0.0, -1)] + [(end[j] + wake, j) for j in x["done"]])
-            s0, why[i] = max(r, free.get(x["q"], (0.0, -1)))
-            late[i] = s0 - r[0]
-            f = pace if x["sem"] in "VAE" else dmas
-            free[x["q"]], end[i] = (s0 + x["hold"] * f, i), s0 + x["cost"] * f
-        i = max(end, key=lambda k: end[k])
-        t_, off = end[i], []
-        while i >= 0:
-            if late[i] > 0:
-                off.append((i, late[i]))
-            i = why[i]
-        return t_, off
-
-    def judge(plan_):
-        got = [span(plan_, *m) for m in PACES]
-        return sum(t_ for t_, off in got), [o for t_, off in got for o in off]
-
-    best, seed = None, 1
-    for m in [] if ORDER else PACES:
-        tail = [0.0] * len(nodes)
-        for i in range(len(nodes) - 1, -1, -1):
-            tail[i] += nodes[i]["cost"] * (m[0] if nodes[i]["sem"] in "VAE" else m[2])
-            for j, done in nodes[i]["need"].items():
-                tail[j] = max(tail[j], tail[i] + m[1] if done else tail[i] - nodes[j]["cost"] + nodes[j]["hold"])
-        key = [-t_ for t_ in tail]
-        for again in range(TURNS):
-            at = place(sort(key), False, *m)
-            plan = sort(at)
-            got = judge(plan)
-            if best is None or got[0] < best[0]:
-                best = (got[0], plan, got[1])
-            at = place(plan[::-1], True, *m)
-            key = []
-            for i in range(len(nodes)):
-                seed = (seed * 1103515245 + 12345) % 2147483648
-                key.append(-at[i] + SHAKE * (again % 3) * (seed >> 16) / 32768)
-    for again in range(0 if ORDER else TRIES):
-        t_, plan, off = best
-        seed = (seed * 1103515245 + 12345) % 2147483648
-        i = off[(seed >> 8) % len(off)][0]
-        at = plan.index(i)
-        lo = max([plan.index(j) for j in nodes[i]["need"]] + [-1]) + 1
-        same = [k for k in range(lo, at) if nodes[plan[k]]["q"] == nodes[i]["q"]]
-        if same:
-            k = same[-1 - (seed >> 20) % min(3, len(same))]
-            new = plan[:k] + [i] + plan[k:at] + plan[at + 1:]
-            got = judge(new)
-            if got[0] < t_:
-                best = (got[0], new, got[1])
-    if not ORDER:
-        ORDER.update({i: k for k, i in enumerate(best[1])})
+        for j in x["need"]:
+            users[j].append(i)
+    key = {i: k for k, i in enumerate(ORDER)}
+    left, plan = [len(x["need"]) for x in nodes], []
+    ready = [i for i in range(len(nodes)) if not left[i]]
+    while ready:
+        i = min(ready, key=lambda k: key[k])
+        ready.remove(i)
+        plan.append(i)
+        for j in users[i]:
+            left[j] -= 1
+            if not left[j]:
+                ready.append(j)
     count, seen, drain = {}, {q: {} for q in Q}, []
-    for i in sort(ORDER):
+    for i in plan:
         x = nodes[i]
         if x["q"] != "R":
             waits = {}

from concourse.bass import DstId, RemoteDMATransfer
from concourse.mybir import dt, AluOpType, ActivationFunctionType

N, P, K, CAPP, R = 8, 160, 16, 6, 3
NS = R * K
NA = N * CAPP
X2, XQ, KID = N * K, N * NS, N * NS + P
POOL = XQ + 2 * (KID + 512)
OWN = P + 512
ML = NA + (NS - K) + P
MO, IT = 520, 264
CODE, U8, F, B, H, I, U = "float8_e4m3fn_x4", "uint8", "float32", "bfloat16", "float16", "int32", "uint16"
SCRATCH = {"ps": ("psum", [128, 4096], "float32")}
for _d, _l in (
    (CODE, dict(quc=128, qxc=P, u0c=128, ubc=128, kxc=2 * P, wcs=1024, pc=POOL, poc=OWN, k2c=256, occ=P, hc=OWN + K, ac=64)),
    (U8, dict(qus=128, qxs=P, u0s=128, ubs=128, kxs=2 * P, wss=1024, pl=POOL, pol=OWN, k2s=256, ocs=P, hs=OWN + K, asc=64)),
    (B, dict(ut=512, u0t=512, xt=640, kt0=1024, kxt=8 * P, bo=2 * P, b0=64, kt1=2048, kt2=1024, kt3=2048, kt4=1024,
             bz=POOL - XQ, m0=322, pb=2, mm=3 * ML, sm=150, e0=322, e0s=322, junk=640, oh=256, oht=256, bits=128,
             bt=128, thr=150, iq=96, iqt=96, cnt=96, em=3 * ML, ems=3 * ML, es=150, ess=150, bx=928, bs=96)),
    (I, dict(pi=2, bi=8, ci=4, exi=42)),
    (U, dict(meta=92, ul=8, ex16=42, iq16=12, c16=44, me16=10, o16=8, p16=4, rk16=4, a16=8, s16=4, n16=4,
             kl16=16, bl16=16, own16=4 * R, l16=16)),
    (H, dict(ml=ML, pos=96)),
    (F, dict(mf=80, bf=8, cc=80, ohs=128, qc0=96, fm2=P, fm3=P, it=4 * IT, iw=128, r16=96, dm=96, dm2=96, hm=P, qc=96,
             neg=NS, xc=NA, sml=48, val=128, plw=16, fe=P, fm=P, sp=XQ, uS=R * 96,
             uI=R * NS, uM=R * NS, sw=2 * 96, swd=96, so2=512, wk=360, aS=96, aI=64, aM=64, kt=1040,
             mx=256, dg=96, dgs=96, so=R * 256, t0=64, tr=64, ti=256, tt=256,
             yt=P + R * 256, yb=R * P, t16=R * 32, hb=192, ht=352, fx=560)),
):
    for _k, _n in _l.items():
        SCRATCH[_k] = ("sbuf", [128, _n], _d)
PART = {"sab": ("sml", 0, 2), "dab": ("sml", 2, 2), "y1": ("sml", 6, 6),
        "y3": ("sml", 18, 4), "da": ("sml", 34, 4), "od": ("sml", 38, 3), "lim": ("sml", 41, 3),
        "xo16": ("c16", 0, 2), "pw16": ("c16", 2, 2), "cw16": ("c16", 4, 4), "ho16": ("c16", 8, 2),
        "ac16": ("c16", 10, 4), "mo16": ("ex16", 32, 10), "xb16": ("c16", 24, 2), "pg16": ("c16", 26, 4),
        "g16": ("c16", 30, 2), "ms": ("c16", 32, 5), "mk16": ("c16", 38, 2), "po16": ("c16", 40, 3),
        "eqx": ("wk", 0, NA), "cap": ("wk", 52, NA), "ys": ("wk", 104, NA), "yr": ("wk", 160, NA),
        "ramp": ("wk", 208, 2 * NA), "cap2": ("wk", 304, NA + 1), "mk": ("bx", 0, 150), "eb": ("bx", 160, 150),
        "ebs": ("bx", 320, 150), "hm2": ("bx", 800, 128), "bits2": ("bx", 480, P), "bt2": ("bx", 640, P),
        "val2": ("fx", 400, P), "qo": ("fx", 128, 96), "ya": ("fx", 224, 64), "dr": ("fx", 288, 4),
        "up5": ("fx", 296, NS), "zz": ("fx", 344, NA + 1), "op": ("fx", 0, K), "w0": ("fx", 16, 40), "mei": ("fx", 56, 10)}
SEMAPHORES = ["V", "A", "E", "G", "lu", "lx", "lw0", "lw1", "lw2", "lw3", "ls", "m0", "a1", "a2", "m1", "m2", "b1", "b2",
              "sent", "kc", "ks", "hc", "hs", "y0", "y1", "y2", "oc", "os"]
CUT = ((0, NS), (50, K), (69, K))
TINY, BIG, STEEP = 1e-37, 1e29, 1e24
UNIT = 16384.0
CYCLE, WAKE, LOCAL, WLOAD, FIRST, LONG = 0.9, 200.0, 1500.0, 800.0, 1500.0, 120.0
FAR = dict(m0=1500, a1=1500, m1=1600, b1=1800, a2=2500, m2=2900, b2=4500)
ORDER = [
    0, 1, 7, 72, 20, 21, 23, 74, 22, 25, 228, 24, 73, 76, 27, 75, 35, 26, 2, 3, 8, 4, 5, 6, 9, 10, 210, 212, 211, 189, 185,
    150, 190, 40, 38, 151, 109, 218, 205, 216, 30, 28, 31, 33, 106, 41, 39, 44, 43, 34, 42, 107, 152, 70, 11, 12, 13, 14,
    15, 16, 17, 45, 110, 71, 46, 18, 49, 36, 153, 32, 48, 47, 219, 157, 50, 213, 111, 19, 77, 51, 84, 55, 86, 52, 56, 29,
    37, 53, 154, 57, 78, 173, 85, 220, 79, 54, 88, 174, 188, 90, 58, 80, 59, 172, 92, 81, 108, 158, 91, 89, 93, 87, 94, 95,
    61, 63, 60, 62, 100, 98, 99, 96, 82, 97, 64, 103, 65, 67, 66, 68, 69, 159, 155, 167, 175, 113, 160, 184, 101, 102, 206,
    229, 112, 104, 143, 105, 161, 120, 114, 121, 115, 163, 127, 128, 122, 162, 116, 230, 118, 251, 126, 83, 123, 117, 168,
    164, 147, 209, 119, 165, 166, 125, 226, 124, 217, 231, 227, 176, 169, 208, 225, 156, 129, 232, 170, 195, 177, 131, 171,
    252, 197, 132, 130, 178, 180, 144, 186, 202, 179, 133, 199, 145, 203, 194, 204, 223, 224, 233, 215, 149, 214, 134, 201,
    234, 191, 193, 135, 192, 221, 222, 182, 242, 183, 238, 181, 253, 196, 246, 198, 243, 200, 136, 249, 244, 235, 255, 137,
    241, 187, 247, 245, 254, 236, 148, 142, 237, 138, 146, 139, 248, 239, 207, 240, 140, 250, 267, 425, 141, 273, 271, 275,
    276, 270, 269, 274, 272, 281, 279, 283, 278, 277, 280, 284, 256, 282, 258, 292, 285, 286, 293, 289, 260, 257, 294, 295,
    296, 259, 287, 290, 291, 298, 297, 262, 316, 288, 320, 318, 299, 264, 322, 263, 261, 321, 314, 300, 266, 302, 265, 303,
    309, 368, 301, 362, 268, 428, 304, 376, 311, 429, 319, 305, 363, 374, 375, 377, 378, 379, 380, 382, 383, 381, 308, 306,
    307, 317, 370, 369, 371, 366, 312, 423, 386, 384, 385, 367, 323, 313, 361, 373, 387, 393, 388, 389, 364, 360, 328, 326,
    324, 329, 395, 325, 310, 330, 390, 391, 365, 340, 344, 372, 392, 394, 327, 331, 398, 400, 341, 346, 396, 401, 399, 402,
    345, 397, 347, 342, 348, 343, 352, 354, 350, 403, 335, 406, 407, 334, 408, 409, 410, 333, 332, 315, 349, 353, 355, 351,
    427, 426, 412, 442, 413, 445, 405, 336, 356, 414, 357, 411, 430, 417, 415, 338, 337, 424, 416, 418, 358, 339, 420, 524,
    431, 419, 441, 446, 359, 404, 421, 525, 422, 530, 588, 444, 589, 447, 448, 453, 454, 449, 455, 443, 450, 451, 459, 452,
    433, 528, 532, 533, 531, 523, 432, 434, 522, 458, 460, 534, 456, 480, 461, 463, 462, 435, 535, 457, 465, 464, 482, 478,
    481, 436, 437, 484, 466, 526, 529, 467, 583, 470, 469, 479, 486, 468, 471, 527, 472, 538, 474, 473, 483, 475, 485, 488,
    536, 541, 540, 539, 537, 542, 544, 545, 543, 490, 548, 546, 547, 439, 440, 585, 492, 489, 491, 487, 493, 549, 555, 504,
    506, 502, 550, 551, 438, 552, 553, 556, 505, 557, 477, 476, 503, 507, 512, 508, 496, 554, 558, 494, 510, 514, 559, 560,
    509, 562, 564, 515, 513, 511, 563, 561, 565, 495, 567, 568, 516, 517, 498, 497, 569, 570, 571, 587, 586, 590, 572, 500,
    499, 608, 607, 591, 519, 573, 518, 574, 602, 520, 566, 619, 501, 578, 576, 593, 577, 575, 601, 609, 610, 580, 521, 605,
    606, 603, 604, 579, 581, 582, 632, 633, 640, 611, 634, 639, 635, 612, 636, 644, 637, 584, 638, 594, 613, 615, 614, 592,
    643, 645, 616, 595, 596, 620, 641, 647, 648, 646, 617, 629, 597, 642, 621, 618, 661, 650, 649, 651, 664, 599, 652, 654,
    600, 663, 653, 622, 656, 598, 657, 655, 627, 628, 662, 669, 668, 673, 672, 671, 670, 631, 658, 659, 660, 666, 630, 667,
    675, 676, 677, 674, 623, 680, 679, 678, 625, 681, 624, 682, 683, 684, 685, 665, 686, 626, 687, 688, 696, 689, 690, 697,
    691, 692, 694, 693, 695, 698]


def rank_program(g, core, T, topo):
    rank = T.rank_of(core)
    if rank is None:
        return
    A_ = AluOpType
    FN = ActivationFunctionType
    mate = [r for r in range(N) if topo.mates(core, T.cores[r])][0]
    peers = [r for r in range(N) if topo.same_plane(core, T.cores[r])]
    low = min(rank, mate)
    assert abs(rank - mate) == 1 and len(peers) == 3
    Q = {"V": g.vector, "A": g.scalar, "E": g.tensor, "G": g, "S": g.sync}
    nodes, gate = [], []

    def v(name, a=None, b=None, s=1, p=(0, 128)):
        name, o, n = PART[name] if name in PART else (name, 0, SCRATCH[name][1][1])
        a, b = (o, o + n) if a is None else (o + a, o + (a + 1 if b is None else b))
        ap_ = T[name][p[0]:p[1], a:b:s] if s != 1 else T[name][p[0]:p[1], a:b]
        if name == "ps":
            m, pm = 1 << (a // 512), 15
        else:
            m = sum(1 << c_ for c_ in range(a, b, s)) if s != 1 else (1 << b) - (1 << a)
            pm = sum(1 << k for k in range(4) if p[0] < 32 * k + 32 and 32 * k < p[1])
        return [ap_, [(name, m, pm)], len(range(a, b, s)), SCRATCH[name][2] in (B, H, U), None]

    def by(win, off):
        return [win[0].indirect(off[0]), win[1] + off[1], 16 * off[2], False, off[1]]

    def w32(x):
        return [x[0].bitcast(dt.uint32)] + x[1:]

    def w8(x):
        return [x[0].bitcast(dt.uint8)] + x[1:]

    def add(q, call, outs, ins, cost, sem=None, inc=1, hold=None, after=()):
        rd, wr = [], []
        for x in ins:
            if isinstance(x, list):
                rd += x[1]
        for x in outs:
            wr += x[1][:1]
            rd += x[4] or []
        nodes.append({"q": q, "call": call, "rd": rd, "wr": wr, "cost": cost, "sem": sem or q, "inc": inc,
                      "hold": cost if hold is None else hold, "after": list(after), "gate": gate[:1] if cost > LONG else []})
        return len(nodes) - 1

    def price(o, i, rate, *more):
        if o[4]:
            return 50 + 3.5 * o[2] * CYCLE
        if i[4]:
            return 55 + 1.6 * i[2] * CYCLE
        if rate is None:
            rate = 0.5 if o[3] and i[3] and all(x[3] for x in more) else 1
        return max(64, rate * i[2]) * CYCLE

    def ap(x):
        return x[0] if isinstance(x, list) else x

    def cp(o, i):
        add("V", lambda: g.vector.tensor_copy(o[0], i[0]), [o], [i], price(o, i, None))

    def tt(o, a, b, op):
        add("V", lambda: g.vector.tensor_tensor(o[0], a[0], b[0], op), [o], [a, b], price(o, a, 2))
        if a[1][0][2] != b[1][0][2]:
            nodes[-1]["drain"] = True
            nodes[-1]["hold"] += WAKE

    def ts(o, a, s1, op0, s2=None, op1=None):
        if op1 is None:
            add("V", lambda: g.vector.tensor_scalar(o[0], a[0], ap(s1), None, op0), [o], [a, s1], price(o, a, None))
        else:
            add("V", lambda: g.vector.tensor_scalar(o[0], a[0], ap(s1), ap(s2), op0, op1), [o], [a, s1, s2], price(o, a, None))

    def scan(o, d0, d1, op0, op1, init=0.0):
        add("V", lambda: g.vector.tensor_tensor_scan(o[0], d0[0], d1[0], ap(init), op0, op1), [o], [d0, d1, init],
            price(o, d0, None, d1))

    def ms(o, c_):
        add("V", lambda: g.vector.memset(o[0], c_), [o], [], price(o, o, None))

    def turn(o, i):
        add("V", lambda: g.vector.transpose(o[0], i[0]), [o], [i], price(o, i, None))

    def quant(c_, s, i):
        add("V", lambda: g.vector.quantize_mx(c_[0], s[0], i[0]), [c_, s], [i], 12 + 0.22 * i[2])

    def act(o, i, fn=None, bias=None, scale=None, acc=None):
        kw = {}
        if bias is not None:
            kw["bias"] = ap(bias)
        if scale is not None:
            kw["scale"] = scale
        if acc is not None:
            kw["accum_out"] = acc[0]
        f = FN.Copy if fn is None else fn
        add("A", lambda: g.scalar.activation(o[0], i[0], f, **kw), [o] + ([acc] if acc else []), [i, bias], price(o, i, 1) + (20 if acc else 0))

    def fill(o, c_):
        act(o, v("it", 0, o[2]), FN.Identity, bias=c_, scale=0.0)

    def lin(o, i, a, b=0.0):
        act(o, i, FN.Identity, bias=b, scale=a)

    def move(o, i):
        add("G", lambda: g.affine_select(o[0], i[0], [[0, o[2]]], A_.is_ge, 0.0, 0, 0), [o], [i], 170 + 2 * CYCLE * o[2])
        nodes[-1]["free"] = True

    def relu(o, z, vector):
        if vector:
            ts(o, z, 0.0, A_.max, 0.05, A_.mult)
        else:
            act(o, z, FN.Relu, scale=0.05)

    def mm(bank, lc, ls, a, rc, rs, b, n, start=True, stop=True):
        o, x = v("ps", 512 * bank, 512 * bank + n), [v(lc, a, a + 128), v(ls, a, a + 128), v(rc, b, b + n), v(rs, b, b + n)]
        add("E", lambda: g.tensor.matmul_mx(o[0], x[0][0], x[1][0], x[2][0], x[3][0], start, stop), [o], x, 0.63 * (n + 16))

    def iota(o, pat, base=0, ch=0):
        if SCRATCH[o[1][0][0]][2] == I:
            add("G", lambda: g.iota(o[0], pat, base, ch), [o], [], 130 + 2 * o[2])
        else:
            add("G", lambda: g.iota(o[0], pat, base, ch, allow_small_or_imprecise_dtypes=True), [o], [], 130 + 2 * o[2])

    def dma(q, sem, o, i, more=0):
        add(q, lambda: Q[q].dma_start(ap(o), ap(i)), [o] if isinstance(o, list) else [], [i], LOCAL + more, sem, 16, 60)

    def pick(oc, os_, a, n, wc_, ws_, wn, off):
        cp(w32(v(oc, a, a + n)), by(w32(v(wc_, 0, wn)), off))
        act(v(os_, a, a + n), by(v(ws_, 0, wn), off))

    def send(x, to, sem, land):
        ids = []
        for r in to:
            rid, pid = topo.addr(T.cores[r], core)
            ids.append(DstId(rid=rid, pnc=pid))
        tr = RemoteDMATransfer(dst_ids=ids, dma_engine_mask=topo.mask(core, T.cores[to[0]]), remote_sem=T.sem[sem],
                               src=x[0], dsts=[y[0] for y in land] if land else [x[0]] * len(to))
        return add("G", lambda: g.remote_dma_fused([tr], local_sem=T.sem.sent), [], [x], 120 + 60 * len(to) + FIRST * (sem == "m0"),
                   "sent", len(topo.engines(core, T.cores[to[0]])))

    def swap(sem, mine, to, theirs, land=None):
        last = [send(x, to, sem, land) for x in mine]
        n = sum(len(topo.engines(T.cores[r], core)) for r in to) * len(mine)
        add("R", None, theirs, [], FAR[sem], sem, n, 0, last)

    def pieces(base, w, r, k):
        return [w8(v("pc", base + w * r, base + w * (r + k))), v("pl", base + w * r, base + w * (r + k))]

    def pair(r):
        return r - rank + low

    def c(j, n=1):
        return v("cc", j, j + n)

    dma("S", "lu", v("ut", 0, 56), T.u[:, 0:56])
    dma("A", "lx", v("xt"), T.x[:], 200)
    dma("S", "ls", v("wss"), T.ws[:], WLOAD)
    for k in range(4):
        dma("S", "lw%d" % k, w8(v("wcs", 256 * k, 256 * k + 256)), T.wc[:, 1024 * k:1024 * k + 1024], WLOAD + 400 * (k + 1))
    iota(v("pi"), [[0, 2]], 0, 1)
    iota(v("it", 0, IT), [[1, IT]])
    iota(v("iw", 0, 32), [[0, 2], [-2, 16]], P)
    for k in range(2):
        iota(v("iw", 32 * k + 32, 32 * k + 64), [[0, 2], [-2, 8], [-32, 2]], P - 32 - 16 * k)
    iota(v("iw", 96, 128), [[-2, 16], [0, 2]], P)
    iota(v("dm"), [[0, 6], [1, 16]])
    iota(v("exi", 0, 16), [[16, 2], [32, 4], [0, 2]], 12)
    k = low or 1
    iota(v("exi", 16, 16 + 2 * k), [[10, k], [0, 2]], -10 * low % 80 + 9)
    iota(v("exi", 16 + 2 * k, 32), [[10, N - k], [0, 2]], 10 * (k - low) + 9)
    iota(v("exi", 32, 42), [[32, 5], [0, 2]], 12)
    iota(v("qc"), [[0, 3], [1, 2], [0, 16]])
    iota(v("mei"), [[1, 5], [10, 2]])
    ms(v("ut", 56, 512), 0.0)
    ms(v("e0", 0, 322, 161), 0.0)
    cp(c(0), v("pi", 0))
    ts(v("bi", 0), v("pi", 0), 15, A_.bitwise_and)
    ts(v("bi", 1), v("pi", 0), 4, A_.logical_shift_right)
    ts(v("bi", 2), v("pi", 0), 5, A_.logical_shift_right)
    cp(c(1, 3), v("bi", 0, 3))
    ts(c(5), c(0), 32.0, A_.add)
    ts(c(4), c(0), 96.0, A_.is_ge, c(5), A_.mult)
    cp(v("pb"), v("cc", 0, 5, 4))
    ts(v("m0", 0, 161), v("it", 0, 161), c(0), A_.not_equal, 2.0, A_.mult)
    ts(v("m0", 161, 322), v("it", 0, 161), c(5), A_.not_equal, 2.0, A_.mult)
    ts(v("m0"), v("m0"), -1.0, A_.add)
    ts(c(44, 8), v("it", 0, 8), 0.0, A_.mult, c(1), A_.add)
    ts(v("ul"), c(44, 8), 1.0, A_.add)
    ts(v("bi", 3), v("pi", 0), 1, A_.bitwise_and)
    ts(c(62), v("bi", 3), float(P), A_.mult)
    ts(c(63), c(0), 32.0, A_.is_lt, c(62), A_.mult)

    for k in range(4):
        if k % 2:
            ts(v("u0t", k, 512, 4), v("ut", 256, 384), v("ut", k), A_.add)
        else:
            act(v("u0t", k, 512, 4), v("ut", 256, 384), FN.Identity, bias=v("ut", k))
    quant(v("u0c"), v("u0s"), v("u0t"))
    quant(v("qxc"), v("qxs"), v("xt"))
    quant(v("quc"), v("qus"), v("ut"))
    mm(0, "qxc", "qxs", 0, "quc", "qus", 0, 128)
    mm(1, "qxc", "qxs", 32, "quc", "qus", 0, 128)
    mm(2, "u0c", "u0s", 0, "qxc", "qxs", 0, P)
    mm(3, "u0c", "u0s", 0, "qxc", "qxs", 0, P)
    ts(v("sab", 0), v("ps", 0), -1.0, A_.mult)
    act(v("sab", 1), v("ps", 512), scale=-1.0)
    for k in range(2):
        a = 161 * k
        act(v("junk", P * k, P * k + P), v("ps", 1536, 1536 + P), FN.Sign, bias=v("sab", k), acc=v("dab", k))
        ts(v("e0", a + 1, a + 161), v("ps", 1024, 1024 + P), v("sab", k), A_.add, 0.0, A_.is_equal)
        scan(v("e0s", a, a + 161), v("e0", a, a + 161), v("m0", a, a + 161), A_.add, A_.mult, v("dab", k))
        ts(v("oh", 128 * k, 128 * k + 128), v("iw"), v("e0s", a + P), A_.is_equal, v("pb", k), A_.mult)
    turn(v("oht"), v("oh"))
    for k in range(0, 128, 32):
        scan(v("ohs", k, k + 32), v("oht", k, k + 32), v("oht", 128 + k, 160 + k), A_.add, A_.add, c(63) if k == 96 else 0.0)
    tt(v("y1", 0, 4, p=(0, 64)), v("ohs", 31, 128, 32, p=(0, 64)), v("ohs", 31, 128, 32, p=(64, 128)), A_.add)
    tt(v("y3", 0, 4, p=(0, 32)), v("y1", 0, 4, p=(0, 32)), v("y1", 0, 4, p=(32, 64)), A_.add)
    for a in range(4):
        cp(v("o16", 0, 8, 2, p=(32 * a, 32 * a + 32)), v("y3", 0, 4, p=(0, 32)))

    pick("ubc", "ubs", 0, 128, "quc", "qus", 128, v("ul"))
    ms(v("hm"), 2.0)
    ms(v("hm", 0, P, 16), 0.0)
    ms(v("hm", 3, P, 16), 0.0)
    ms(v("hm", 1, P, 16), 0.5)
    ms(v("hm", 2, P, 16), 0.5)
    mm(5, "ubc", "ubs", 0, "qxc", "qxs", 0, P)
    act(v("bits2"), v("ps", 2560, 2560 + P), FN.Sign, bias=-TINY)
    turn(v("bt2"), v("bits2"))
    scan(v("val2"), v("hm"), v("bt2"), A_.mult, A_.add)
    mine, its = (6, 16) if rank == low else (16, 6)
    ts(v("ms"), v("val2", 12, P, 32), 4.0, A_.mult, 4096.0, A_.add)
    swap("m0", [v("ms")], [mate], [v("meta", its, its + 5)], [v("meta", mine, mine + 5)])
    for i in range(8):
        k, a = (4, 6, 7, 5, 0, 1, 2, 3)[i], i // 4 * P
        mm(k, "wcs", "wss", 128 * i, "qxc", "qxs", 0, P)
        relu(v("kxt", 4 * a + i % 4, 4 * a + 4 * P, 4), v("ps", 512 * k, 512 * k + P), False)
    for k, a in ((4, 0), (6, P)):
        quant(v("kxc", a, a + P), v("kxs", a, a + P), v("kxt", 4 * a, 4 * a + 4 * P))
        mm(k, "ubc", "ubs", 0, "kxc", "kxs", a, P)
        act(v("bo", a, a + P), v("ps", 512 * k, 512 * k + P), FN.Sign, bias=-TINY)
    ts(c(64), c(1), -6.0 if rank == low else 0.0, A_.add, 0.0, A_.max)
    ts(c(65), c(64), 9.0, A_.min, 32.0, A_.add)
    ts(c(66), c(65), 40.0, A_.is_ge)
    lin(c(67), c(2), 16.0, -398.0)
    lin(c(68), c(3), -32.0, c(67))
    lin(c(69), c(65), 9.0, c(68))
    ts(v("g16", 0), c(69), c(66), A_.mult, c(65), A_.add)
    act(v("w0", 32, 37), v("val2", 12, P, 32))
    first = len(nodes)
    cp(v("b0", 0, 16), by(v("bo"), v("o16", 6)))
    act(v("b0", 16, 32), by(v("bo"), v("o16", 6)))
    turn(v("b0", 32, 64), v("b0", 0, 32))
    scan(v("w0", 0, 32), v("hm", 0, 32), v("b0", 32, 64), A_.mult, A_.add)
    cp(v("w0", 37, 40), v("o16", 0, 6, 2))
    half = 16 * (rank - low)
    ts(v("meta", half, half + 16), by(v("w0"), v("g16", 0)), 4.0, A_.mult, 4096.0, A_.add)
    pick("pc", "pl", K * rank, K, "qxc", "qxs", P, v("o16", 0))
    swap("a1", pieces(0, K, rank, 1), [mate], pieces(0, K, mate, 1))
    for k in range(2):
        pick("pc", "pl", X2 + 2 * K * rank + K * k, K, "qxc", "qxs", P, v("o16", 2 + 2 * k))
    swap("m1", [v("meta", mine + 5, mine + 10)], [mate], [v("meta", its + 5, its + 10)])
    swap("b1", pieces(X2, 2 * K, rank, 1), [mate], pieces(X2, 2 * K, mate, 1))
    swap("a2", pieces(0, K, low, 2), peers, sum([pieces(0, K, pair(r), 2) for r in peers], []))
    swap("m2", [v("meta", 6, 26)], peers, [v("meta", 32, 92)],
         [v("meta", 12 + 10 * ((rank - r) % N), 32 + 10 * ((rank - r) % N)) for r in peers])
    swap("b2", pieces(X2, 2 * K, low, 2), peers, sum([pieces(X2, 2 * K, pair(r), 2) for r in peers], []))

    gate.append(first)
    quant(v("poc", 0, P), v("pol", 0, P), v("xt"))
    mm(4, "wcs", "wss", 0, "qxc", "qxs", 0, P)
    for k in range(1, 4):
        lin(v("it", IT * k, IT * k + IT), v("it", 0, IT), 1.0, float(IT * k))
    act(v("yt", 0, P), v("ps", 2048, 2048 + P))
    lin(v("hb"), v("it", 0, 192), 1.0, -16.0)
    fill(v("bz", 4 * X2, 2 * KID), 0.0)
    lin(c(6, 3), v("it", 0, 3), 16.0, c(1))
    lin(c(9, 3), c(6, 3), -1.0, float(NA - 1))
    ts(c(18, 3), c(9, 3), -(CAPP - 1) / 2, A_.add, 1.0 / CAPP, A_.mult)
    cp(v("ci", 0, 3), c(18, 3))
    cp(c(12, 3), v("ci", 0, 3))
    lin(c(32, 3), c(12, 3), float(CAPP), -0.5)
    tt(c(15, 3), c(32, 3), c(9, 3), A_.subtract)
    lin(c(21, 3), c(6, 3), -128.0)
    lin(c(54, 3), c(12, 3), -32.0 / 1024)
    for k in range(3):
        lin(v("bs", 32 * k, 32 * k + 32), v("it", 0, 32), -1.0 / 1024, c(54 + k))
    ts(c(35, 3), c(12, 3), 4.0, A_.is_ge, -112.0, A_.mult)
    lin(c(38, 3), c(12, 3), 32.0, 2.0)
    tt(c(27, 3), c(35, 3), c(38, 3), A_.add)
    cp(v("iq16", 0, 6, 2), c(27, 3))
    cp(v("iq16", 1, 6, 2), c(27, 3))
    lin(c(70, 3), c(12, 3), 10.0, float(88 - 10 * low))
    ts(c(73, 3), c(70, 3), 88.0, A_.is_ge, -80.0, A_.mult)
    tt(c(76, 3), c(70, 3), c(73, 3), A_.add)
    cp(v("iq16", 6, 12, 2), c(76, 3))
    cp(v("iq16", 7, 12, 2), c(76, 3))
    cp(v("ex16"), v("exi"))
    lin(c(30), c(3), 1.0, -1.75)
    lin(v("qc"), v("qc"), 0.5, c(30))
    lin(v("qc0"), v("qc"), 4.0, 4096.0)
    lin(c(28), c(3), 1.0, float(4 - low // 2))
    ts(c(29), c(28), 4.0, A_.is_ge, -4.0, A_.mult)
    ts(c(31), c(28), c(29), A_.add, 20.0, A_.mult)
    ts(v("me16"), v("mei"), c(31), A_.add)
    ts(v("dm"), v("dm"), c(1), A_.is_equal)
    lin(v("dm2", 0, 48), v("dm", 0, 48), -1.0)
    act(v("dm2", 48, 80), v("dm", 0, 32))
    act(v("dm2", 80, 96), v("dm", 0, 16), scale=-128.0)
    act(v("hm2"), v("hm", 0, 128))
    fill(v("r16"), 1.0)
    ms(v("r16", 0, 96, 16), 0.0)
    fill(v("qo"), rank * 0.5 - 1.75)
    fill(v("thr", 0, 87), 1.0)
    fill(v("mk", 0, 87), 1.0)
    fill(v("eb", 0, 87), 0.0)
    ms(v("thr", 69), 0.0)
    ms(v("mk", 0, 51, 50), 0.0)
    ms(v("eb", 49), float(NS))
    fill(v("sm"), 1.0)
    for k in range(3):
        if k < 2:
            act(v("mm", ML * k, ML * k + ML), v("it", 0, ML), FN.Relu, bias=c(21 + k), scale=128.0)
        else:
            ts(v("mm", ML * k, ML * k + ML), v("it", 0, ML), c(6 + k), A_.is_le, 128.0, A_.mult)
        lin(v("sm", 66 * k + 1, 66 * k + 17), v("dm", 0, 16), -2.0, 1.0)
    ms(v("sm", 0, 150, 50), 0.0)
    ms(v("es", 0, 150, 50), 0.0)
    ms(v("es", 49, 100, 50), float(NA))
    ms(v("es", 149), float(NA + 128))
    for t in range(R):
        fill(v("so", 256 * t, 256 * t + 2 * NA), 0.0)
    fill(v("kt", 256, MO), 0.0)
    fill(v("kt", MO + 256, 1040), 0.0)
    fill(v("neg"), 0.0)
    for k in range(2):
        lin(v("ramp", NA * k, NA * k + NA), v("it", 0, NA), -64.0, -64.0 - UNIT * k)
    lin(v("xc"), v("it", 0, NA), 1.0, K + UNIT)
    ts(v("n16", 1, 3), c(7, 2), float(NA), A_.add)
    ms(v("cap2", NA), BIG)
    for t in range(R - 1):
        fill(v("so2", 256 * t, 256 * t + 2 * NA), -BIG)
    lin(c(25), c(2), 16.0)
    lin(c(26), c(2), 32.0, float(X2 - K))
    lin(v("uI", 0, K), v("it", 0, K), 1.0, c(25))
    for k in range(2):
        ts(v("uI", K + k, NS, 2), v("it", 0, K), c(25), A_.add, float(X2 * (k + 1)), A_.add)
    cp(v("cw16", 0), c(0))
    ts(v("cw16", 1, 3), c(7, 2), c(26), A_.add)
    ts(c(41), c(1), 2.0, A_.min, 5.0, A_.add)
    for k, sh in enumerate((6, 4, 3, 2, 1, 0)):
        ts(v("bi", 2 + k), v("pi", 0), sh, A_.logical_shift_right, 1, A_.bitwise_and)
    cp(v("bf", 2, 8), v("bi", 2, 8))
    lin(c(79), v("bf", 3), 10.0, c(41))
    ts(v("pw16", 0), c(79), c(31), A_.add)
    lin(c(42), v("bf", 7), 32.0)
    lin(c(43), v("bf", 6), 16.0, c(42))
    lin(c(52), v("bf", 5), 8.0, c(43))
    ts(v("bf", 0, 2), v("bf", 3, 5), v("bf", 2), A_.not_equal, 4.0, A_.mult)
    ts(v("xb16", 0), v("bf", 0), c(52), A_.add)
    ts(v("xo16", 0), v("bf", 1), c(52), A_.add)
    lin(c(53), v("bf", 7), 1.0, float(XQ))
    ts(v("pg16", 0, 2), c(44, 2), v("bf", 7), A_.subtract, 0.5, A_.mult)
    ts(v("pg16", 2, 4), v("pg16", 0, 2), 8.0, A_.add)
    lin(c(57), v("bf", 7), 31.0, float(K))
    ts(v("eb", 67, 87, 19), c(6, 2), c(57), A_.add)
    ts(c(18), v("bf", 7), v("bf", 3), A_.not_equal, float(P), A_.mult)
    lin(c(19), v("bf", 3), -32.0, 16.0)
    ts(c(20), v("bf", 7), c(19), A_.mult, c(18), A_.add)
    ts(c(32), c(1), 16.0, A_.mult, 144.0, A_.min)
    ts(v("ho16", 0), c(32), c(20), A_.add)

    def held(name, t, a=0, b=NS):
        name, o = {"uS": ("uS", 96 * t), "uP": ("uS", 96 * t + NS)}.get(name, (name, NS * t))
        return v(name, o + a, o + b)

    act(v("fe"), by(v("val2"), v("mo16")))
    turn(v("fm2"), v("fe"))
    cp(v("po16"), v("o16", 0, 6, 2))
    cp(by(v("fm2"), v("po16")), v("neg"))
    cp(v("mf", 0, 20), v("meta", 6, 26))
    cp(v("mf", 20, 80), v("meta", 32, 92))
    cp(v("plw"), by(v("mf"), v("pw16", 0)))
    act(v("fe"), by(v("mf"), v("me16")), FN.Identity, bias=-1024.0, scale=0.25)
    ts(v("p16", 0, 3), v("plw", 0, 3), 0.25, A_.mult, -1024.0, A_.add)
    turn(v("fm"), v("fe"))
    act(held("uP", 0), by(v("it", 0, P), v("p16", 0, 3)))
    act(v("fm3"), v("fm"))
    act(held("uM", 0), by(v("fm3"), v("p16", 0, 3)))
    cp(by(v("fm"), v("p16", 0, 3)), v("neg"))
    act(v("ml", ML - P, ML), v("fm"))

    def opens(t):
        for name in (("uM", "uP", "uS") if t < R - 1 else ("uM", "uP")) if t else ():
            cp(by(held(name, t), v("rk16", 0, 3)), held(name, t - 1))
        if t < R - 1:
            act(v("ml", NA, NA + NS - K), held("uM", t, K))
            move(v("aI", 0, K), held("uI", t, 0, K))
            move(v("aM", 0, K), held("uM", t, 0, K))
        else:
            for k in range(4):
                act(v("ti", 192 + K * k, 208 + K * k), held("uM", t, K + K * (k // 2), 2 * K + K * (k // 2)))

    oq, oh_ = (32 * (rank // 2), 32 * (rank // 2) + 32), 16 * (rank % 2)

    def rising(t, places, own):
        act(v("junk", 320, 320 + K), places, FN.Sign, bias=own, scale=-1.0, acc=v("od", t))
        ts(v("lim", t), v("od", t), 17.0, A_.add, -UNIT / 2, A_.mult)

    def table(a, k):
        mm(k, "ubc", "ubs", 0, "pc", "pl", a, 256)
        act(v("bz", a - XQ, a - XQ + 256), v("ps", 512 * k, 512 * k + 256), FN.Sign, bias=-TINY)

    def ahead(tile, cn, sn, a, n, to, banks, e=0):
        for i in range(8):
            k = 4 + i % 4
            mm(k, "wcs", "wss", 128 * i, cn, sn, a, 256)
            relu(v(tile, i, 8 * n, 8), v("ps", 512 * k + e, 512 * k + 256, 256 // n), tile == "kt1" and i % 4 == 1)
        for h in range(0, 2 * n, 128):
            quant(v("pc", to + h, to + h + 128), v("pl", to + h, to + h + 128), v(tile, 4 * h, 4 * h + 512))
        for h in range(n // 128):
            table(to + 256 * h, banks[h])

    def outputs(t):
        h, w = 64 * t + oh_, 64 if t < R - 1 else 128
        n, new, at = P + 256 * (t + 1), v("own16", 4 * t), v("own16", 4 * t + 2)
        for k in range(4):
            (move if t < R - 1 else act)(v("ti", 64 * t + K * k, 64 * t + K * k + K), held("uP" if k // 2 else "uI", t, 0, K))
        turn(v("tt", 64 * t, 64 * t + w), v("ti", 64 * t, 64 * t + w))
        ts(v("tt", h, p=oq), v("tt", h, p=oq), float(XQ), A_.subtract, v("tt", 32 + h, p=oq), A_.max)
        for o in range(0, 128, 32):
            if o != oq[0]:
                act(v("tt", h, h + w - 31, 32, p=(o, o + 32)), v("tt", h, h + w - 31, 32, p=oq))
        cp(v("own16", 4 * t, 4 * t + 4, 2), v("tt", h, h + 33, 32))
        cols, yn = v("t16", 32 * t + 16, 32 * t + 32), v("t16", 32 * t, 32 * t + 16)
        if t < R - 1:
            act(yn, by(v("yt", 0, n), new))
            act(cols, by(v("it", 0, n), new))
            cp(by(v("hb", 16, 16 + P), at), cols)
            store(t)
            return
        ts(v("mk16"), v("tt", h + 64, h + 97, 32), 1023.0, A_.add, 0.5, A_.mult)
        act(v("ml", NA, NA + NS - K), by(v("it", 0, 1024), v("mk16")), FN.Identity, bias=-1023.0, scale=2.0)
        act(v("ml", ML - P, ML), v("fm2"))
        act(v("op"), by(v("it", 0, P), at))
        rising(t, v("op"), v("tt", 32 + h))
        cp(by(v("hb", 16, 16 + P), at), v("it", OWN, OWN + K))
        turn(v("ht", 0, P), v("hb", 16, 16 + P))
        turn(v("ht", P, 352), v("hb"))
        cp(v("l16"), by(v("ht"), v("ho16", 0)))
        dma("S", "hc", w8(v("hc", 0, OWN)), w8(v("poc")))
        dma("S", "hs", v("hs", 0, OWN), v("pol"))
        pick("ac", "asc", 0, K, "poc", "pol", OWN, new)
        act(v("ya", 0, K), by(v("yt", 0, n - 256), new))

    def ys(t):
        cn, sn, a = ("poc", "pol", P + 256 * t) if t < R - 1 else kids[t]
        mm(2, "wcs", "wss", 0, cn, sn, a, 256)
        act(v("yt", P + 256 * t, P + 256 * t + 256), v("ps", 1024, 1280))
        move(v("yb", P * t, P * t + P), v("yt", 0, P) if t == 0 else v("yb", P * t - P, P * t))

    def store(t):
        cp(by(v("yb", P * t, P * t + P), v("own16", 4 * t + 2)), v("t16", 32 * t, 32 * t + 16))
        dma("S", "y%d" % t, T.y[:, P * t:P * t + P], v("yb", P * t, P * t + P))

    kids = [("pc", "pl", XQ), ("poc", "pol", P + 256), ("k2c", "k2s", 0)]
    for t in range(R):
        kid, (kc, ks, k0) = KID + 256 * t, kids[t]
        end = t == R - 1
        opens(t)
        if end:
            outputs(t)
        if t == 0:
            for i in range(8):
                mm(i, "wcs", "wss", 128 * i, "pc", "pl", 0, 128)
            for i in range(8):
                relu(v("kt0", i, 1024, 8), v("ps", 512 * i, 512 * i + 128), i in (5, 7))
            for a in (0, 128):
                quant(v("pc", XQ + a, XQ + a + 128), v("pl", XQ + a, XQ + a + 128), v("kt0", 4 * a, 4 * a + 512))
        else:
            cp(v("bits", 0, 64), by(v("bz", 0, 2 * kid), v("bl16", 0, 4)))
            act(v("bits", 64, 128), by(v("bz", 0, 2 * kid), v("bl16", 4, 8)))
            turn(v("bt"), v("bits"))
            scan(v("bits"), v("hm2"), v("bt"), A_.mult, A_.add)
            scan(v("val"), v("hm", 0, 128), v("bt"), A_.mult, A_.add)
            for k in (0, 8):
                pick(kc, ks, k0 + 16 * k, 128, "pc", "pl", XQ + 2 * kid, v("kl16", k, k + 8))
        mm(1, "u0c", "u0s", 0, kc, ks, k0, 256)
        act(v("kt", 0, 256), v("ps", 512, 768))
        if t:
            act(v("mx"), by(v("val"), v("ex16", 0, 16)))
        else:
            act(v("mx"), by(v("mf"), v("ex16", 16, 32)), FN.Identity, bias=-1024.0, scale=0.25)
            dma("S", "kc", w8(v("poc", P, P + 256)), w8(v("pc", XQ, XQ + 256)))
            dma("S", "ks", v("pol", P, P + 256), v("pl", XQ, XQ + 256))
        if t:
            tt(v("iq"), by(v("bits"), v("iq16", 0, 6)), v("qo" if end else "qc"), A_.is_equal)
        else:
            tt(v("iq"), by(v("mf"), v("iq16", 6, 12)), v("qc0"), A_.is_equal)
        turn(v("iqt"), v("iq"))
        for k in range(0, 96, 32):
            scan(v("cnt", k, k + 32), v("iqt", k, k + 32), v("neg", 0, 32), A_.add, A_.add, c(15 + k // 32))
        turn(v("kt", MO, MO + 256), v("mx"))
        scan(v("pos"), v("bs"), v("cnt"), A_.max, A_.min, -1.0)
        ts(v("a16", 0, 3), v("pos", 31, 96, 32), -1024.0, A_.mult, 511.0, A_.min)
        tt(v("dg", 48, 96), by(v("kt", MO, 1040), v("a16", 0, 3)), v("dm2", 48, 96), A_.mult)
        tt(v("dg", 0, 48), by(v("kt", 0, MO), v("a16", 0, 3)), v("dm2", 0, 48), A_.mult)
        act(v("ml", 0, NA), by(v("kt", MO, 1040), v("a16", 0, 3)))
        act(v("aS", K, 64), by(v("kt", 0, MO), v("a16", 0, 3)))
        for k in (48, 0):
            scan(v("dgs", k, k + 48), v("r16", 0, 48), v("dg", k, k + 48), A_.mult, A_.add)
        for k in range(3):
            act(v("junk", 480 + NA * k, 480 + NA * k + NA), v("aS", K, 64), FN.Sign, bias=v("dgs", 16 * k + 15), acc=v("da", k))
        if not end:
            act(v("aI", K, 64), by(v("it", 0, MO), v("a16", 0, 3)), FN.Identity, bias=float(kid))
            act(v("aM", K, 64), by(v("kt", MO, 1040), v("a16", 0, 3)))
        if end:
            ys(t)
            ts(v("ac16", 0, 3), v("pos", 31, 96, 32), -1024.0, A_.mult, 255.0, A_.min)
            pick("ac", "asc", K, NA, kc, ks, 256, v("ac16", 0, 3))
            act(v("ya", K, 64), by(v("yt", P + 256 * t, P + 256 * t + 256), v("ac16", 0, 3)))
        if t == 0:
            mm(3, "u0c", "u0s", 0, "pc", "pl", 0, XQ)
            act(v("sp"), v("ps", 1536, 1536 + XQ))
            act(held("uS", 0), by(v("sp"), v("cw16", 0, 3)))
            table(XQ, 0)
            ahead("kt1", "pc", "pl", XQ, 256, XQ + 2 * KID, (0, 1))
            ahead("kt2", "pc", "pl", X2, 128, XQ + 2 * X2, (3,))
        elif not end:
            ahead("kt3", kc, ks, k0, 256, XQ + 2 * kid, (0, 1))
            ahead("kt4", "pc", "pl", X2, 128, XQ + 4 * X2, (3,), 1)
        sw = 96 * t
        if not end:
            move(v("aS", 0, K), held("uS", t, 0, K))
            move(v("aS", 64, 96), held("uS", t, K))
            for k in (NS, 0):
                tt(v("swd", k, k + NS), v("uS", sw + k, sw + k + NS), v("dm", 0, NS), A_.mult)
                scan(v("sw", sw + k, sw + k + NS), v("r16", 0, NS), v("swd", k, k + NS), A_.mult, A_.add)
            rising(t, held("uP", t, 0, K), v("sw", sw + 63))
            act(v("up5"), held("uP", t), FN.Identity, bias=0.5)
            for k, (a, n) in enumerate(CUT):
                act(v("thr", a + 1, a + n + 1), v("up5", 0, n), FN.Sign, bias=v("sw", sw + 63 + 16 * k), scale=-1.0)
            for a, b in ((1, 49), (51, 86)):
                tt(v("mk", a, b), v("thr", a, b), v("thr", a + 1, b + 1), A_.mult)
        for k in range(3):
            if k == 2:
                act(v("em", ML * k, ML * k + ML), v("ml"), FN.Abs, bias=v("dgs", 63 + 16 * k), scale=128.0)
            else:
                ts(v("em", ML * k, ML * k + ML), v("ml"), v("dgs", 63 + 16 * k), A_.is_equal, 128.0, A_.mult)
        for k in range(3):
            ts(v("es", 50 * k + 1, 50 * k + 49), v("aS", K, 64), v("dgs", 16 * k + 15), A_.add, 0.0, A_.is_equal)
        for k in range(0, 3 * ML, ML):
            scan(v("ems", k, k + ML), v("em", k, k + ML), v("mm", k, k + ML),
                 *((A_.min, A_.max, 128.0) if k == 2 * ML else (A_.max, A_.min)))
        scan(v("ess"), v("es"), v("sm"), A_.add, A_.mult)
        for k in range(3):
            ts(v("s16", k), v("da", k), v("ess", 50 * k + 49), A_.add, v("ems", ML * k + ML - 1), A_.subtract if k == 2 else A_.add)
        cp(by(v("so", 256 * t, 256 * t + 256), v("s16", 0, 3)), v("xc"))
        srt = v("so", 256 * t, 256 * t + 2 * NA, 2)
        scan(v("cap"), srt, v("neg"), A_.add, A_.add, v("lim", t))
        tt(v("eqx"), srt, v("ramp", NA, 2 * NA), A_.add)
        scan(v("yr"), v("ramp", 0, NA), v("cap"), A_.max, A_.min, -BIG)
        scan(v("ys"), v("eqx"), v("cap"), A_.max, A_.min, -BIG)
        ts(v("n16", 0), v("ys", NA - 1), v("yr", NA - 1), A_.subtract, c(1), A_.max)
        if end:
            pick("hc", "hs", OWN, K, "ac", "asc", 64, v("n16", 0))
            pick("occ", "ocs", 0, P, "hc", "hs", OWN + K, v("l16", 0, 10))
            dma("S", "oc", T.oc[:], w8(v("occ")))
            for k in range(4):
                dma("S" if k == 3 else "A", "os", T.osc[4 * k:4 * k + 4, :], v("ocs", p=(32 * k, 32 * k + 4)))
            act(v("t16", 32 * t, 32 * t + 16), by(v("ya"), v("n16", 0)))
            store(t)
            break
        cp(by(v("so2", 256 * t, 256 * t + 256), v("s16", 0, 3)), v("aS", K, 64))
        ts(v("so2", 256 * t + 2 * NA), v("cap", NA - 1), -STEEP, A_.mult, v("sw", sw + 15), A_.min)
        act(v("cap2", 0, NA), v("cap"), scale=STEEP)
        scan(v("zz"), v("so2", 256 * t, 256 * t + 2 * NA + 2, 2), v("cap2"), A_.max, A_.min, -BIG)
        act(held("uI", t, 0, K), by(v("aI"), v("n16", 0)))
        for k in (1, 2, 0):
            own, (a, n) = v("sw", sw + 15 + 16 * k) if k else v("zz", NA), CUT[k]
            new = by(v("aS"), v("n16", 0, n // 16))
            act(v("junk", NS * k, NS * k + n), new, FN.Sign, bias=own, scale=-1.0, acc=v("dr", k))
            ts(v("eb", a + 1, a + n + 1), new, own, A_.is_equal)
        if t == 0:
            act(held("uS", t, 0, K), by(v("aS"), v("n16", 0)))
        act(held("uM", t, 0, K), by(v("aM"), v("n16", 0)))
        for a, b in ((50, 87), (0, 50)):
            scan(v("ebs", a, b), v("eb", a, b), v("mk", a, b), A_.add, A_.mult)
        for k in (1, 2, 0):
            ts(v("rk16", k), v("ebs", CUT[k][0] + CUT[k][1] + 1), v("dr", k), A_.subtract, 0.5, A_.mult)
        if t == 0:
            ts(v("eb", 67, 87, 19), c(6, 2), 2.0, A_.mult, float(K), A_.add)
        cp(by(held("uI", t + 1), v("rk16", 0, 3)), held("uI", t))
        cp(v("t0"), by(held("uI", t + 1), v("pg16")))
        turn(v("tr"), v("t0"))
        for a in range(4):
            o = 8 * (1 - a % 2)
            (act if a % 2 else cp)(v("tr", o, 64, 16, p=(32 * a, 32 * a + 32)), v("tr", o, 64, 16, p=(32 * (a ^ 1), 32 * (a ^ 1) + 32)))
        cp(v("tr", 4, 64, 8, p=(0, 64)), v("tr", 0, 64, 8, p=(64, 128)))
        act(v("tr", 4, 64, 8, p=(64, 128)), v("tr", 0, 64, 8, p=(0, 64)))
        ts(v("bl16"), by(v("tr"), v("xb16", 0)), 2.0, A_.mult, v("bf", 7), A_.add)
        ts(v("kl16"), by(v("tr"), v("xo16", 0)), 2.0, A_.mult, c(53), A_.add)
        ys(t)
        outputs(t)

    log, last = {}, {}
    for i, x in enumerate(nodes):
        need = {j: False for j in x["gate"]}
        need.update({j: True for j in x["after"]})
        if x["q"] in "GS":
            if x["q"] in last:
                need[last[x["q"]]] = False
            if not x.get("free"):
                last[x["q"]] = i
        for regs, write in ((x["rd"], False), (x["wr"], True)):
            for name, m, pm in regs:
                for em, ep, ew, j in log.get(name, []):
                    if em & m and ep & pm and (write or ew or name == "ps"):
                        y = nodes[j]
                        inorder = y["q"] == x["q"] == y["sem"] and (x["q"] == "E" or not (write or ew))
                        need[j] = need.get(j, False) or not inorder
        for regs, write in ((x["rd"], False), (x["wr"], True)):
            for name, m, pm in regs:
                log.setdefault(name, []).append((m, pm, write, i))
        x["need"] = need
    users = [[] for x in nodes]
    for i, x in enumerate(nodes):
        for j in x["need"]:
            users[j].append(i)
    key = {i: k for k, i in enumerate(ORDER)}
    left, plan = [len(x["need"]) for x in nodes], []
    ready = [i for i in range(len(nodes)) if not left[i]]
    while ready:
        i = min(ready, key=lambda k: key[k])
        ready.remove(i)
        plan.append(i)
        for j in users[i]:
            left[j] -= 1
            if not left[j]:
                ready.append(j)
    count, seen, drain = {}, {q: {} for q in Q}, []
    for i in plan:
        x = nodes[i]
        if x["q"] != "R":
            waits = {}
            if x["q"] == "V":
                x["need"].update({j: True for j in drain})
                drain[:] = [i] if x.get("drain") else []
            for j, done in x["need"].items():
                s_, val = nodes[j]["sem"], nodes[j]["val"]
                if done and seen[x["q"]].get(s_, 0) < val:
                    seen[x["q"]][s_] = waits[s_] = val
            for s_, val in waits.items():
                Q[x["q"]].wait_ge(T.sem[s_], val)
            ins = x["call"]()
            if x["sem"] != "sent":
                ins.then_inc(T.sem[x["sem"]], x["inc"])
        count[x["sem"]] = count.get(x["sem"], 0) + x["inc"]
        x["val"] = count[x["sem"]]
    for s_ in SEMAPHORES:
        g.wait_ge(T.sem[s_], count[s_])
